import numpy as np
import ml_dtypes


def mxq(x, axis, fmt="e4m3"):
    dtype, down = {"e4m3": (ml_dtypes.float8_e4m3fn, 7), "e5m2": (ml_dtypes.float8_e5m2, 14)}[fmt]
    v = np.moveaxis(np.asarray(x, np.float32).astype(ml_dtypes.bfloat16).astype(np.float64), axis, -1)
    blocks = v.reshape(v.shape[:-1] + (-1, 32))
    amax = np.abs(blocks).max(-1, keepdims=True)
    byte = np.maximum(np.where(amax > 0, np.frexp(amax)[1] - 1 + 127, 0) - down, 1)
    scale = np.exp2(byte - 127.0)
    codes = (blocks / scale).astype(np.float32).astype(dtype).astype(np.float64)
    return np.moveaxis((codes * scale).reshape(v.shape), -1, axis)


WIDE = False


def mx_kscale(k):
    if not WIDE:
        return np.ones(k)
    levels = np.array([24, -24, 12, -12, 0])
    if k % 512:
        return np.exp2(np.random.permutation(np.resize(levels, k // 32))).repeat(32)
    a = np.empty((k // 512, 16))
    for p in range(k // 512):
        a[p, :8] = np.random.permutation(np.resize(levels, 8))
        for g in range(8):
            far = levels[np.abs(levels - a[p, g]) >= 10]
            a[p, g + 8] = far[np.random.randint(len(far))]
    return np.exp2(a.ravel()).repeat(32)


def f64(x):
    return np.asarray(x).astype(np.float64)


def striped(idx):
    return np.tile(idx.reshape(-1, 16).T, (8, 1)).astype(np.uint16)


def unstriped(offs):
    return offs[:16].T.reshape(-1).astype(np.int64)


E2M1 = np.array([0.0, 0.5, 1.0, 1.5, 2.0, 3.0, 4.0, 6.0, -0.0, -0.5, -1.0, -1.5, -2.0, -3.0, -4.0, -6.0])


def pack_weight(w, fmt):
    k, n = w.shape
    w = f64(np.asarray(w, np.float32).astype(ml_dtypes.bfloat16)).reshape(k // 32, 32, n)
    amax = np.abs(w).max(1)
    if fmt == "e4m3":
        byte = np.frexp(amax)[1] - 1 + 127 - 7
    else:
        mant, ex = np.frexp(amax / 6.0)
        byte = np.where(mant > 0.5, ex, ex - 1) + 127
    byte = np.clip(np.where(amax > 0, byte, 1), 1, 254)
    scaled = (w * np.exp2(127.0 - byte)[:, None, :]).reshape(k, n).astype(np.float32)
    by_word = np.ascontiguousarray(scaled.reshape(k // 512, 128, 4, n).transpose(0, 1, 3, 2))
    if fmt == "e4m3":
        words = by_word.astype(ml_dtypes.float8_e4m3fn).view(np.uint8)
    else:
        c = by_word.astype(ml_dtypes.float4_e2m1fn).view(np.uint8) & 0xF
        words = (c[..., 0::2] | (c[..., 1::2] << 4)).reshape(k // 512, 128, 2 * n)
    return np.ascontiguousarray(words), np.ascontiguousarray(byte.astype(np.uint8).reshape(k // 512, 16, n))


def unpack_weight(words, scales, fmt):
    g, _, n = scales.shape
    words = np.ascontiguousarray(words).reshape(g, 128, n, -1)
    if fmt == "e4m3":
        vals = words.view(ml_dtypes.float8_e4m3fn).astype(np.float64)
    else:
        nib = np.empty((g, 128, n, 4), np.uint8)
        nib[..., 0::2] = words & 0xF
        nib[..., 1::2] = words >> 4
        vals = E2M1[nib]
    vals = vals * np.repeat(np.exp2(scales.astype(np.float64) - 127.0), 8, axis=1)[..., None]
    return vals.transpose(0, 1, 3, 2).reshape(g * 512, n)


def planes(y):
    n, m = y.shape
    v = y.astype(np.float32).astype(ml_dtypes.bfloat16).astype(np.float64).reshape(n // 32, 32, m)
    top = np.abs(v).max(1)
    byte = np.clip(np.where(top > 0, np.frexp(top)[1] - 1 + 127 - 7, 1), 1, 254)
    codes = (v * np.exp2(127.0 - byte)[:, None, :]).reshape(n, m).astype(np.float32).astype(ml_dtypes.float8_e4m3fn).view(np.uint8)
    words = codes.reshape(n // 512, 128, 4, m).transpose(0, 1, 3, 2)
    return np.ascontiguousarray(words), np.ascontiguousarray(byte.astype(np.uint8).reshape(n // 512, 16, m))


def sigm(f):
    return 1.0 / (1.0 + np.exp(-np.maximum(f, -700.0)))


K, L, N, T, J = 512, 512, 512, 2048, 1024


def setup_inputs():
    n = np.random.standard_normal
    s = mx_kscale(K)[:, None]
    s2 = mx_kscale(L)[:, None]
    p_tab = pack_weight(n((K, T)) * s, "e4m3")
    p_tab2 = pack_weight(n((L, T)) * s2, "e4m3")
    p_zv = pack_weight(n((K, N)) / np.sqrt(K) / s, "e4m3")
    p_zt = pack_weight(n((L, N)) / np.sqrt(L) / s2, "e2m1")
    p_wv = pack_weight(n((K, N)) / np.sqrt(K) / s, "e4m3")
    return {
        "tab_words": p_tab[0],
        "tab_scales": p_tab[1],
        "tab2_words": p_tab2[0],
        "tab2_scales": p_tab2[1],
        "zv_words": p_zv[0],
        "zv_scales": p_zv[1],
        "zt_words": p_zt[0],
        "zt_scales": p_zt[1],
        "b": (0.3 * n(N)).astype(np.float32),
        "wv_words": p_wv[0],
        "wv_scales": p_wv[1],
        "wt": (n((L, N)) / np.sqrt(L) / s2).astype(np.float32),
        "wgo": np.tile(np.random.uniform(0.5, 2.0, J), (128, 1)).astype(np.float32),
        "offs": striped(np.random.permutation(T)[:J]),
        "offs2": striped(np.random.permutation(T)[:J]),
    }


def reference(tab_words, tab_scales, tab2_words, tab2_scales, zv_words, zv_scales, zt_words, zt_scales, b, wv_words, wv_scales, wt, wgo, offs, offs2):
    idx = unstriped(offs)
    idx2 = unstriped(offs2)
    tab_ = unpack_weight(tab_words, tab_scales, "e4m3")[:, idx]
    tab2_ = unpack_weight(tab2_words, tab2_scales, "e4m3")[:, idx2]
    zv_ = unpack_weight(zv_words, zv_scales, "e4m3")
    zt_ = unpack_weight(zt_words, zt_scales, "e2m1")
    z = zv_.T @ tab_ + zt_.T @ tab2_
    gate = sigm(z + f64(b)[:, None])
    wv_ = unpack_weight(wv_words, wv_scales, "e4m3")
    wt_ = mxq(f64(wt), 0, "e4m3")
    hv = wv_.T @ tab_
    ht = wt_.T @ tab2_
    av = np.tanh(hv)
    at = np.tanh(ht)
    out = np.zeros((N, T))
    out[:, idx] = f64(wgo)[0] * (at + gate * (av - at))
    return (out,) + planes(out)

@@ -1,0 +1,237 @@
+from contextlib import ExitStack
+
+import concourse.mybir as mybir
+from concourse.masks import make_identity
+
+K, L, N, T, J = 512, 512, 512, 2048, 1024
+FLOPS = 4 * 2 * 512 * N * J
+
+F32 = mybir.dt.float32
+BF16 = mybir.dt.bfloat16
+I32 = mybir.dt.int32
+U32 = mybir.dt.uint32
+U16 = mybir.dt.uint16
+U8 = mybir.dt.uint8
+FP8X4 = mybir.dt.float8_e4m3fn_x4
+FP4X4 = mybir.dt.float4_e2m1fn_x4
+ACT = mybir.ActivationFunctionType
+ALU = mybir.AluOpType
+
+P = 128
+PACK = 4
+HALF = 512
+HALVES = J // HALF
+BLOCKS = HALF // P
+CHUNK = 512
+CHUNKS = T // CHUNK
+VECTOR_CHUNKS = 2
+ZT_ROW, ZV_ROW = 0, 4
+
+
+def load_scale_rows(queue, plane, first_row, scales):
+    for q in range(4):
+        queue.dma_start(
+            out=plane[32 * q + first_row : 32 * q + first_row + 4, :].bitcast(I32),
+            in_=scales[0, 4 * q : 4 * q + 4, :].bitcast(I32),
+        )
+
+
+def words_of(dram):
+    return dram[0].rearrange("p n i -> p (n i)").bitcast(I32)
+
+
+def tile_list_gmu_tanh_scatP_kernel(
+    tc, tab_words, tab_scales, tab2_words, tab2_scales, zv_words, zv_scales, zt_words, zt_scales,
+    b, wv_words, wv_scales, wt, wgo, offs, offs2, out_0, out_1, out_2,
+):
+    nc = tc.nc
+    with ExitStack() as ctx:
+        keep = ctx.enter_context(tc.tile_pool(name="keep", bufs=1))
+        ring = ctx.enter_context(tc.tile_pool(name="ring", bufs=3))
+        sums = ctx.enter_context(tc.psum_pool(name="sums", bufs=4))
+        turned = ctx.enter_context(tc.psum_pool(name="turned", bufs=2))
+
+        list1 = keep.tile([P, J // 16], U16, name="list1")
+        list2 = keep.tile([P, J // 16], U16, name="list2")
+        tab_w = keep.tile([P, T], U32, name="tab_w", align_bytes=64)
+        tab_s = keep.tile([P, T], U8, name="tab_s", align_bytes=64)
+        tab2_w = keep.tile([P, T], U32, name="tab2_w", tag="tab2_w", align_bytes=64)
+        tab2_s = keep.tile([P, T], U8, name="tab2_s", tag="tab2_s", align_bytes=64)
+        weight_s = keep.tile([P, N], U8, name="weight_s", align_bytes=64)
+        wv_s = keep.tile([P, N], U8, name="wv_s", align_bytes=64)
+        wv_w = keep.tile([P, N], U32, name="wv_w", align_bytes=64)
+        zv_raw = keep.tile([P, N], I32, name="zv_raw", align_bytes=64)
+        zt_raw = keep.tile([P, 2 * N], U8, name="zt_raw", align_bytes=64)
+        wt_raw = keep.tile([P, PACK, N], F32, name="wt_raw", align_bytes=64)
+        bias = keep.tile([P, PACK], F32, name="bias")
+        half_bias = keep.tile([P, PACK], F32, name="half_bias")
+        wgo_sb = keep.tile([P, J], F32, name="wgo_sb", align_bytes=64)
+        ident = keep.tile([P, P], F32, name="ident", align_bytes=64)
+        warm = keep.tile([P, 1], F32, name="warm")
+        warm2 = keep.tile([P, 1], F32, name="warm2")
+
+        nc.vector.memset(tab_s[:].bitcast(I32), 0)
+        nc.vector.memset(weight_s[:].bitcast(I32), 0)
+        nc.vector.memset(wv_s[:].bitcast(I32), 0)
+        nc.vector.memset(tab2_s[:].bitcast(I32), 0)
+        nc.vector.memset(warm[:], 0.0)
+        nc.scalar.activation(warm2[:], warm[:], ACT.Tanh)
+
+        nc.sync.dma_start(list1[:], offs)
+        nc.sync.dma_start(out=tab_w[:].bitcast(I32), in_=words_of(tab_words))
+        load_scale_rows(nc.sync, tab_s, 0, tab_scales)
+        nc.sync.dma_start(out=wt_raw[:], in_=wt.rearrange("(p j) n -> p j n", j=PACK))
+        nc.sync.dma_start(out=tab2_w[:].bitcast(I32), in_=words_of(tab2_words))
+        nc.sync.dma_start(out=wv_w[:].bitcast(I32), in_=words_of(wv_words))
+        load_scale_rows(nc.sync, wv_s, 0, wv_scales)
+        nc.sync.dma_start(list2[:], offs2)
+        load_scale_rows(nc.sync, tab2_s, 0, tab2_scales)
+        nc.sync.dma_start(out=zv_raw[:], in_=words_of(zv_words))
+        nc.sync.dma_start(out=zt_raw[:].bitcast(I32), in_=zt_words[0].bitcast(I32))
+        nc.sync.dma_start(out=bias[:], in_=b.rearrange("(p t) -> p t", t=PACK))
+        nc.sync.dma_start(out=wgo_sb[:], in_=wgo)
+        load_scale_rows(nc.gpsimd, weight_s, ZV_ROW, zv_scales)
+        load_scale_rows(nc.gpsimd, weight_s, ZT_ROW, zt_scales)
+        make_identity(nc, ident[:])
+
+        pages = []
+        for t in range(2):
+            page = keep.tile([P, T], F32, name="page%d" % t, align_bytes=64)
+            nc.vector.memset(page[:], 0.0)
+            pages.append(page)
+
+        def gather(name, words, plane, offsets, h):
+            cols = slice(h * HALF // 16, (h + 1) * HALF // 16)
+            got_w = keep.tile([P, HALF], U32, name="%s_w%d" % (name, h), align_bytes=64)
+            got_s = keep.tile([P, HALF], U8, name="%s_s%d" % (name, h), align_bytes=64)
+            nc.vector.tensor_copy(got_w[:], words[:].indirect(offsets[:, cols]))
+            nc.vector.tensor_copy(got_s[:], plane[:].indirect(offsets[:, cols]))
+            return got_w, got_s
+
+        def branch(name, got, w_words, w_plane, sign, h):
+            got_w, got_s = got
+            tiles = []
+            for blk in range(BLOCKS):
+                cols = slice(blk * P, (blk + 1) * P)
+                acc = sums.tile([P, N], F32, name="acc", tag="acc")
+                nc.tensor.matmul_mx(
+                    out=acc[:], lhsT=got_w[:, cols].bitcast(FP8X4), lhsT_scale=got_s[:, cols],
+                    rhs=w_words.bitcast(FP8X4), rhs_scale=w_plane, start=True, stop=True,
+                )
+                act = keep.tile([P, PACK, P], F32, name="%s%d_%d" % (name, h, blk), align_bytes=64)
+                nc.scalar.activation(act[:], acc[:].rearrange("j (m t) -> j t m", t=PACK), ACT.Tanh, scale=sign)
+                tiles.append(act)
+            return tiles
+
+        v = [gather("v", tab_w, tab_s, list1, h) for h in range(HALVES)]
+
+        wt_bf = keep.tile([P, N, PACK], BF16, name="wt_bf", align_bytes=64)
+        nc.scalar.copy(
+            wt_bf[:].rearrange("p (c i) j -> p c j i", i=4),
+            wt_raw[:].rearrange("p j (c i) -> p c j i", i=4),
+        )
+        av = [branch("av", v[0], wv_w[:], wv_s[:], 1.0, 0)]
+
+        v2 = [gather("v2", tab2_w, tab2_s, list2, 0)]
+        wt_w = keep.tile([P, N], U32, name="wt_w", align_bytes=64)
+        wt_s = keep.tile([P, N], U8, name="wt_s", align_bytes=64)
+        nc.vector.quantize_mx(out=wt_w[:].bitcast(FP8X4), scales=wt_s[:], in_=wt_bf[:].rearrange("p n j -> p (n j)"))
+        neg_at = [branch("neg_at", v2[0], wt_w[:], wt_s[:], -1.0, 0)]
+
+        zv_w = keep.tile([P, PACK, P], I32, name="zv_w", align_bytes=64)
+        zt_w = keep.tile([P, PACK, P, 2], U8, name="zt_w", align_bytes=64)
+        z_s = keep.tile([P, PACK, P], U8, name="z_s", align_bytes=64)
+        nc.vector.tensor_copy(zv_w[:], zv_raw[:].rearrange("p (m t) -> p t m", t=PACK))
+        nc.vector.tensor_copy(zt_w[:], zt_raw[:].rearrange("p (m t e) -> p t m e", t=PACK, e=2))
+        nc.vector.tensor_copy(z_s[:], weight_s[:].rearrange("p (m t) -> p t m", t=PACK))
+        nc.scalar.activation(half_bias[:], bias[:], ACT.Copy, scale=0.5)
+
+        def gate(t, h):
+            acc = sums.tile([P, HALF], F32, name="acc", tag="acc")
+            nc.tensor.matmul_mx(
+                out=acc[:], lhsT=zv_w[:, t, :].bitcast(FP8X4), lhsT_scale=z_s[ZV_ROW:, t, :],
+                rhs=v[h][0][:].bitcast(FP8X4), rhs_scale=v[h][1][:], start=True, stop=False,
+            )
+            nc.tensor.matmul_mx(
+                out=acc[:], lhsT=zt_w[:, t, :, :].rearrange("p m e -> p (m e)").bitcast(FP4X4), lhsT_scale=z_s[ZT_ROW:, t, :],
+                rhs=v2[h][0][:].bitcast(FP8X4), rhs_scale=v2[h][1][:], start=False, stop=True,
+            )
+            s = keep.tile([P, HALF], F32, name="s%d_%d" % (t, h), align_bytes=64)
+            nc.scalar.activation(s[:], acc[:], ACT.Tanh, bias=half_bias[:, t : t + 1], scale=0.5)
+            return s
+
+        gates = {(0, 0): gate(0, 0)}
+        v2.append(gather("v2", tab2_w, tab2_s, list2, 1))
+        av.append(branch("av", v[1], wv_w[:], wv_s[:], 1.0, 1))
+        neg_at.append(branch("neg_at", v2[1], wt_w[:], wt_s[:], -1.0, 1))
+        for t in range(PACK):
+            for h in range(HALVES):
+                if (t, h) not in gates:
+                    gates[(t, h)] = gate(t, h)
+
+        for t, tenant in ((2, "tab2_w"), (3, "tab2_s")):
+            page = keep.tile([P, T], F32, name="page%d" % t, tag=tenant, align_bytes=64)
+            nc.gpsimd.memset(page[:], 0.0)
+            pages.append(page)
+
+        woven = [keep.tile([P, CHUNK, PACK], BF16, name="woven%d" % c, align_bytes=64) for c in range(CHUNKS)]
+        rows = out_0.rearrange("(p t) c -> p t c", t=PACK)
+
+        def mix(t, h):
+            diff = turned.tile([P, HALF], F32, name="diff", tag="diff")
+            text = turned.tile([P, HALF], F32, name="text", tag="text")
+            for blk in range(BLOCKS):
+                cols = slice(blk * P, (blk + 1) * P)
+                nc.tensor.matmul(diff[:, cols], av[h][blk][:, t, :], ident[:], start=True, stop=False, is_transpose=True)
+                nc.tensor.matmul(diff[:, cols], neg_at[h][blk][:, t, :], ident[:], start=False, stop=True, is_transpose=True)
+            for blk in range(BLOCKS):
+                cols = slice(blk * P, (blk + 1) * P)
+                nc.tensor.transpose(text[:, cols], neg_at[h][blk][:, t, :], ident[:])
+            gated = ring.tile([P, HALF], F32, name="gated", tag="gated", align_bytes=64)
+            nc.vector.scalar_tensor_tensor(gated[:], gates[(t, h)][:], 1.0, diff[:], ALU.add, ALU.mult)
+            mixed = ring.tile([P, HALF], F32, name="mixed", tag="mixed", align_bytes=64)
+            nc.vector.scalar_tensor_tensor(mixed[:], gated[:], 0.5, text[:], ALU.mult, ALU.subtract)
+            return mixed
+
+        def place(t, h, mixed):
+            nc.vector.tensor_tensor(
+                pages[t][:].indirect(list1[:, h * HALF // 16 : (h + 1) * HALF // 16]),
+                mixed[:], wgo_sb[:, h * HALF : (h + 1) * HALF], ALU.mult,
+            )
+
+        def weave(t):
+            for c in range(CHUNKS):
+                cols = slice(c * CHUNK, (c + 1) * CHUNK)
+                if t == PACK - 2 and c < VECTOR_CHUNKS:
+                    nc.scalar.copy(woven[c][:, :, t:], pages[t][:, cols].unsqueeze(2).to_broadcast([P, CHUNK, 2]))
+                elif t == PACK - 1 and c < VECTOR_CHUNKS:
+                    nc.vector.tensor_copy(woven[c][:, :, t], pages[t][:, cols])
+                else:
+                    nc.scalar.copy(woven[c][:, :, t], pages[t][:, cols])
+
+        units = [(t, h) for t in range(PACK) for h in range(HALVES)]
+        ready = mix(*units[0])
+        for u, (t, h) in enumerate(units):
+            following = mix(*units[u + 1]) if u + 1 < len(units) else None
+            place(t, h, ready)
+            ready = following
+            if h == HALVES - 1:
+                nc.sync.dma_start(out=rows[:, t, :], in_=pages[t][:])
+                weave(t)
+
+        out_words = out_1[0].rearrange("p c i -> p (c i)").bitcast(I32)
+        planes = [keep.tile([P, 2 * CHUNK], U8, name="plane%d" % g, align_bytes=64) for g in range(CHUNKS // 2)]
+        for c in range(CHUNKS):
+            codes = keep.tile([P, CHUNK], U32, name="codes%d" % c, align_bytes=64)
+            plane = planes[c // 2]
+            nc.vector.quantize_mx(
+                out=codes[:].bitcast(FP8X4), scales=plane[:, (c % 2) * CHUNK : (c % 2 + 1) * CHUNK],
+                in_=woven[c][:].rearrange("p c i -> p (c i)"),
+            )
+            nc.sync.dma_start(out=out_words[:, c * CHUNK : (c + 1) * CHUNK], in_=codes[:].bitcast(I32))
+            if c % 2 == 1:
+                for q in range(4):
+                    nc.scalar.dma_start(
+                        out=out_2[0, 4 * q : 4 * q + 4, (c - 1) * CHUNK : (c + 1) * CHUNK].bitcast(I32),
+                        in_=plane[32 * q : 32 * q + 4, :].bitcast(I32),
+                    )

@@ -3,8 +3,9 @@ from contextlib import ExitStack
 import concourse.mybir as mybir
 from concourse.masks import make_identity
 
-K, L, N, T, J = 512, 512, 512, 2048, 1024
-FLOPS = 4 * 2 * 512 * N * J
+N, T, J = 512, 2048, 1024
+CONTRACTION = 512
+FLOPS = 4 * 2 * CONTRACTION * N * J
 
 F32 = mybir.dt.float32
 BF16 = mybir.dt.bfloat16
@@ -19,18 +20,20 @@ ALU = mybir.AluOpType
 
 P = 128
 PACK = 4
+PER_COLUMN = 16
 HALF = 512
-HALVES = J // HALF
 BLOCKS = HALF // P
 CHUNK = 512
 CHUNKS = T // CHUNK
 VECTOR_CHUNKS = 2
+SUM_BANKS = 4
+PAGE_TILES = 2
 ZT_ROW, ZV_ROW = 0, 4
 
 
-def load_scale_rows(queue, plane, first_row, scales):
+def load_plane(nc, plane, first_row, scales):
     for q in range(4):
-        queue.dma_start(
+        nc.sync.dma_start(
             out=plane[32 * q + first_row : 32 * q + first_row + 4, :].bitcast(I32),
             in_=scales[0, 4 * q : 4 * q + 4, :].bitcast(I32),
         )
@@ -38,6 +41,10 @@ def load_scale_rows(queue, plane, first_row, scales):
 
 def words_of(dram):
     return dram[0].rearrange("p n i -> p (n i)").bitcast(I32)
+
+
+def entries(offsets, first, last):
+    return offsets[:, first // PER_COLUMN : last // PER_COLUMN]
 
 
 def tile_list_gmu_tanh_scatP_kernel(
@@ -48,178 +55,198 @@ def tile_list_gmu_tanh_scatP_kernel(
     with ExitStack() as ctx:
         keep = ctx.enter_context(tc.tile_pool(name="keep", bufs=1))
         ring = ctx.enter_context(tc.tile_pool(name="ring", bufs=3))
-        sums = ctx.enter_context(tc.psum_pool(name="sums", bufs=4))
+        sums = ctx.enter_context(tc.psum_pool(name="sums", bufs=1))
         turned = ctx.enter_context(tc.psum_pool(name="turned", bufs=2))
 
-        list1 = keep.tile([P, J // 16], U16, name="list1")
-        list2 = keep.tile([P, J // 16], U16, name="list2")
+        banks_taken = []
+
+        def next_bank():
+            banks_taken.append(len(banks_taken) % SUM_BANKS)
+            return sums.tile([P, N], F32, name="sum%d" % len(banks_taken), tag="bank%d" % banks_taken[-1])
+
+        list1 = keep.tile([P, J // PER_COLUMN], U16, name="list1")
+        list2 = keep.tile([P, J // PER_COLUMN], U16, name="list2")
         tab_w = keep.tile([P, T], U32, name="tab_w", align_bytes=64)
         tab_s = keep.tile([P, T], U8, name="tab_s", align_bytes=64)
-        tab2_w = keep.tile([P, T], U32, name="tab2_w", tag="tab2_w", align_bytes=64)
+        tab2_w = keep.tile([P, T], U32, name="tab2_w", align_bytes=64)
         tab2_s = keep.tile([P, T], U8, name="tab2_s", tag="tab2_s", align_bytes=64)
-        weight_s = keep.tile([P, N], U8, name="weight_s", align_bytes=64)
+        z_raw_s = keep.tile([P, N], U8, name="z_raw_s", tag="z_raw_s", align_bytes=64)
         wv_s = keep.tile([P, N], U8, name="wv_s", align_bytes=64)
         wv_w = keep.tile([P, N], U32, name="wv_w", align_bytes=64)
         zv_raw = keep.tile([P, N], I32, name="zv_raw", align_bytes=64)
         zt_raw = keep.tile([P, 2 * N], U8, name="zt_raw", align_bytes=64)
-        wt_raw = keep.tile([P, PACK, N], F32, name="wt_raw", align_bytes=64)
+        wt_raw = keep.tile([P, PACK, N], F32, name="wt_raw", tag="wt_raw", align_bytes=64)
         bias = keep.tile([P, PACK], F32, name="bias")
         half_bias = keep.tile([P, PACK], F32, name="half_bias")
         wgo_sb = keep.tile([P, J], F32, name="wgo_sb", align_bytes=64)
         ident = keep.tile([P, P], F32, name="ident", align_bytes=64)
-        warm = keep.tile([P, 1], F32, name="warm")
-        warm2 = keep.tile([P, 1], F32, name="warm2")
+        cleared = keep.tile([P, 1], F32, name="cleared")
+        no_bias = keep.tile([P, 1], F32, name="no_bias")
 
-        nc.vector.memset(tab_s[:].bitcast(I32), 0)
-        nc.vector.memset(weight_s[:].bitcast(I32), 0)
-        nc.vector.memset(wv_s[:].bitcast(I32), 0)
+        nc.gpsimd.memset(tab_s[:].bitcast(I32), 0)
+        nc.vector.memset(cleared[:], 0.0)
         nc.vector.memset(tab2_s[:].bitcast(I32), 0)
-        nc.vector.memset(warm[:], 0.0)
-        nc.scalar.activation(warm2[:], warm[:], ACT.Tanh)
+        nc.vector.memset(wv_s[:].bitcast(I32), 0)
+        nc.vector.memset(z_raw_s[:].bitcast(I32), 0)
+        nc.scalar.activation(no_bias[:], cleared[:], ACT.Tanh)
 
         nc.sync.dma_start(list1[:], offs)
-        nc.sync.dma_start(out=tab_w[:].bitcast(I32), in_=words_of(tab_words))
-        load_scale_rows(nc.sync, tab_s, 0, tab_scales)
-        nc.sync.dma_start(out=wt_raw[:], in_=wt.rearrange("(p j) n -> p j n", j=PACK))
-        nc.sync.dma_start(out=tab2_w[:].bitcast(I32), in_=words_of(tab2_words))
         nc.sync.dma_start(out=wv_w[:].bitcast(I32), in_=words_of(wv_words))
-        load_scale_rows(nc.sync, wv_s, 0, wv_scales)
+        load_plane(nc, tab_s, 0, tab_scales)
+        nc.sync.dma_start(out=tab_w[:].bitcast(I32), in_=words_of(tab_words))
+        nc.sync.dma_start(out=wt_raw[:], in_=wt.rearrange("(p i) n -> p i n", i=PACK))
         nc.sync.dma_start(list2[:], offs2)
-        load_scale_rows(nc.sync, tab2_s, 0, tab2_scales)
+        load_plane(nc, tab2_s, 0, tab2_scales)
+        nc.sync.dma_start(out=tab2_w[:].bitcast(I32), in_=words_of(tab2_words))
+        load_plane(nc, wv_s, 0, wv_scales)
         nc.sync.dma_start(out=zv_raw[:], in_=words_of(zv_words))
         nc.sync.dma_start(out=zt_raw[:].bitcast(I32), in_=zt_words[0].bitcast(I32))
+        load_plane(nc, z_raw_s, ZV_ROW, zv_scales)
+        load_plane(nc, z_raw_s, ZT_ROW, zt_scales)
         nc.sync.dma_start(out=bias[:], in_=b.rearrange("(p t) -> p t", t=PACK))
         nc.sync.dma_start(out=wgo_sb[:], in_=wgo)
-        load_scale_rows(nc.gpsimd, weight_s, ZV_ROW, zv_scales)
-        load_scale_rows(nc.gpsimd, weight_s, ZT_ROW, zt_scales)
+
+        page_tiles = [keep.tile([P, T], F32, name="page%d" % t, align_bytes=64) for t in range(PAGE_TILES)]
+        nc.vector.memset(page_tiles[0][:].bitcast(I32), 0)
+        for c in range(CHUNKS):
+            nc.gpsimd.memset(page_tiles[1][:, c * CHUNK : (c + 1) * CHUNK], 0.0)
         make_identity(nc, ident[:])
 
-        pages = []
-        for t in range(2):
-            page = keep.tile([P, T], F32, name="page%d" % t, align_bytes=64)
-            nc.vector.memset(page[:], 0.0)
-            pages.append(page)
+        def pick(name, window, dtype, offsets, h, tag=None):
+            got = keep.tile([P, HALF], dtype, name="%s%d" % (name, h), tag=tag or "%s%d" % (name, h), align_bytes=64)
+            nc.vector.tensor_copy(got[:], window[:].indirect(entries(offsets, h * HALF, (h + 1) * HALF)))
+            return got
 
-        def gather(name, words, plane, offsets, h):
-            cols = slice(h * HALF // 16, (h + 1) * HALF // 16)
-            got_w = keep.tile([P, HALF], U32, name="%s_w%d" % (name, h), align_bytes=64)
-            got_s = keep.tile([P, HALF], U8, name="%s_s%d" % (name, h), align_bytes=64)
-            nc.vector.tensor_copy(got_w[:], words[:].indirect(offsets[:, cols]))
-            nc.vector.tensor_copy(got_s[:], plane[:].indirect(offsets[:, cols]))
-            return got_w, got_s
-
-        def branch(name, got, w_words, w_plane, sign, h):
-            got_w, got_s = got
-            tiles = []
-            for blk in range(BLOCKS):
-                cols = slice(blk * P, (blk + 1) * P)
-                acc = sums.tile([P, N], F32, name="acc", tag="acc")
-                nc.tensor.matmul_mx(
-                    out=acc[:], lhsT=got_w[:, cols].bitcast(FP8X4), lhsT_scale=got_s[:, cols],
-                    rhs=w_words.bitcast(FP8X4), rhs_scale=w_plane, start=True, stop=True,
-                )
-                act = keep.tile([P, PACK, P], F32, name="%s%d_%d" % (name, h, blk), align_bytes=64)
-                nc.scalar.activation(act[:], acc[:].rearrange("j (m t) -> j t m", t=PACK), ACT.Tanh, scale=sign)
-                tiles.append(act)
-            return tiles
-
-        v = [gather("v", tab_w, tab_s, list1, h) for h in range(HALVES)]
+        v_s = [pick("v_s", tab_s, U8, list1, h) for h in range(2)]
+        v_w = [pick("v_w", tab_w, U32, list1, h) for h in range(2)]
+        v2_s = [pick("v2_s", tab2_s, U8, list2, h) for h in range(2)]
 
         wt_bf = keep.tile([P, N, PACK], BF16, name="wt_bf", align_bytes=64)
         nc.scalar.copy(
-            wt_bf[:].rearrange("p (c i) j -> p c j i", i=4),
-            wt_raw[:].rearrange("p j (c i) -> p c j i", i=4),
+            wt_bf[:].rearrange("p (c e) i -> p c i e", e=4),
+            wt_raw[:].rearrange("p i (c e) -> p c i e", e=4),
         )
-        av = [branch("av", v[0], wv_w[:], wv_s[:], 1.0, 0)]
-
-        v2 = [gather("v2", tab2_w, tab2_s, list2, 0)]
-        wt_w = keep.tile([P, N], U32, name="wt_w", align_bytes=64)
+        wt_w = keep.tile([P, N], U32, name="wt_w", tag="tab2_s", align_bytes=64)
         wt_s = keep.tile([P, N], U8, name="wt_s", align_bytes=64)
-        nc.vector.quantize_mx(out=wt_w[:].bitcast(FP8X4), scales=wt_s[:], in_=wt_bf[:].rearrange("p n j -> p (n j)"))
-        neg_at = [branch("neg_at", v2[0], wt_w[:], wt_s[:], -1.0, 0)]
+        nc.vector.quantize_mx(out=wt_w[:].bitcast(FP8X4), scales=wt_s[:], in_=wt_bf[:].rearrange("p n i -> p (n i)"))
+        v2_w = [pick("v2_w", tab2_w, U32, list2, 0)]
 
         zv_w = keep.tile([P, PACK, P], I32, name="zv_w", align_bytes=64)
         zt_w = keep.tile([P, PACK, P, 2], U8, name="zt_w", align_bytes=64)
         z_s = keep.tile([P, PACK, P], U8, name="z_s", align_bytes=64)
         nc.vector.tensor_copy(zv_w[:], zv_raw[:].rearrange("p (m t) -> p t m", t=PACK))
         nc.vector.tensor_copy(zt_w[:], zt_raw[:].rearrange("p (m t e) -> p t m e", t=PACK, e=2))
-        nc.vector.tensor_copy(z_s[:], weight_s[:].rearrange("p (m t) -> p t m", t=PACK))
+        nc.vector.tensor_copy(z_s[:], z_raw_s[:].rearrange("p (m t) -> p t m", t=PACK))
         nc.scalar.activation(half_bias[:], bias[:], ACT.Copy, scale=0.5)
+        v2_w.append(pick("v2_w", tab2_w, U32, list2, 1, "z_raw_s"))
+
+        av = [keep.tile([P, BLOCKS, PACK, P], F32, name="av0", tag="wt_raw", align_bytes=64),
+              keep.tile([P, BLOCKS, PACK, P], F32, name="av1", align_bytes=64)]
+        neg_at = [keep.tile([P, BLOCKS, PACK, P], F32, name="neg_at%d" % h, align_bytes=64) for h in range(2)]
+
+        def branch(result, got_w, got_s, weight_w, weight_s, sign, first, last):
+            for j in range(first, last, P):
+                h, cols = j // HALF, slice(j % HALF, j % HALF + P)
+                acc = next_bank()
+                nc.tensor.matmul_mx(
+                    out=acc[:], lhsT=got_w[h][:, cols].bitcast(FP8X4), lhsT_scale=got_s[h][:, cols],
+                    rhs=weight_w[:].bitcast(FP8X4), rhs_scale=weight_s[:], start=True, stop=True,
+                )
+                nc.scalar.activation(
+                    result[h][:, j % HALF // P, :, :], acc[:].rearrange("j (m t) -> j t m", t=PACK),
+                    ACT.Tanh, bias=no_bias[:], scale=sign,
+                )
+
+        def picture(first, last):
+            branch(av, v_w, v_s, wv_w, wv_s, 1.0, first, last)
+
+        def text(first, last):
+            branch(neg_at, v2_w, v2_s, wt_w, wt_s, -1.0, first, last)
+
+        gates = [keep.tile([P, J], F32, name="gates%d" % t, align_bytes=64) for t in range(PACK)]
 
         def gate(t, h):
-            acc = sums.tile([P, HALF], F32, name="acc", tag="acc")
+            acc = next_bank()
             nc.tensor.matmul_mx(
                 out=acc[:], lhsT=zv_w[:, t, :].bitcast(FP8X4), lhsT_scale=z_s[ZV_ROW:, t, :],
-                rhs=v[h][0][:].bitcast(FP8X4), rhs_scale=v[h][1][:], start=True, stop=False,
+                rhs=v_w[h][:].bitcast(FP8X4), rhs_scale=v_s[h][:], start=True, stop=False,
             )
             nc.tensor.matmul_mx(
-                out=acc[:], lhsT=zt_w[:, t, :, :].rearrange("p m e -> p (m e)").bitcast(FP4X4), lhsT_scale=z_s[ZT_ROW:, t, :],
-                rhs=v2[h][0][:].bitcast(FP8X4), rhs_scale=v2[h][1][:], start=False, stop=True,
+                out=acc[:], lhsT=zt_w[:, t, :, :].rearrange("p m e -> p (m e)").bitcast(FP4X4),
+                lhsT_scale=z_s[ZT_ROW:, t, :],
+                rhs=v2_w[h][:].bitcast(FP8X4), rhs_scale=v2_s[h][:], start=False, stop=True,
             )
-            s = keep.tile([P, HALF], F32, name="s%d_%d" % (t, h), align_bytes=64)
-            nc.scalar.activation(s[:], acc[:], ACT.Tanh, bias=half_bias[:, t : t + 1], scale=0.5)
-            return s
+            nc.scalar.activation(
+                gates[t][:, h * HALF : (h + 1) * HALF], acc[:], ACT.Tanh, bias=half_bias[:, t : t + 1], scale=0.5,
+            )
 
-        gates = {(0, 0): gate(0, 0)}
-        v2.append(gather("v2", tab2_w, tab2_s, list2, 1))
-        av.append(branch("av", v[1], wv_w[:], wv_s[:], 1.0, 1))
-        neg_at.append(branch("neg_at", v2[1], wt_w[:], wt_s[:], -1.0, 1))
-        for t in range(PACK):
-            for h in range(HALVES):
-                if (t, h) not in gates:
-                    gates[(t, h)] = gate(t, h)
+        def mix(t, first, last):
+            spans = [(lo, min(lo + HALF, last)) for lo in range(first, last, HALF)]
+            diff = [turned.tile([P, hi - lo], F32, name="diff", tag="diff") for lo, hi in spans]
+            minus = [turned.tile([P, hi - lo], F32, name="minus", tag="minus") for lo, hi in spans]
 
-        for t, tenant in ((2, "tab2_w"), (3, "tab2_s")):
-            page = keep.tile([P, T], F32, name="page%d" % t, tag=tenant, align_bytes=64)
-            nc.gpsimd.memset(page[:], 0.0)
-            pages.append(page)
+            def block(source, j):
+                return source[j // HALF][:, j % HALF // P, t, :]
 
-        woven = [keep.tile([P, CHUNK, PACK], BF16, name="woven%d" % c, align_bytes=64) for c in range(CHUNKS)]
-        rows = out_0.rearrange("(p t) c -> p t c", t=PACK)
-
-        def mix(t, h):
-            diff = turned.tile([P, HALF], F32, name="diff", tag="diff")
-            text = turned.tile([P, HALF], F32, name="text", tag="text")
-            for blk in range(BLOCKS):
-                cols = slice(blk * P, (blk + 1) * P)
-                nc.tensor.matmul(diff[:, cols], av[h][blk][:, t, :], ident[:], start=True, stop=False, is_transpose=True)
-                nc.tensor.matmul(diff[:, cols], neg_at[h][blk][:, t, :], ident[:], start=False, stop=True, is_transpose=True)
-            for blk in range(BLOCKS):
-                cols = slice(blk * P, (blk + 1) * P)
-                nc.tensor.transpose(text[:, cols], neg_at[h][blk][:, t, :], ident[:])
-            gated = ring.tile([P, HALF], F32, name="gated", tag="gated", align_bytes=64)
-            nc.vector.scalar_tensor_tensor(gated[:], gates[(t, h)][:], 1.0, diff[:], ALU.add, ALU.mult)
-            mixed = ring.tile([P, HALF], F32, name="mixed", tag="mixed", align_bytes=64)
-            nc.vector.scalar_tensor_tensor(mixed[:], gated[:], 0.5, text[:], ALU.mult, ALU.subtract)
+            for bank, (lo, hi) in zip(diff, spans):
+                for j in range(lo, hi, P):
+                    nc.tensor.matmul(bank[:, j - lo : j - lo + P], block(av, j), ident[:],
+                                     start=j == lo, stop=False, is_transpose=True)
+                for j in range(lo, hi, P):
+                    nc.tensor.matmul(bank[:, j - lo : j - lo + P], block(neg_at, j), ident[:],
+                                     start=False, stop=j + P == hi, is_transpose=True)
+            for bank, (lo, hi) in zip(minus, spans):
+                for j in range(lo, hi, P):
+                    nc.tensor.transpose(bank[:, j - lo : j - lo + P], block(neg_at, j), ident[:])
+            gated = ring.tile([P, last - first], F32, name="gated", tag="gated", align_bytes=64)
+            mixed = ring.tile([P, last - first], F32, name="mixed", tag="mixed", align_bytes=64)
+            for bank, (lo, hi) in zip(diff, spans):
+                nc.vector.scalar_tensor_tensor(
+                    gated[:, lo - first : hi - first], gates[t][:, lo:hi], 1.0, bank[:], ALU.add, ALU.mult)
+            for bank, (lo, hi) in zip(minus, spans):
+                nc.vector.scalar_tensor_tensor(
+                    mixed[:, lo - first : hi - first], gated[:, lo - first : hi - first], 0.5, bank[:],
+                    ALU.mult, ALU.subtract)
             return mixed
 
-        def place(t, h, mixed):
-            nc.vector.tensor_tensor(
-                pages[t][:].indirect(list1[:, h * HALF // 16 : (h + 1) * HALF // 16]),
-                mixed[:], wgo_sb[:, h * HALF : (h + 1) * HALF], ALU.mult,
-            )
+        woven = [keep.tile([P, CHUNK, PACK], BF16, name="woven%d" % c, align_bytes=64) for c in range(CHUNKS)]
+        out_rows = out_0.rearrange("(p t) c -> p t c", t=PACK)
 
-        def weave(t):
+        def place(t, first, last, mixed):
+            page = page_tiles[t % PAGE_TILES]
+            nc.vector.tensor_tensor(
+                page[:].indirect(entries(list1, first, last)), mixed[:], wgo_sb[:, first:last], ALU.mult)
+            if last < J:
+                return
+            nc.sync.dma_start(out=out_rows[:, t, :], in_=page[:])
             for c in range(CHUNKS):
                 cols = slice(c * CHUNK, (c + 1) * CHUNK)
                 if t == PACK - 2 and c < VECTOR_CHUNKS:
-                    nc.scalar.copy(woven[c][:, :, t:], pages[t][:, cols].unsqueeze(2).to_broadcast([P, CHUNK, 2]))
+                    nc.scalar.copy(woven[c][:, :, t:], page[:, cols].unsqueeze(2).to_broadcast([P, CHUNK, 2]))
                 elif t == PACK - 1 and c < VECTOR_CHUNKS:
-                    nc.vector.tensor_copy(woven[c][:, :, t], pages[t][:, cols])
+                    nc.vector.tensor_copy(woven[c][:, :, t], page[:, cols])
                 else:
-                    nc.scalar.copy(woven[c][:, :, t], pages[t][:, cols])
+                    nc.scalar.copy(woven[c][:, :, t], page[:, cols])
 
-        units = [(t, h) for t in range(PACK) for h in range(HALVES)]
-        ready = mix(*units[0])
-        for u, (t, h) in enumerate(units):
-            following = mix(*units[u + 1]) if u + 1 < len(units) else None
-            place(t, h, ready)
-            ready = following
-            if h == HALVES - 1:
-                nc.sync.dma_start(out=rows[:, t, :], in_=pages[t][:])
-                weave(t)
+        picture(0, HALF)
+        text(0, HALF)
+        gate(0, 0)
+        gate(1, 0)
+        steps = [(t, first, first + HALF) for first in (0, HALF) for t in range(PAGE_TILES)]
+        steps = steps + [(t, 0, J) for t in range(PAGE_TILES, PACK)]
+        ready = mix(*steps[0])
+        for step, following in zip(steps, steps[1:] + [None]):
+            if following == (0, HALF, J):
+                picture(HALF, J)
+                text(HALF, J)
+                for t in range(PACK):
+                    for h in range(1 if t < PAGE_TILES else 0, 2):
+                        gate(t, h)
+            ahead = mix(*following) if following else None
+            place(*step, ready)
+            ready = ahead
 
-        out_words = out_1[0].rearrange("p c i -> p (c i)").bitcast(I32)
+        out_words = words_of(out_1)
         planes = [keep.tile([P, 2 * CHUNK], U8, name="plane%d" % g, align_bytes=64) for g in range(CHUNKS // 2)]
         for c in range(CHUNKS):
             codes = keep.tile([P, CHUNK], U32, name="codes%d" % c, align_bytes=64)

@@ -22,13 +22,13 @@ P = 128
 PACK = 4
 PER_COLUMN = 16
 HALF = 512
+SEGMENT = 256
 BLOCKS = HALF // P
 CHUNK = 512
 CHUNKS = T // CHUNK
 VECTOR_CHUNKS = 2
-SUM_BANKS = 4
-PAGE_TILES = 2
-ZT_ROW, ZV_ROW = 0, 4
+SUM_BANKS = 6
+ZT_ROW, ZV_ROW, WV_ROW = 0, 4, 8
 
 
 def load_plane(nc, plane, first_row, scales):
@@ -55,196 +55,194 @@ def tile_list_gmu_tanh_scatP_kernel(
     with ExitStack() as ctx:
         keep = ctx.enter_context(tc.tile_pool(name="keep", bufs=1))
         ring = ctx.enter_context(tc.tile_pool(name="ring", bufs=3))
+        single = ctx.enter_context(tc.tile_pool(name="single", bufs=1))
         sums = ctx.enter_context(tc.psum_pool(name="sums", bufs=1))
-        turned = ctx.enter_context(tc.psum_pool(name="turned", bufs=2))
 
         banks_taken = []
 
         def next_bank():
             banks_taken.append(len(banks_taken) % SUM_BANKS)
-            return sums.tile([P, N], F32, name="sum%d" % len(banks_taken), tag="bank%d" % banks_taken[-1])
+            return sums.tile([P, HALF], F32, name="sum%d" % len(banks_taken), tag="bank%d" % banks_taken[-1])
 
         list1 = keep.tile([P, J // PER_COLUMN], U16, name="list1")
         list2 = keep.tile([P, J // PER_COLUMN], U16, name="list2")
         tab_w = keep.tile([P, T], U32, name="tab_w", align_bytes=64)
         tab_s = keep.tile([P, T], U8, name="tab_s", align_bytes=64)
         tab2_w = keep.tile([P, T], U32, name="tab2_w", align_bytes=64)
-        tab2_s = keep.tile([P, T], U8, name="tab2_s", tag="tab2_s", align_bytes=64)
-        z_raw_s = keep.tile([P, N], U8, name="z_raw_s", tag="z_raw_s", align_bytes=64)
-        wv_s = keep.tile([P, N], U8, name="wv_s", align_bytes=64)
-        wv_w = keep.tile([P, N], U32, name="wv_w", align_bytes=64)
+        tab2_s = keep.tile([P, T], U8, name="tab2_s", align_bytes=64)
+        raw_s = keep.tile([P, N], U8, name="raw_s", tag="raw_s", align_bytes=64)
+        wv_raw = keep.tile([P, N], I32, name="wv_raw", align_bytes=64)
         zv_raw = keep.tile([P, N], I32, name="zv_raw", align_bytes=64)
-        zt_raw = keep.tile([P, 2 * N], U8, name="zt_raw", align_bytes=64)
-        wt_raw = keep.tile([P, PACK, N], F32, name="wt_raw", tag="wt_raw", align_bytes=64)
+        zt_raw = keep.tile([P, 2 * N], U8, name="zt_raw", tag="zt_raw", align_bytes=64)
+        wt_raw = keep.tile([P, PACK, N], F32, name="wt_raw", align_bytes=64)
         bias = keep.tile([P, PACK], F32, name="bias")
-        half_bias = keep.tile([P, PACK], F32, name="half_bias")
-        wgo_sb = keep.tile([P, J], F32, name="wgo_sb", align_bytes=64)
+        wgo_rows = keep.tile([P, P], F32, name="wgo_rows", align_bytes=64)
+        wgo_cols = keep.tile([P, J // P], F32, name="wgo_cols", align_bytes=64)
         ident = keep.tile([P, P], F32, name="ident", align_bytes=64)
         cleared = keep.tile([P, 1], F32, name="cleared")
+        half = keep.tile([P, 1], F32, name="half")
         no_bias = keep.tile([P, 1], F32, name="no_bias")
 
         nc.gpsimd.memset(tab_s[:].bitcast(I32), 0)
         nc.vector.memset(cleared[:], 0.0)
         nc.vector.memset(tab2_s[:].bitcast(I32), 0)
-        nc.vector.memset(wv_s[:].bitcast(I32), 0)
-        nc.vector.memset(z_raw_s[:].bitcast(I32), 0)
-        nc.scalar.activation(no_bias[:], cleared[:], ACT.Tanh)
+        nc.vector.memset(raw_s[:].bitcast(I32), 0)
+        nc.vector.memset(wgo_rows[:], 0.0)
+        nc.scalar.activation(half[:], cleared[:], ACT.Sigmoid)
+        nc.scalar.activation(no_bias[:], half[:], ACT.Tanh, scale=0.0)
 
         nc.sync.dma_start(list1[:], offs)
-        nc.sync.dma_start(out=wv_w[:].bitcast(I32), in_=words_of(wv_words))
         load_plane(nc, tab_s, 0, tab_scales)
-        nc.sync.dma_start(out=tab_w[:].bitcast(I32), in_=words_of(tab_words))
-        nc.sync.dma_start(out=wt_raw[:], in_=wt.rearrange("(p i) n -> p i n", i=PACK))
         nc.sync.dma_start(list2[:], offs2)
+        nc.sync.dma_start(out=wt_raw[:], in_=wt.rearrange("(p i) n -> p i n", i=PACK))
+        nc.sync.dma_start(out=tab_w[:].bitcast(I32), in_=words_of(tab_words))
         load_plane(nc, tab2_s, 0, tab2_scales)
-        nc.sync.dma_start(out=tab2_w[:].bitcast(I32), in_=words_of(tab2_words))
-        load_plane(nc, wv_s, 0, wv_scales)
+        nc.sync.dma_start(out=wv_raw[:], in_=words_of(wv_words))
         nc.sync.dma_start(out=zv_raw[:], in_=words_of(zv_words))
+        nc.sync.dma_start(out=tab2_w[:].bitcast(I32), in_=words_of(tab2_words))
         nc.sync.dma_start(out=zt_raw[:].bitcast(I32), in_=zt_words[0].bitcast(I32))
-        load_plane(nc, z_raw_s, ZV_ROW, zv_scales)
-        load_plane(nc, z_raw_s, ZT_ROW, zt_scales)
+        load_plane(nc, raw_s, WV_ROW, wv_scales)
+        load_plane(nc, raw_s, ZV_ROW, zv_scales)
+        load_plane(nc, raw_s, ZT_ROW, zt_scales)
         nc.sync.dma_start(out=bias[:], in_=b.rearrange("(p t) -> p t", t=PACK))
-        nc.sync.dma_start(out=wgo_sb[:], in_=wgo)
+        nc.sync.dma_start(out=wgo_rows[0 : J // P, :], in_=wgo[0:1, :].rearrange("o (r j) -> (o r) j", j=P))
 
-        page_tiles = [keep.tile([P, T], F32, name="page%d" % t, align_bytes=64) for t in range(PAGE_TILES)]
-        nc.vector.memset(page_tiles[0][:].bitcast(I32), 0)
-        for c in range(CHUNKS):
-            nc.gpsimd.memset(page_tiles[1][:, c * CHUNK : (c + 1) * CHUNK], 0.0)
+        pages = [keep.tile([P, T], F32, name="page%d" % t, align_bytes=64) for t in range(PACK)]
         make_identity(nc, ident[:])
+        nc.vector.memset(pages[0][:].bitcast(I32), 0)
+        for t in range(1, PACK):
+            for c in range(CHUNKS):
+                nc.gpsimd.memset(pages[t][:, c * CHUNK : (c + 1) * CHUNK], 0.0)
 
-        def pick(name, window, dtype, offsets, h, tag=None):
-            got = keep.tile([P, HALF], dtype, name="%s%d" % (name, h), tag=tag or "%s%d" % (name, h), align_bytes=64)
-            nc.vector.tensor_copy(got[:], window[:].indirect(entries(offsets, h * HALF, (h + 1) * HALF)))
+        def pick(name, window, dtype, offsets, first, last, tag=None):
+            got = keep.tile([P, last - first], dtype, name="%s%d" % (name, first),
+                            tag=tag or "%s%d" % (name, first), align_bytes=64)
+            nc.vector.tensor_copy(got[:], window[:].indirect(entries(offsets, first, last)))
             return got
 
-        v_s = [pick("v_s", tab_s, U8, list1, h) for h in range(2)]
-        v_w = [pick("v_w", tab_w, U32, list1, h) for h in range(2)]
-        v2_s = [pick("v2_s", tab2_s, U8, list2, h) for h in range(2)]
+        v_s = pick("v_s", tab_s, U8, list1, 0, J)
+        v2_s = pick("v2_s", tab2_s, U8, list2, 0, J)
+        v_w = [pick("v_w", tab_w, U32, list1, 0, HALF)]
 
-        wt_bf = keep.tile([P, N, PACK], BF16, name="wt_bf", align_bytes=64)
+        wt_bf = keep.tile([P, PACK, P, PACK], BF16, name="wt_bf", align_bytes=64)
         nc.scalar.copy(
-            wt_bf[:].rearrange("p (c e) i -> p c i e", e=4),
-            wt_raw[:].rearrange("p i (c e) -> p c i e", e=4),
+            wt_bf[:].rearrange("p t m i -> p m i t"),
+            wt_raw[:].rearrange("p i (m t) -> p m i t", t=PACK),
         )
-        wt_w = keep.tile([P, N], U32, name="wt_w", tag="tab2_s", align_bytes=64)
-        wt_s = keep.tile([P, N], U8, name="wt_s", align_bytes=64)
-        nc.vector.quantize_mx(out=wt_w[:].bitcast(FP8X4), scales=wt_s[:], in_=wt_bf[:].rearrange("p n i -> p (n i)"))
-        v2_w = [pick("v2_w", tab2_w, U32, list2, 0)]
+        wt_w = keep.tile([P, PACK, P], U32, name="wt_w", align_bytes=64)
+        wt_s = keep.tile([P, PACK, P], U8, name="wt_s", align_bytes=64)
+        nc.vector.quantize_mx(
+            out=wt_w[:].rearrange("p t m -> p (t m)").bitcast(FP8X4), scales=wt_s[:].rearrange("p t m -> p (t m)"),
+            in_=wt_bf[:].rearrange("p t m i -> p (t m i)"))
 
+        wv_w = keep.tile([P, PACK, P], I32, name="wv_w", align_bytes=64)
         zv_w = keep.tile([P, PACK, P], I32, name="zv_w", align_bytes=64)
         zt_w = keep.tile([P, PACK, P, 2], U8, name="zt_w", align_bytes=64)
-        z_s = keep.tile([P, PACK, P], U8, name="z_s", align_bytes=64)
+        dealt_s = keep.tile([P, PACK, P], U8, name="dealt_s", align_bytes=64)
+        nc.vector.tensor_copy(wv_w[:], wv_raw[:].rearrange("p (m t) -> p t m", t=PACK))
         nc.vector.tensor_copy(zv_w[:], zv_raw[:].rearrange("p (m t) -> p t m", t=PACK))
+        v2_w = [pick("v2_w", tab2_w, U32, list2, 0, HALF)]
         nc.vector.tensor_copy(zt_w[:], zt_raw[:].rearrange("p (m t e) -> p t m e", t=PACK, e=2))
-        nc.vector.tensor_copy(z_s[:], z_raw_s[:].rearrange("p (m t) -> p t m", t=PACK))
-        nc.scalar.activation(half_bias[:], bias[:], ACT.Copy, scale=0.5)
-        v2_w.append(pick("v2_w", tab2_w, U32, list2, 1, "z_raw_s"))
+        nc.vector.tensor_copy(dealt_s[:], raw_s[:].rearrange("p (m t) -> p t m", t=PACK))
+        v_w.append(pick("v_w", tab_w, U32, list1, HALF, J, "zt_raw"))
+        v2_w.append(pick("v2_w", tab2_w, U32, list2, HALF, J, "raw_s"))
 
-        av = [keep.tile([P, BLOCKS, PACK, P], F32, name="av0", tag="wt_raw", align_bytes=64),
-              keep.tile([P, BLOCKS, PACK, P], F32, name="av1", align_bytes=64)]
-        neg_at = [keep.tile([P, BLOCKS, PACK, P], F32, name="neg_at%d" % h, align_bytes=64) for h in range(2)]
+        def picture_pass(acc, weight_w, row, t, h, start, stop):
+            nc.tensor.matmul_mx(
+                out=acc[:], lhsT=weight_w[:, t, :].bitcast(FP8X4), lhsT_scale=dealt_s[row:, t, :],
+                rhs=v_w[h][:].bitcast(FP8X4), rhs_scale=v_s[:, h * HALF : (h + 1) * HALF], start=start, stop=stop,
+            )
 
-        def branch(result, got_w, got_s, weight_w, weight_s, sign, first, last):
-            for j in range(first, last, P):
-                h, cols = j // HALF, slice(j % HALF, j % HALF + P)
-                acc = next_bank()
-                nc.tensor.matmul_mx(
-                    out=acc[:], lhsT=got_w[h][:, cols].bitcast(FP8X4), lhsT_scale=got_s[h][:, cols],
-                    rhs=weight_w[:].bitcast(FP8X4), rhs_scale=weight_s[:], start=True, stop=True,
-                )
-                nc.scalar.activation(
-                    result[h][:, j % HALF // P, :, :], acc[:].rearrange("j (m t) -> j t m", t=PACK),
-                    ACT.Tanh, bias=no_bias[:], scale=sign,
-                )
+        def text_pass(acc, weight, weight_s, h, start, stop):
+            nc.tensor.matmul_mx(
+                out=acc[:], lhsT=weight, lhsT_scale=weight_s,
+                rhs=v2_w[h][:].bitcast(FP8X4), rhs_scale=v2_s[:, h * HALF : (h + 1) * HALF], start=start, stop=stop,
+            )
 
-        def picture(first, last):
-            branch(av, v_w, v_s, wv_w, wv_s, 1.0, first, last)
-
-        def text(first, last):
-            branch(neg_at, v2_w, v2_s, wt_w, wt_s, -1.0, first, last)
-
-        gates = [keep.tile([P, J], F32, name="gates%d" % t, align_bytes=64) for t in range(PACK)]
-
-        def gate(t, h):
+        def activate(t, h):
+            av = keep.tile([P, HALF], F32, name="av%d%d" % (t, h), align_bytes=64)
+            at = keep.tile([P, HALF], F32, name="at%d%d" % (t, h), align_bytes=64)
+            gate = keep.tile([P, HALF], F32, name="gate%d%d" % (t, h), align_bytes=64)
             acc = next_bank()
-            nc.tensor.matmul_mx(
-                out=acc[:], lhsT=zv_w[:, t, :].bitcast(FP8X4), lhsT_scale=z_s[ZV_ROW:, t, :],
-                rhs=v_w[h][:].bitcast(FP8X4), rhs_scale=v_s[h][:], start=True, stop=False,
-            )
-            nc.tensor.matmul_mx(
-                out=acc[:], lhsT=zt_w[:, t, :, :].rearrange("p m e -> p (m e)").bitcast(FP4X4),
-                lhsT_scale=z_s[ZT_ROW:, t, :],
-                rhs=v2_w[h][:].bitcast(FP8X4), rhs_scale=v2_s[h][:], start=False, stop=True,
-            )
-            nc.scalar.activation(
-                gates[t][:, h * HALF : (h + 1) * HALF], acc[:], ACT.Tanh, bias=half_bias[:, t : t + 1], scale=0.5,
-            )
+            text_pass(acc, wt_w[:, t, :].bitcast(FP8X4), wt_s[:, t, :], h, True, True)
+            nc.scalar.activation(at[:], acc[:], ACT.Tanh, bias=no_bias[:])
+            acc = next_bank()
+            picture_pass(acc, wv_w, WV_ROW, t, h, True, True)
+            nc.scalar.activation(av[:], acc[:], ACT.Tanh, bias=no_bias[:])
+            acc = next_bank()
+            picture_pass(acc, zv_w, ZV_ROW, t, h, True, False)
+            text_pass(acc, zt_w[:, t, :, :].rearrange("p m e -> p (m e)").bitcast(FP4X4), dealt_s[ZT_ROW:, t, :],
+                      h, False, True)
+            nc.scalar.activation(gate[:], acc[:], ACT.Sigmoid, bias=bias[:, t : t + 1])
+            return av, at, gate
 
-        def mix(t, first, last):
-            spans = [(lo, min(lo + HALF, last)) for lo in range(first, last, HALF)]
-            diff = [turned.tile([P, hi - lo], F32, name="diff", tag="diff") for lo, hi in spans]
-            minus = [turned.tile([P, hi - lo], F32, name="minus", tag="minus") for lo, hi in spans]
+        def differ(engine, av, at, gate):
+            diff = single.tile([P, HALF], F32, name="diff", tag="diff", align_bytes=64)
+            engine.tensor_tensor(diff[:], av[:], at[:], ALU.subtract)
+            return diff
 
-            def block(source, j):
-                return source[j // HALF][:, j % HALF // P, t, :]
+        def weigh(engine, diff, gate):
+            gated = ring.tile([P, HALF], F32, name="gated", tag="gated", align_bytes=64)
+            engine.tensor_tensor(gated[:], diff[:], gate[:], ALU.mult)
+            return gated
 
-            for bank, (lo, hi) in zip(diff, spans):
-                for j in range(lo, hi, P):
-                    nc.tensor.matmul(bank[:, j - lo : j - lo + P], block(av, j), ident[:],
-                                     start=j == lo, stop=False, is_transpose=True)
-                for j in range(lo, hi, P):
-                    nc.tensor.matmul(bank[:, j - lo : j - lo + P], block(neg_at, j), ident[:],
-                                     start=False, stop=j + P == hi, is_transpose=True)
-            for bank, (lo, hi) in zip(minus, spans):
-                for j in range(lo, hi, P):
-                    nc.tensor.transpose(bank[:, j - lo : j - lo + P], block(neg_at, j), ident[:])
-            gated = ring.tile([P, last - first], F32, name="gated", tag="gated", align_bytes=64)
-            mixed = ring.tile([P, last - first], F32, name="mixed", tag="mixed", align_bytes=64)
-            for bank, (lo, hi) in zip(diff, spans):
-                nc.vector.scalar_tensor_tensor(
-                    gated[:, lo - first : hi - first], gates[t][:, lo:hi], 1.0, bank[:], ALU.add, ALU.mult)
-            for bank, (lo, hi) in zip(minus, spans):
-                nc.vector.scalar_tensor_tensor(
-                    mixed[:, lo - first : hi - first], gated[:, lo - first : hi - first], 0.5, bank[:],
-                    ALU.mult, ALU.subtract)
+        def join(engine, gated, at):
+            mixed = ring.tile([P, HALF], F32, name="mixed", tag="mixed", align_bytes=64)
+            engine.tensor_tensor(mixed[:], gated[:], at[:], ALU.add)
             return mixed
 
-        woven = [keep.tile([P, CHUNK, PACK], BF16, name="woven%d" % c, align_bytes=64) for c in range(CHUNKS)]
+        def spread_wgo():
+            turned = next_bank()
+            nc.tensor.transpose(turned[:, 0:P], wgo_rows[:], ident[:])
+            nc.scalar.copy(wgo_cols[:], turned[:, 0 : J // P])
+            banks = [sums.tile([P, HALF], F32, name="wgo%d" % h) for h in range(2)]
+            for r in range(J // P):
+                nc.tensor.transpose(banks[r // BLOCKS][:, r % BLOCKS * P : (r % BLOCKS + 1) * P],
+                                    wgo_cols[:, r : r + 1].to_broadcast([P, P]), ident[:])
+            return banks
+
         out_rows = out_0.rearrange("(p t) c -> p t c", t=PACK)
 
-        def place(t, first, last, mixed):
-            page = page_tiles[t % PAGE_TILES]
-            nc.vector.tensor_tensor(
-                page[:].indirect(entries(list1, first, last)), mixed[:], wgo_sb[:, first:last], ALU.mult)
-            if last < J:
-                return
-            nc.sync.dma_start(out=out_rows[:, t, :], in_=page[:])
+        def place(t, h, mixed):
+            weighted = ring.tile([P, HALF], F32, name="weighted", tag="weighted", align_bytes=64)
+            for lo in range(0, HALF, SEGMENT):
+                cols = slice(lo, lo + SEGMENT)
+                nc.vector.tensor_tensor(weighted[:, cols], mixed[:, cols], wgo_banks[h][:, cols], ALU.mult)
+            for lo in range(0, HALF, SEGMENT):
+                first = h * HALF + lo
+                nc.vector.tensor_copy(
+                    pages[t][:].indirect(entries(list1, first, first + SEGMENT)), weighted[:, lo : lo + SEGMENT])
+            if h == 1:
+                nc.sync.dma_start(out=out_rows[:, t, :], in_=pages[t][:])
+
+        def weave(t):
             for c in range(CHUNKS):
                 cols = slice(c * CHUNK, (c + 1) * CHUNK)
                 if t == PACK - 2 and c < VECTOR_CHUNKS:
-                    nc.scalar.copy(woven[c][:, :, t:], page[:, cols].unsqueeze(2).to_broadcast([P, CHUNK, 2]))
+                    nc.scalar.copy(woven[c][:, :, t:], pages[t][:, cols].unsqueeze(2).to_broadcast([P, CHUNK, 2]))
                 elif t == PACK - 1 and c < VECTOR_CHUNKS:
-                    nc.vector.tensor_copy(woven[c][:, :, t], page[:, cols])
+                    nc.vector.tensor_copy(woven[c][:, :, t], pages[t][:, cols])
                 else:
-                    nc.scalar.copy(woven[c][:, :, t], page[:, cols])
+                    nc.scalar.copy(woven[c][:, :, t], pages[t][:, cols])
 
-        picture(0, HALF)
-        text(0, HALF)
-        gate(0, 0)
-        gate(1, 0)
-        steps = [(t, first, first + HALF) for first in (0, HALF) for t in range(PAGE_TILES)]
-        steps = steps + [(t, 0, J) for t in range(PAGE_TILES, PACK)]
-        ready = mix(*steps[0])
-        for step, following in zip(steps, steps[1:] + [None]):
-            if following == (0, HALF, J):
-                picture(HALF, J)
-                text(HALF, J)
-                for t in range(PACK):
-                    for h in range(1 if t < PAGE_TILES else 0, 2):
-                        gate(t, h)
-            ahead = mix(*following) if following else None
-            place(*step, ready)
-            ready = ahead
+        units = [(t, h) for t in range(PACK) for h in range(2)]
+        made = [activate(*units[0])]
+        wgo_banks = spread_wgo()
+        made = made + [activate(*unit) for unit in units[1:]]
+        av, at, gate = made[0]
+        first_diff = keep.tile([P, HALF], F32, name="first_diff", align_bytes=64)
+        nc.vector.tensor_tensor(first_diff[:], av[:], at[:], ALU.subtract)
+        place(*units[0], join(nc.vector, weigh(nc.vector, first_diff, gate), at))
+        diff = differ(nc.gpsimd, *made[1])
+        for i in range(1, len(units)):
+            gated = weigh(nc.gpsimd, diff, made[i][2])
+            if i + 1 < len(units):
+                diff = differ(nc.gpsimd, *made[i + 1])
+            place(*units[i], join(nc.gpsimd, gated, made[i][1]))
+        woven = [keep.tile([P, CHUNK, PACK], BF16, name="woven%d" % c, tag=tag, align_bytes=64)
+                 for c, tag in enumerate(["zt_raw", "raw_s", "v_s0", "v2_s0"])]
+        for t in range(PACK):
+            weave(t)
 
         out_words = words_of(out_1)
         planes = [keep.tile([P, 2 * CHUNK], U8, name="plane%d" % g, align_bytes=64) for g in range(CHUNKS // 2)]

@@ -22,21 +22,21 @@ P = 128
 PACK = 4
 PER_COLUMN = 16
 HALF = 512
-SEGMENT = 256
 BLOCKS = HALF // P
 CHUNK = 512
 CHUNKS = T // CHUNK
 VECTOR_CHUNKS = 2
-SUM_BANKS = 6
-ZT_ROW, ZV_ROW, WV_ROW = 0, 4, 8
+EARLY_UNITS = 4
+RING_BANKS = 3
+ZT_ROW, ZV_ROW = 0, 4
 
 
-def load_plane(nc, plane, first_row, scales):
-    for q in range(4):
-        nc.sync.dma_start(
-            out=plane[32 * q + first_row : 32 * q + first_row + 4, :].bitcast(I32),
-            in_=scales[0, 4 * q : 4 * q + 4, :].bitcast(I32),
-        )
+def plane_loads(plane, first_row, scales):
+    return [
+        (plane[32 * q + first_row : 32 * q + first_row + 4, :].bitcast(I32),
+         scales[0, 4 * q : 4 * q + 4, :].bitcast(I32))
+        for q in range(4)
+    ]
 
 
 def words_of(dram):
@@ -58,11 +58,12 @@ def tile_list_gmu_tanh_scatP_kernel(
         single = ctx.enter_context(tc.tile_pool(name="single", bufs=1))
         sums = ctx.enter_context(tc.psum_pool(name="sums", bufs=1))
 
-        banks_taken = []
+        taken = {"early": [], "late": []}
 
-        def next_bank():
-            banks_taken.append(len(banks_taken) % SUM_BANKS)
-            return sums.tile([P, HALF], F32, name="sum%d" % len(banks_taken), tag="bank%d" % banks_taken[-1])
+        def next_bank(kind):
+            taken[kind].append(len(taken[kind]) % RING_BANKS)
+            return sums.tile([P, HALF], F32, name="%s%d" % (kind, len(taken[kind])),
+                             tag="%s%d" % (kind, taken[kind][-1]))
 
         list1 = keep.tile([P, J // PER_COLUMN], U16, name="list1")
         list2 = keep.tile([P, J // PER_COLUMN], U16, name="list2")
@@ -70,7 +71,8 @@ def tile_list_gmu_tanh_scatP_kernel(
         tab_s = keep.tile([P, T], U8, name="tab_s", align_bytes=64)
         tab2_w = keep.tile([P, T], U32, name="tab2_w", align_bytes=64)
         tab2_s = keep.tile([P, T], U8, name="tab2_s", align_bytes=64)
-        raw_s = keep.tile([P, N], U8, name="raw_s", tag="raw_s", align_bytes=64)
+        z_raw_s = single.tile([P, N], U8, name="z_raw_s", tag="diff", align_bytes=64)
+        wv_raw_s = keep.tile([P, N], U8, name="wv_raw_s", align_bytes=64)
         wv_raw = keep.tile([P, N], I32, name="wv_raw", align_bytes=64)
         zv_raw = keep.tile([P, N], I32, name="zv_raw", align_bytes=64)
         zt_raw = keep.tile([P, 2 * N], U8, name="zt_raw", tag="zt_raw", align_bytes=64)
@@ -85,34 +87,42 @@ def tile_list_gmu_tanh_scatP_kernel(
 
         nc.gpsimd.memset(tab_s[:].bitcast(I32), 0)
         nc.vector.memset(cleared[:], 0.0)
-        nc.vector.memset(tab2_s[:].bitcast(I32), 0)
-        nc.vector.memset(raw_s[:].bitcast(I32), 0)
-        nc.vector.memset(wgo_rows[:], 0.0)
+        nc.gpsimd.memset(tab2_s[:].bitcast(I32), 0)
+        nc.vector.memset(wv_raw_s[:].bitcast(I32), 0)
+        nc.vector.memset(z_raw_s[:].bitcast(I32), 0)
+        nc.gpsimd.memset(wgo_rows[:], 0.0)
         nc.scalar.activation(half[:], cleared[:], ACT.Sigmoid)
         nc.scalar.activation(no_bias[:], half[:], ACT.Tanh, scale=0.0)
 
-        nc.sync.dma_start(list1[:], offs)
-        load_plane(nc, tab_s, 0, tab_scales)
-        nc.sync.dma_start(list2[:], offs2)
-        nc.sync.dma_start(out=wt_raw[:], in_=wt.rearrange("(p i) n -> p i n", i=PACK))
-        nc.sync.dma_start(out=tab_w[:].bitcast(I32), in_=words_of(tab_words))
-        load_plane(nc, tab2_s, 0, tab2_scales)
-        nc.sync.dma_start(out=wv_raw[:], in_=words_of(wv_words))
-        nc.sync.dma_start(out=zv_raw[:], in_=words_of(zv_words))
-        nc.sync.dma_start(out=tab2_w[:].bitcast(I32), in_=words_of(tab2_words))
-        nc.sync.dma_start(out=zt_raw[:].bitcast(I32), in_=zt_words[0].bitcast(I32))
-        load_plane(nc, raw_s, WV_ROW, wv_scales)
-        load_plane(nc, raw_s, ZV_ROW, zv_scales)
-        load_plane(nc, raw_s, ZT_ROW, zt_scales)
-        nc.sync.dma_start(out=bias[:], in_=b.rearrange("(p t) -> p t", t=PACK))
-        nc.sync.dma_start(out=wgo_rows[0 : J // P, :], in_=wgo[0:1, :].rearrange("o (r j) -> (o r) j", j=P))
+        tab_planes = plane_loads(tab_s, 0, tab_scales)
+        tab2_planes = plane_loads(tab2_s, 0, tab2_scales)
+        wv_planes = plane_loads(wv_raw_s, 0, wv_scales)
+        z_planes = plane_loads(z_raw_s, ZV_ROW, zv_scales) + plane_loads(z_raw_s, ZT_ROW, zt_scales)
+        loads = (
+            [(list1[:], offs), (list2[:], offs2)] + tab_planes
+            + [(tab_w[:].bitcast(I32), words_of(tab_words)),
+               (wgo_rows[0 : J // P, :], wgo[0:1, :].rearrange("o (r j) -> (o r) j", j=P))]
+            + tab2_planes
+            + [(wt_raw[:], wt.rearrange("(p i) n -> p i n", i=PACK)),
+               (wv_raw[:], words_of(wv_words))]
+            + wv_planes
+            + [(zv_raw[:], words_of(zv_words)), (tab2_w[:].bitcast(I32), words_of(tab2_words))]
+            + z_planes[:-2]
+            + [(zt_raw[:].bitcast(I32), zt_words[0].bitcast(I32)), (bias[:], b.rearrange("(p t) -> p t", t=PACK))]
+        )
+        for out, in_ in loads:
+            nc.sync.dma_start(out, in_)
+        for out, in_ in z_planes[-2:]:
+            nc.gpsimd.dma_start(out, in_)
 
-        pages = [keep.tile([P, T], F32, name="page%d" % t, align_bytes=64) for t in range(PACK)]
+        def clear(page):
+            for c in range(CHUNKS):
+                nc.gpsimd.memset(page[:, c * CHUNK : (c + 1) * CHUNK], 0.0)
+
+        pages = [keep.tile([P, T], F32, name="page%d" % t, align_bytes=64) for t in range(2)]
         make_identity(nc, ident[:])
         nc.vector.memset(pages[0][:].bitcast(I32), 0)
-        for t in range(1, PACK):
-            for c in range(CHUNKS):
-                nc.gpsimd.memset(pages[t][:, c * CHUNK : (c + 1) * CHUNK], 0.0)
+        clear(pages[1])
 
         def pick(name, window, dtype, offsets, first, last, tag=None):
             got = keep.tile([P, last - first], dtype, name="%s%d" % (name, first),
@@ -121,8 +131,8 @@ def tile_list_gmu_tanh_scatP_kernel(
             return got
 
         v_s = pick("v_s", tab_s, U8, list1, 0, J)
+        v_w = pick("v_w", tab_w, U32, list1, 0, J)
         v2_s = pick("v2_s", tab2_s, U8, list2, 0, J)
-        v_w = [pick("v_w", tab_w, U32, list1, 0, HALF)]
 
         wt_bf = keep.tile([P, PACK, P, PACK], BF16, name="wt_bf", align_bytes=64)
         nc.scalar.copy(
@@ -138,19 +148,22 @@ def tile_list_gmu_tanh_scatP_kernel(
         wv_w = keep.tile([P, PACK, P], I32, name="wv_w", align_bytes=64)
         zv_w = keep.tile([P, PACK, P], I32, name="zv_w", align_bytes=64)
         zt_w = keep.tile([P, PACK, P, 2], U8, name="zt_w", align_bytes=64)
-        dealt_s = keep.tile([P, PACK, P], U8, name="dealt_s", align_bytes=64)
-        nc.vector.tensor_copy(wv_w[:], wv_raw[:].rearrange("p (m t) -> p t m", t=PACK))
-        nc.vector.tensor_copy(zv_w[:], zv_raw[:].rearrange("p (m t) -> p t m", t=PACK))
-        v2_w = [pick("v2_w", tab2_w, U32, list2, 0, HALF)]
-        nc.vector.tensor_copy(zt_w[:], zt_raw[:].rearrange("p (m t e) -> p t m e", t=PACK, e=2))
-        nc.vector.tensor_copy(dealt_s[:], raw_s[:].rearrange("p (m t) -> p t m", t=PACK))
-        v_w.append(pick("v_w", tab_w, U32, list1, HALF, J, "zt_raw"))
-        v2_w.append(pick("v2_w", tab2_w, U32, list2, HALF, J, "raw_s"))
+        wv_s = keep.tile([P, PACK, P], U8, name="wv_s", align_bytes=64)
+        z_s = keep.tile([P, PACK, P], U8, name="z_s", align_bytes=64)
+        nc.gpsimd.tensor_copy(wv_w[:], wv_raw[:].rearrange("p (m t) -> p t m", t=PACK))
+        nc.gpsimd.tensor_copy(wv_s[:], wv_raw_s[:].rearrange("p (m t) -> p t m", t=PACK))
+        nc.gpsimd.tensor_copy(zv_w[:], zv_raw[:].rearrange("p (m t) -> p t m", t=PACK))
+        nc.gpsimd.tensor_copy(z_s[:], z_raw_s[:].rearrange("p (m t) -> p t m", t=PACK))
+        nc.gpsimd.tensor_copy(zt_w[:], zt_raw[:].rearrange("p (m t e) -> p t m e", t=PACK, e=2))
+        pages = pages + [keep.tile([P, T], F32, name="page2", tag="zt_raw", align_bytes=64), pages[0]]
+        clear(pages[2])
+        v2_w = [pick("v2_w", tab2_w, U32, list2, first, first + HALF) for first in (0, HALF)]
 
-        def picture_pass(acc, weight_w, row, t, h, start, stop):
+        def picture_pass(acc, weight_w, weight_s, h, start, stop):
+            cols = slice(h * HALF, (h + 1) * HALF)
             nc.tensor.matmul_mx(
-                out=acc[:], lhsT=weight_w[:, t, :].bitcast(FP8X4), lhsT_scale=dealt_s[row:, t, :],
-                rhs=v_w[h][:].bitcast(FP8X4), rhs_scale=v_s[:, h * HALF : (h + 1) * HALF], start=start, stop=stop,
+                out=acc[:], lhsT=weight_w.bitcast(FP8X4), lhsT_scale=weight_s,
+                rhs=v_w[:, cols].bitcast(FP8X4), rhs_scale=v_s[:, cols], start=start, stop=stop,
             )
 
         def text_pass(acc, weight, weight_s, h, start, stop):
@@ -159,22 +172,25 @@ def tile_list_gmu_tanh_scatP_kernel(
                 rhs=v2_w[h][:].bitcast(FP8X4), rhs_scale=v2_s[:, h * HALF : (h + 1) * HALF], start=start, stop=stop,
             )
 
-        def activate(t, h):
+        def picture(t, h, kind):
             av = keep.tile([P, HALF], F32, name="av%d%d" % (t, h), align_bytes=64)
+            acc = next_bank(kind)
+            picture_pass(acc, wv_w[:, t, :], wv_s[:, t, :], h, True, True)
+            nc.scalar.activation(av[:], acc[:], ACT.Tanh, bias=no_bias[:])
+            return av
+
+        def text_and_gate(t, h):
             at = keep.tile([P, HALF], F32, name="at%d%d" % (t, h), align_bytes=64)
             gate = keep.tile([P, HALF], F32, name="gate%d%d" % (t, h), align_bytes=64)
-            acc = next_bank()
+            acc = next_bank("late")
             text_pass(acc, wt_w[:, t, :].bitcast(FP8X4), wt_s[:, t, :], h, True, True)
             nc.scalar.activation(at[:], acc[:], ACT.Tanh, bias=no_bias[:])
-            acc = next_bank()
-            picture_pass(acc, wv_w, WV_ROW, t, h, True, True)
-            nc.scalar.activation(av[:], acc[:], ACT.Tanh, bias=no_bias[:])
-            acc = next_bank()
-            picture_pass(acc, zv_w, ZV_ROW, t, h, True, False)
-            text_pass(acc, zt_w[:, t, :, :].rearrange("p m e -> p (m e)").bitcast(FP4X4), dealt_s[ZT_ROW:, t, :],
+            acc = next_bank("late")
+            picture_pass(acc, zv_w[:, t, :], z_s[ZV_ROW:, t, :], h, True, False)
+            text_pass(acc, zt_w[:, t, :, :].rearrange("p m e -> p (m e)").bitcast(FP4X4), z_s[ZT_ROW:, t, :],
                       h, False, True)
             nc.scalar.activation(gate[:], acc[:], ACT.Sigmoid, bias=bias[:, t : t + 1])
-            return av, at, gate
+            return at, gate
 
         def differ(engine, av, at, gate):
             diff = single.tile([P, HALF], F32, name="diff", tag="diff", align_bytes=64)
@@ -192,7 +208,7 @@ def tile_list_gmu_tanh_scatP_kernel(
             return mixed
 
         def spread_wgo():
-            turned = next_bank()
+            turned = next_bank("early")
             nc.tensor.transpose(turned[:, 0:P], wgo_rows[:], ident[:])
             nc.scalar.copy(wgo_cols[:], turned[:, 0 : J // P])
             banks = [sums.tile([P, HALF], F32, name="wgo%d" % h) for h in range(2)]
@@ -204,14 +220,13 @@ def tile_list_gmu_tanh_scatP_kernel(
         out_rows = out_0.rearrange("(p t) c -> p t c", t=PACK)
 
         def place(t, h, mixed):
-            weighted = ring.tile([P, HALF], F32, name="weighted", tag="weighted", align_bytes=64)
-            for lo in range(0, HALF, SEGMENT):
-                cols = slice(lo, lo + SEGMENT)
-                nc.vector.tensor_tensor(weighted[:, cols], mixed[:, cols], wgo_banks[h][:, cols], ALU.mult)
-            for lo in range(0, HALF, SEGMENT):
-                first = h * HALF + lo
-                nc.vector.tensor_copy(
-                    pages[t][:].indirect(entries(list1, first, first + SEGMENT)), weighted[:, lo : lo + SEGMENT])
+            window = pages[t][:].indirect(entries(list1, h * HALF, (h + 1) * HALF))
+            if (t, h) == units[-1]:
+                nc.vector.tensor_tensor(window, mixed[:], wgo_last[:], ALU.mult)
+            else:
+                weighted = ring.tile([P, HALF], F32, name="weighted", tag="weighted", align_bytes=64)
+                nc.vector.tensor_tensor(weighted[:], mixed[:], wgo_banks[h][:], ALU.mult)
+                nc.vector.tensor_copy(window, weighted[:])
             if h == 1:
                 nc.sync.dma_start(out=out_rows[:, t, :], in_=pages[t][:])
 
@@ -226,23 +241,27 @@ def tile_list_gmu_tanh_scatP_kernel(
                     nc.scalar.copy(woven[c][:, :, t], pages[t][:, cols])
 
         units = [(t, h) for t in range(PACK) for h in range(2)]
-        made = [activate(*units[0])]
         wgo_banks = spread_wgo()
-        made = made + [activate(*unit) for unit in units[1:]]
+        wgo_last = keep.tile([P, HALF], F32, name="wgo_last", align_bytes=64)
+        nc.scalar.copy(wgo_last[:], wgo_banks[1][:])
+        early = [picture(*unit, "early") for unit in units[:EARLY_UNITS]]
+        made = []
+        for i in range(len(units)):
+            made.append((early[i] if i < EARLY_UNITS else picture(*units[i], "late"),) + text_and_gate(*units[i]))
         av, at, gate = made[0]
         first_diff = keep.tile([P, HALF], F32, name="first_diff", align_bytes=64)
         nc.vector.tensor_tensor(first_diff[:], av[:], at[:], ALU.subtract)
         place(*units[0], join(nc.vector, weigh(nc.vector, first_diff, gate), at))
         diff = differ(nc.gpsimd, *made[1])
+        woven = [keep.tile([P, CHUNK, PACK], BF16, name="woven%d" % c, tag=tag, align_bytes=64)
+                 for c, tag in enumerate(["v_w0", "v2_w512", "v_s0", "v2_s0"])]
         for i in range(1, len(units)):
             gated = weigh(nc.gpsimd, diff, made[i][2])
             if i + 1 < len(units):
                 diff = differ(nc.gpsimd, *made[i + 1])
             place(*units[i], join(nc.gpsimd, gated, made[i][1]))
-        woven = [keep.tile([P, CHUNK, PACK], BF16, name="woven%d" % c, tag=tag, align_bytes=64)
-                 for c, tag in enumerate(["zt_raw", "raw_s", "v_s0", "v2_s0"])]
-        for t in range(PACK):
-            weave(t)
+            if units[i][1] == 1:
+                weave(units[i][0])
 
         out_words = words_of(out_1)
         planes = [keep.tile([P, 2 * CHUNK], U8, name="plane%d" % g, align_bytes=64) for g in range(CHUNKS // 2)]
@@ -256,7 +275,7 @@ def tile_list_gmu_tanh_scatP_kernel(
             nc.sync.dma_start(out=out_words[:, c * CHUNK : (c + 1) * CHUNK], in_=codes[:].bitcast(I32))
             if c % 2 == 1:
                 for q in range(4):
-                    nc.scalar.dma_start(
+                    nc.sync.dma_start(
                         out=out_2[0, 4 * q : 4 * q + 4, (c - 1) * CHUNK : (c + 1) * CHUNK].bitcast(I32),
                         in_=plane[32 * q : 32 * q + 4, :].bitcast(I32),
                     )

@@ -27,6 +27,7 @@ CHUNK = 512
 CHUNKS = T // CHUNK
 VECTOR_CHUNKS = 2
 EARLY_UNITS = 4
+QUARTER = 256
 RING_BANKS = 3
 ZT_ROW, ZV_ROW = 0, 4
 
@@ -71,12 +72,12 @@ def tile_list_gmu_tanh_scatP_kernel(
         tab_s = keep.tile([P, T], U8, name="tab_s", align_bytes=64)
         tab2_w = keep.tile([P, T], U32, name="tab2_w", align_bytes=64)
         tab2_s = keep.tile([P, T], U8, name="tab2_s", align_bytes=64)
-        z_raw_s = single.tile([P, N], U8, name="z_raw_s", tag="diff", align_bytes=64)
+        z_raw_s = keep.tile([P, N], U8, name="z_raw_s", tag="z_raw_s", align_bytes=64)
         wv_raw_s = keep.tile([P, N], U8, name="wv_raw_s", align_bytes=64)
         wv_raw = keep.tile([P, N], I32, name="wv_raw", align_bytes=64)
         zv_raw = keep.tile([P, N], I32, name="zv_raw", align_bytes=64)
-        zt_raw = keep.tile([P, 2 * N], U8, name="zt_raw", tag="zt_raw", align_bytes=64)
-        wt_raw = keep.tile([P, PACK, N], F32, name="wt_raw", align_bytes=64)
+        zt_raw = keep.tile([P, 2 * N], U8, name="zt_raw", align_bytes=64)
+        wt_raw = keep.tile([P, PACK, N], F32, name="wt_raw", tag="wt_raw", align_bytes=64)
         bias = keep.tile([P, PACK], F32, name="bias")
         wgo_rows = keep.tile([P, P], F32, name="wgo_rows", align_bytes=64)
         wgo_cols = keep.tile([P, J // P], F32, name="wgo_cols", align_bytes=64)
@@ -87,10 +88,9 @@ def tile_list_gmu_tanh_scatP_kernel(
 
         nc.gpsimd.memset(tab_s[:].bitcast(I32), 0)
         nc.vector.memset(cleared[:], 0.0)
-        nc.gpsimd.memset(tab2_s[:].bitcast(I32), 0)
+        nc.vector.memset(tab2_s[:].bitcast(I32), 0)
         nc.vector.memset(wv_raw_s[:].bitcast(I32), 0)
         nc.vector.memset(z_raw_s[:].bitcast(I32), 0)
-        nc.gpsimd.memset(wgo_rows[:], 0.0)
         nc.scalar.activation(half[:], cleared[:], ACT.Sigmoid)
         nc.scalar.activation(no_bias[:], half[:], ACT.Tanh, scale=0.0)
 
@@ -99,30 +99,26 @@ def tile_list_gmu_tanh_scatP_kernel(
         wv_planes = plane_loads(wv_raw_s, 0, wv_scales)
         z_planes = plane_loads(z_raw_s, ZV_ROW, zv_scales) + plane_loads(z_raw_s, ZT_ROW, zt_scales)
         loads = (
-            [(list1[:], offs), (list2[:], offs2)] + tab_planes
-            + [(tab_w[:].bitcast(I32), words_of(tab_words)),
-               (wgo_rows[0 : J // P, :], wgo[0:1, :].rearrange("o (r j) -> (o r) j", j=P))]
+            [(list1[:], offs), (wgo_rows[:], wgo[0 : P * P // J, :].rearrange("o (r j) -> (o r) j", j=P))]
+            + tab_planes
+            + [(tab_w[:].bitcast(I32), words_of(tab_words)), (wv_raw[:], words_of(wv_words)), (list2[:], offs2)]
             + tab2_planes
-            + [(wt_raw[:], wt.rearrange("(p i) n -> p i n", i=PACK)),
-               (wv_raw[:], words_of(wv_words))]
+            + [(wt_raw[:], wt.rearrange("(p i) n -> p i n", i=PACK))]
             + wv_planes
-            + [(zv_raw[:], words_of(zv_words)), (tab2_w[:].bitcast(I32), words_of(tab2_words))]
-            + z_planes[:-2]
-            + [(zt_raw[:].bitcast(I32), zt_words[0].bitcast(I32)), (bias[:], b.rearrange("(p t) -> p t", t=PACK))]
+            + [(zv_raw[:], words_of(zv_words)), (zt_raw[:].bitcast(I32), zt_words[0].bitcast(I32)),
+               (tab2_w[:].bitcast(I32), words_of(tab2_words))]
+            + z_planes[:-1]
+            + [(bias[:], b.rearrange("(p t) -> p t", t=PACK))]
         )
         for out, in_ in loads:
             nc.sync.dma_start(out, in_)
-        for out, in_ in z_planes[-2:]:
-            nc.gpsimd.dma_start(out, in_)
+        nc.gpsimd.dma_start(*z_planes[-1])
 
-        def clear(page):
-            for c in range(CHUNKS):
-                nc.gpsimd.memset(page[:, c * CHUNK : (c + 1) * CHUNK], 0.0)
-
-        pages = [keep.tile([P, T], F32, name="page%d" % t, align_bytes=64) for t in range(2)]
+        middle_pages = [keep.tile([P, T], F32, name="page%d" % t, align_bytes=64) for t in range(1, PACK - 1)]
         make_identity(nc, ident[:])
-        nc.vector.memset(pages[0][:].bitcast(I32), 0)
-        clear(pages[1])
+        nc.vector.memset(middle_pages[0][:].bitcast(I32), 0)
+        for first in range(0, T, J):
+            nc.gpsimd.memset(middle_pages[1][:, first : first + J], 0.0)
 
         def pick(name, window, dtype, offsets, first, last, tag=None):
             got = keep.tile([P, last - first], dtype, name="%s%d" % (name, first),
@@ -134,16 +130,21 @@ def tile_list_gmu_tanh_scatP_kernel(
         v_w = pick("v_w", tab_w, U32, list1, 0, J)
         v2_s = pick("v2_s", tab2_s, U8, list2, 0, J)
 
-        wt_bf = keep.tile([P, PACK, P, PACK], BF16, name="wt_bf", align_bytes=64)
-        nc.scalar.copy(
-            wt_bf[:].rearrange("p t m i -> p m i t"),
-            wt_raw[:].rearrange("p i (m t) -> p m i t", t=PACK),
-        )
-        wt_w = keep.tile([P, PACK, P], U32, name="wt_w", align_bytes=64)
-        wt_s = keep.tile([P, PACK, P], U8, name="wt_s", align_bytes=64)
-        nc.vector.quantize_mx(
-            out=wt_w[:].rearrange("p t m -> p (t m)").bitcast(FP8X4), scales=wt_s[:].rearrange("p t m -> p (t m)"),
-            in_=wt_bf[:].rearrange("p t m i -> p (t m i)"))
+        def quantise_wt(pair):
+            wt_bf = keep.tile([P, 2, P, PACK], BF16, name="wt_bf%d" % pair, align_bytes=64)
+            nc.scalar.copy(
+                wt_bf[:].rearrange("p t m i -> p m i t"),
+                wt_raw[:].rearrange("p i (m t) -> p m i t", t=PACK)[:, :, :, 2 * pair : 2 * pair + 2],
+            )
+            codes = keep.tile([P, 2, P], U32, name="wt_w%d" % pair, align_bytes=64)
+            scales = keep.tile([P, 2, P], U8, name="wt_s%d" % pair, align_bytes=64)
+            nc.vector.quantize_mx(
+                out=codes[:].rearrange("p t m -> p (t m)").bitcast(FP8X4),
+                scales=scales[:].rearrange("p t m -> p (t m)"),
+                in_=wt_bf[:].rearrange("p t m i -> p (t m i)"))
+            return codes, scales
+
+        wt_q = [quantise_wt(pair) for pair in range(2)]
 
         wv_w = keep.tile([P, PACK, P], I32, name="wv_w", align_bytes=64)
         zv_w = keep.tile([P, PACK, P], I32, name="zv_w", align_bytes=64)
@@ -153,11 +154,13 @@ def tile_list_gmu_tanh_scatP_kernel(
         nc.gpsimd.tensor_copy(wv_w[:], wv_raw[:].rearrange("p (m t) -> p t m", t=PACK))
         nc.gpsimd.tensor_copy(wv_s[:], wv_raw_s[:].rearrange("p (m t) -> p t m", t=PACK))
         nc.gpsimd.tensor_copy(zv_w[:], zv_raw[:].rearrange("p (m t) -> p t m", t=PACK))
-        nc.gpsimd.tensor_copy(z_s[:], z_raw_s[:].rearrange("p (m t) -> p t m", t=PACK))
         nc.gpsimd.tensor_copy(zt_w[:], zt_raw[:].rearrange("p (m t e) -> p t m e", t=PACK, e=2))
-        pages = pages + [keep.tile([P, T], F32, name="page2", tag="zt_raw", align_bytes=64), pages[0]]
-        clear(pages[2])
+        nc.gpsimd.tensor_copy(z_s[:], z_raw_s[:].rearrange("p (m t) -> p t m", t=PACK))
         v2_w = [pick("v2_w", tab2_w, U32, list2, first, first + HALF) for first in (0, HALF)]
+        outer_page = keep.tile([P, T], F32, name="page0", tag="z_raw_s", align_bytes=64)
+        for first in range(0, T, CHUNK):
+            nc.gpsimd.memset(outer_page[:, first : first + CHUNK], 0.0)
+        pages = [outer_page] + middle_pages + [outer_page]
 
         def picture_pass(acc, weight_w, weight_s, h, start, stop):
             cols = slice(h * HALF, (h + 1) * HALF)
@@ -172,40 +175,45 @@ def tile_list_gmu_tanh_scatP_kernel(
                 rhs=v2_w[h][:].bitcast(FP8X4), rhs_scale=v2_s[:, h * HALF : (h + 1) * HALF], start=start, stop=stop,
             )
 
+        av = keep.tile([P, PACK * J], F32, name="av", align_bytes=64)
+        at = keep.tile([P, PACK * J], F32, name="at", align_bytes=64)
+        gate = keep.tile([P, PACK * J], F32, name="gate", align_bytes=64)
+        mixed = keep.tile([P, PACK * J], F32, name="mixed", align_bytes=64)
+        weighted = keep.tile([P, PACK * J], F32, name="weighted", align_bytes=64)
+
+        def span(t, h):
+            return slice(t * J + h * HALF, t * J + (h + 1) * HALF)
+
         def picture(t, h, kind):
-            av = keep.tile([P, HALF], F32, name="av%d%d" % (t, h), align_bytes=64)
             acc = next_bank(kind)
             picture_pass(acc, wv_w[:, t, :], wv_s[:, t, :], h, True, True)
-            nc.scalar.activation(av[:], acc[:], ACT.Tanh, bias=no_bias[:])
-            return av
+            nc.scalar.activation(av[:, span(t, h)], acc[:], ACT.Tanh, bias=no_bias[:])
 
-        def text_and_gate(t, h):
-            at = keep.tile([P, HALF], F32, name="at%d%d" % (t, h), align_bytes=64)
-            gate = keep.tile([P, HALF], F32, name="gate%d%d" % (t, h), align_bytes=64)
-            acc = next_bank("late")
-            text_pass(acc, wt_w[:, t, :].bitcast(FP8X4), wt_s[:, t, :], h, True, True)
-            nc.scalar.activation(at[:], acc[:], ACT.Tanh, bias=no_bias[:])
+        def gate_of(t, h):
             acc = next_bank("late")
             picture_pass(acc, zv_w[:, t, :], z_s[ZV_ROW:, t, :], h, True, False)
             text_pass(acc, zt_w[:, t, :, :].rearrange("p m e -> p (m e)").bitcast(FP4X4), z_s[ZT_ROW:, t, :],
                       h, False, True)
-            nc.scalar.activation(gate[:], acc[:], ACT.Sigmoid, bias=bias[:, t : t + 1])
-            return at, gate
+            nc.scalar.activation(gate[:, span(t, h)], acc[:], ACT.Sigmoid, bias=bias[:, t : t + 1])
 
-        def differ(engine, av, at, gate):
-            diff = single.tile([P, HALF], F32, name="diff", tag="diff", align_bytes=64)
-            engine.tensor_tensor(diff[:], av[:], at[:], ALU.subtract)
+        def text(t, h):
+            acc = next_bank("late")
+            wt_w, wt_s = wt_q[t // 2]
+            text_pass(acc, wt_w[:, t % 2, :].bitcast(FP8X4), wt_s[:, t % 2, :], h, True, True)
+            nc.scalar.activation(at[:, span(t, h)], acc[:], ACT.Tanh, bias=no_bias[:])
+
+        def differ(engine, pool, lo, hi):
+            diff = pool.tile([P, hi - lo], F32, name="diff", tag="diff", align_bytes=64)
+            engine.tensor_tensor(diff[:], av[:, lo:hi], at[:, lo:hi], ALU.subtract)
             return diff
 
-        def weigh(engine, diff, gate):
-            gated = ring.tile([P, HALF], F32, name="gated", tag="gated", align_bytes=64)
-            engine.tensor_tensor(gated[:], diff[:], gate[:], ALU.mult)
+        def weigh(engine, diff, lo, hi):
+            gated = ring.tile([P, hi - lo], F32, name="gated", tag="gated", align_bytes=64)
+            engine.tensor_tensor(gated[:], diff[:], gate[:, lo:hi], ALU.mult)
             return gated
 
-        def join(engine, gated, at):
-            mixed = ring.tile([P, HALF], F32, name="mixed", tag="mixed", align_bytes=64)
-            engine.tensor_tensor(mixed[:], gated[:], at[:], ALU.add)
-            return mixed
+        def join(engine, gated, lo, hi):
+            engine.tensor_tensor(mixed[:, lo:hi], gated[:], at[:, lo:hi], ALU.add)
 
         def spread_wgo():
             turned = next_bank("early")
@@ -219,16 +227,22 @@ def tile_list_gmu_tanh_scatP_kernel(
 
         out_rows = out_0.rearrange("(p t) c -> p t c", t=PACK)
 
-        def place(t, h, mixed):
+        def scale(lo, hi):
+            j = lo % J
+            nc.vector.tensor_tensor(
+                weighted[:, lo:hi], mixed[:, lo:hi], wgo_banks[j // HALF][:, j % HALF : j % HALF + hi - lo], ALU.mult)
+
+        def place(t, h):
             window = pages[t][:].indirect(entries(list1, h * HALF, (h + 1) * HALF))
             if (t, h) == units[-1]:
-                nc.vector.tensor_tensor(window, mixed[:], wgo_last[:], ALU.mult)
+                nc.vector.tensor_tensor(window, mixed[:, span(t, h)], wgo_last[:], ALU.mult)
             else:
-                weighted = ring.tile([P, HALF], F32, name="weighted", tag="weighted", align_bytes=64)
-                nc.vector.tensor_tensor(weighted[:], mixed[:], wgo_banks[h][:], ALU.mult)
-                nc.vector.tensor_copy(window, weighted[:])
+                nc.vector.tensor_copy(window, weighted[:, span(t, h)])
+            if (t, h) == (PACK - 2, 1):
+                nc.scalar.copy(wgo_last[:], wgo_banks[1][:])
             if h == 1:
                 nc.sync.dma_start(out=out_rows[:, t, :], in_=pages[t][:])
+                weave(t)
 
         def weave(t):
             for c in range(CHUNKS):
@@ -242,26 +256,41 @@ def tile_list_gmu_tanh_scatP_kernel(
 
         units = [(t, h) for t in range(PACK) for h in range(2)]
         wgo_banks = spread_wgo()
+        for unit in units[:EARLY_UNITS]:
+            picture(*unit, "early")
+        for i, unit in enumerate(units):
+            gate_of(*unit)
+            if i >= EARLY_UNITS:
+                picture(*unit, "late")
+            text(*unit)
         wgo_last = keep.tile([P, HALF], F32, name="wgo_last", align_bytes=64)
-        nc.scalar.copy(wgo_last[:], wgo_banks[1][:])
-        early = [picture(*unit, "early") for unit in units[:EARLY_UNITS]]
-        made = []
-        for i in range(len(units)):
-            made.append((early[i] if i < EARLY_UNITS else picture(*units[i], "late"),) + text_and_gate(*units[i]))
-        av, at, gate = made[0]
-        first_diff = keep.tile([P, HALF], F32, name="first_diff", align_bytes=64)
-        nc.vector.tensor_tensor(first_diff[:], av[:], at[:], ALU.subtract)
-        place(*units[0], join(nc.vector, weigh(nc.vector, first_diff, gate), at))
-        diff = differ(nc.gpsimd, *made[1])
         woven = [keep.tile([P, CHUNK, PACK], BF16, name="woven%d" % c, tag=tag, align_bytes=64)
                  for c, tag in enumerate(["v_w0", "v2_w512", "v_s0", "v2_s0"])]
-        for i in range(1, len(units)):
-            gated = weigh(nc.gpsimd, diff, made[i][2])
-            if i + 1 < len(units):
-                diff = differ(nc.gpsimd, *made[i + 1])
-            place(*units[i], join(nc.gpsimd, gated, made[i][1]))
-            if units[i][1] == 1:
-                weave(units[i][0])
+
+        quarters = [(0, QUARTER), (QUARTER, HALF)]
+        diffs = [differ(nc.vector, ring, *cols) for cols in quarters]
+        gateds = [weigh(nc.vector, diff, *cols) for diff, cols in zip(diffs, quarters)]
+        for gated, cols in zip(gateds, quarters):
+            join(nc.vector, gated, *cols)
+        for cols in quarters:
+            scale(*cols)
+        place(*units[0])
+
+        edges = list(range(HALF, PACK * J + 1, HALF))
+        pieces = list(zip(edges, edges[1:]))
+        last_unit = span(*units[-1]).start
+        diff = differ(nc.gpsimd, single, *pieces[0])
+        for i, (lo, hi) in enumerate(pieces):
+            gated = weigh(nc.gpsimd, diff, lo, hi)
+            if i == 0:
+                join(nc.gpsimd, gated, lo, hi)
+            if i + 1 < len(pieces):
+                diff = differ(nc.gpsimd, single, *pieces[i + 1])
+            if i > 0:
+                join(nc.gpsimd, gated, lo, hi)
+            if lo < last_unit:
+                scale(lo, hi)
+            place(*units[lo // HALF])
 
         out_words = words_of(out_1)
         planes = [keep.tile([P, 2 * CHUNK], U8, name="plane%d" % g, align_bytes=64) for g in range(CHUNKS // 2)]

@@ -34,9 +34,8 @@ ZT_ROW, ZV_ROW = 0, 4
 
 def plane_loads(plane, first_row, scales):
     return [
-        (plane[32 * q + first_row : 32 * q + first_row + 4, :].bitcast(I32),
-         scales[0, 4 * q : 4 * q + 4, :].bitcast(I32))
-        for q in range(4)
+        (plane[first_row + r : P : 32, :].bitcast(I32), scales[0, r : 16 : 4, :].bitcast(I32))
+        for r in range(4)
     ]
 
 
@@ -303,8 +302,8 @@ def tile_list_gmu_tanh_scatP_kernel(
             )
             nc.sync.dma_start(out=out_words[:, c * CHUNK : (c + 1) * CHUNK], in_=codes[:].bitcast(I32))
             if c % 2 == 1:
-                for q in range(4):
+                for r in range(4):
                     nc.sync.dma_start(
-                        out=out_2[0, 4 * q : 4 * q + 4, (c - 1) * CHUNK : (c + 1) * CHUNK].bitcast(I32),
-                        in_=plane[32 * q : 32 * q + 4, :].bitcast(I32),
+                        out=out_2[0, r : 16 : 4, (c - 1) * CHUNK : (c + 1) * CHUNK].bitcast(I32),
+                        in_=plane[r : P : 32, :].bitcast(I32),
                     )

@@ -24,8 +24,8 @@ PER_COLUMN = 16
 HALF = 512
 BLOCKS = HALF // P
 CHUNK = 512
-CHUNKS = T // CHUNK
-VECTOR_CHUNKS = 2
+CHUNKS = [(0, 512), (512, 1024), (1024, 1536), (1536, 1792), (1792, 2048)]
+VECTOR_COLUMNS = 896
 EARLY_UNITS = 4
 QUARTER = 256
 RING_BANKS = 3
@@ -54,7 +54,7 @@ def tile_list_gmu_tanh_scatP_kernel(
     nc = tc.nc
     with ExitStack() as ctx:
         keep = ctx.enter_context(tc.tile_pool(name="keep", bufs=1))
-        ring = ctx.enter_context(tc.tile_pool(name="ring", bufs=3))
+        ring = ctx.enter_context(tc.tile_pool(name="ring", bufs=4))
         single = ctx.enter_context(tc.tile_pool(name="single", bufs=1))
         sums = ctx.enter_context(tc.psum_pool(name="sums", bufs=1))
 
@@ -69,7 +69,7 @@ def tile_list_gmu_tanh_scatP_kernel(
         list2 = keep.tile([P, J // PER_COLUMN], U16, name="list2")
         tab_w = keep.tile([P, T], U32, name="tab_w", align_bytes=64)
         tab_s = keep.tile([P, T], U8, name="tab_s", align_bytes=64)
-        tab2_w = keep.tile([P, T], U32, name="tab2_w", align_bytes=64)
+        tab2_w = keep.tile([P, T], U32, name="tab2_w", tag="tab2_w", align_bytes=64)
         tab2_s = keep.tile([P, T], U8, name="tab2_s", align_bytes=64)
         z_raw_s = keep.tile([P, N], U8, name="z_raw_s", tag="z_raw_s", align_bytes=64)
         wv_raw_s = keep.tile([P, N], U8, name="wv_raw_s", align_bytes=64)
@@ -129,13 +129,13 @@ def tile_list_gmu_tanh_scatP_kernel(
         v_w = pick("v_w", tab_w, U32, list1, 0, J)
         v2_s = pick("v2_s", tab2_s, U8, list2, 0, J)
 
-        def quantise_wt(pair):
+        def quantise_wt(pair, codes_tag):
             wt_bf = keep.tile([P, 2, P, PACK], BF16, name="wt_bf%d" % pair, align_bytes=64)
             nc.scalar.copy(
                 wt_bf[:].rearrange("p t m i -> p m i t"),
                 wt_raw[:].rearrange("p i (m t) -> p m i t", t=PACK)[:, :, :, 2 * pair : 2 * pair + 2],
             )
-            codes = keep.tile([P, 2, P], U32, name="wt_w%d" % pair, align_bytes=64)
+            codes = keep.tile([P, 2, P], U32, name="wt_w%d" % pair, tag=codes_tag, align_bytes=64)
             scales = keep.tile([P, 2, P], U8, name="wt_s%d" % pair, align_bytes=64)
             nc.vector.quantize_mx(
                 out=codes[:].rearrange("p t m -> p (t m)").bitcast(FP8X4),
@@ -143,7 +143,7 @@ def tile_list_gmu_tanh_scatP_kernel(
                 in_=wt_bf[:].rearrange("p t m i -> p (t m i)"))
             return codes, scales
 
-        wt_q = [quantise_wt(pair) for pair in range(2)]
+        wt_q = [quantise_wt(0, "wt_w0")]
 
         wv_w = keep.tile([P, PACK, P], I32, name="wv_w", align_bytes=64)
         zv_w = keep.tile([P, PACK, P], I32, name="zv_w", align_bytes=64)
@@ -154,25 +154,31 @@ def tile_list_gmu_tanh_scatP_kernel(
         nc.gpsimd.tensor_copy(wv_s[:], wv_raw_s[:].rearrange("p (m t) -> p t m", t=PACK))
         nc.gpsimd.tensor_copy(zv_w[:], zv_raw[:].rearrange("p (m t) -> p t m", t=PACK))
         nc.gpsimd.tensor_copy(zt_w[:], zt_raw[:].rearrange("p (m t e) -> p t m e", t=PACK, e=2))
-        nc.gpsimd.tensor_copy(z_s[:], z_raw_s[:].rearrange("p (m t) -> p t m", t=PACK))
-        v2_w = [pick("v2_w", tab2_w, U32, list2, first, first + HALF) for first in (0, HALF)]
+        for pages_dealt in (slice(0, 1), slice(1, PACK)):
+            nc.gpsimd.tensor_copy(
+                z_s[:, pages_dealt, :], z_raw_s[:].rearrange("p (m t) -> p t m", t=PACK)[:, pages_dealt, :])
+        v2_w = {first: pick("v2_w", tab2_w, U32, list2, first, last)
+                for first, last in ((0, QUARTER), (QUARTER, HALF), (HALF, J))}
+        wt_q.append(quantise_wt(1, "tab2_w"))
         outer_page = keep.tile([P, T], F32, name="page0", tag="z_raw_s", align_bytes=64)
         for first in range(0, T, CHUNK):
             nc.gpsimd.memset(outer_page[:, first : first + CHUNK], 0.0)
         pages = [outer_page] + middle_pages + [outer_page]
 
-        def picture_pass(acc, weight_w, weight_s, h, start, stop):
-            cols = slice(h * HALF, (h + 1) * HALF)
+        def picture_pass(acc, weight_w, weight_s, first, last, start, stop):
             nc.tensor.matmul_mx(
-                out=acc[:], lhsT=weight_w.bitcast(FP8X4), lhsT_scale=weight_s,
-                rhs=v_w[:, cols].bitcast(FP8X4), rhs_scale=v_s[:, cols], start=start, stop=stop,
+                out=acc, lhsT=weight_w.bitcast(FP8X4), lhsT_scale=weight_s,
+                rhs=v_w[:, first:last].bitcast(FP8X4), rhs_scale=v_s[:, first:last], start=start, stop=stop,
             )
 
-        def text_pass(acc, weight, weight_s, h, start, stop):
-            nc.tensor.matmul_mx(
-                out=acc[:], lhsT=weight, lhsT_scale=weight_s,
-                rhs=v2_w[h][:].bitcast(FP8X4), rhs_scale=v2_s[:, h * HALF : (h + 1) * HALF], start=start, stop=stop,
-            )
+        def text_passes(acc, weight, weight_s, first, last, start):
+            gathered = [j for j in sorted(v2_w) if first <= j < last]
+            for j, end in zip(gathered, gathered[1:] + [last]):
+                nc.tensor.matmul_mx(
+                    out=acc[:, j - first : end - first], lhsT=weight, lhsT_scale=weight_s,
+                    rhs=v2_w[j][:].bitcast(FP8X4), rhs_scale=v2_s[:, j:end],
+                    start=start and j == first, stop=end == last,
+                )
 
         av = keep.tile([P, PACK * J], F32, name="av", align_bytes=64)
         at = keep.tile([P, PACK * J], F32, name="at", align_bytes=64)
@@ -183,31 +189,31 @@ def tile_list_gmu_tanh_scatP_kernel(
         def span(t, h):
             return slice(t * J + h * HALF, t * J + (h + 1) * HALF)
 
-        def picture(t, h, kind):
-            acc = next_bank(kind)
-            picture_pass(acc, wv_w[:, t, :], wv_s[:, t, :], h, True, True)
-            nc.scalar.activation(av[:, span(t, h)], acc[:], ACT.Tanh, bias=no_bias[:])
+        def picture(t, first, last, kind):
+            acc = next_bank(kind)[:, : last - first]
+            picture_pass(acc, wv_w[:, t, :], wv_s[:, t, :], first, last, True, True)
+            nc.scalar.activation(av[:, t * J + first : t * J + last], acc, ACT.Tanh, bias=no_bias[:])
 
-        def gate_of(t, h):
-            acc = next_bank("late")
-            picture_pass(acc, zv_w[:, t, :], z_s[ZV_ROW:, t, :], h, True, False)
-            text_pass(acc, zt_w[:, t, :, :].rearrange("p m e -> p (m e)").bitcast(FP4X4), z_s[ZT_ROW:, t, :],
-                      h, False, True)
-            nc.scalar.activation(gate[:, span(t, h)], acc[:], ACT.Sigmoid, bias=bias[:, t : t + 1])
+        def gate_of(t, first, last):
+            acc = next_bank("late")[:, : last - first]
+            picture_pass(acc, zv_w[:, t, :], z_s[ZV_ROW:, t, :], first, last, True, False)
+            text_passes(acc, zt_w[:, t, :, :].rearrange("p m e -> p (m e)").bitcast(FP4X4), z_s[ZT_ROW:, t, :],
+                        first, last, False)
+            nc.scalar.activation(gate[:, t * J + first : t * J + last], acc, ACT.Sigmoid, bias=bias[:, t : t + 1])
 
-        def text(t, h):
-            acc = next_bank("late")
+        def text(t, first, last):
+            acc = next_bank("late")[:, : last - first]
             wt_w, wt_s = wt_q[t // 2]
-            text_pass(acc, wt_w[:, t % 2, :].bitcast(FP8X4), wt_s[:, t % 2, :], h, True, True)
-            nc.scalar.activation(at[:, span(t, h)], acc[:], ACT.Tanh, bias=no_bias[:])
+            text_passes(acc, wt_w[:, t % 2, :].bitcast(FP8X4), wt_s[:, t % 2, :], first, last, True)
+            nc.scalar.activation(at[:, t * J + first : t * J + last], acc, ACT.Tanh, bias=no_bias[:])
 
         def differ(engine, pool, lo, hi):
-            diff = pool.tile([P, hi - lo], F32, name="diff", tag="diff", align_bytes=64)
+            diff = pool.tile([P, hi - lo], F32, name="diff", tag="work", align_bytes=64)
             engine.tensor_tensor(diff[:], av[:, lo:hi], at[:, lo:hi], ALU.subtract)
             return diff
 
-        def weigh(engine, diff, lo, hi):
-            gated = ring.tile([P, hi - lo], F32, name="gated", tag="gated", align_bytes=64)
+        def weigh(engine, pool, diff, lo, hi):
+            gated = pool.tile([P, hi - lo], F32, name="gated", tag="work", align_bytes=64)
             engine.tensor_tensor(gated[:], diff[:], gate[:, lo:hi], ALU.mult)
             return gated
 
@@ -244,66 +250,61 @@ def tile_list_gmu_tanh_scatP_kernel(
                 weave(t)
 
         def weave(t):
-            for c in range(CHUNKS):
-                cols = slice(c * CHUNK, (c + 1) * CHUNK)
-                if t == PACK - 2 and c < VECTOR_CHUNKS:
-                    nc.scalar.copy(woven[c][:, :, t:], pages[t][:, cols].unsqueeze(2).to_broadcast([P, CHUNK, 2]))
-                elif t == PACK - 1 and c < VECTOR_CHUNKS:
-                    nc.vector.tensor_copy(woven[c][:, :, t], pages[t][:, cols])
-                else:
-                    nc.scalar.copy(woven[c][:, :, t], pages[t][:, cols])
+            for (lo, hi), tile in zip(CHUNKS, woven):
+                split = min(max(VECTOR_COLUMNS, lo), hi)
+                if t == PACK - 2 and split > lo:
+                    nc.scalar.copy(tile[:, : split - lo, t:],
+                                   pages[t][:, lo:split].unsqueeze(2).to_broadcast([P, split - lo, 2]))
+                elif t == PACK - 1 and split > lo:
+                    nc.vector.tensor_copy(tile[:, : split - lo, t], pages[t][:, lo:split])
+                first = split if t >= PACK - 2 else lo
+                if first < hi:
+                    nc.scalar.copy(tile[:, first - lo :, t], pages[t][:, first:hi])
 
         units = [(t, h) for t in range(PACK) for h in range(2)]
         wgo_banks = spread_wgo()
-        for unit in units[:EARLY_UNITS]:
-            picture(*unit, "early")
-        for i, unit in enumerate(units):
-            gate_of(*unit)
-            if i >= EARLY_UNITS:
-                picture(*unit, "late")
-            text(*unit)
-        wgo_last = keep.tile([P, HALF], F32, name="wgo_last", align_bytes=64)
-        woven = [keep.tile([P, CHUNK, PACK], BF16, name="woven%d" % c, tag=tag, align_bytes=64)
-                 for c, tag in enumerate(["v_w0", "v2_w512", "v_s0", "v2_s0"])]
-
         quarters = [(0, QUARTER), (QUARTER, HALF)]
+        for t, h in units[:EARLY_UNITS]:
+            picture(t, h * HALF, (h + 1) * HALF, "early")
+        for cols in quarters:
+            gate_of(0, *cols)
+            text(0, *cols)
+        for i, (t, h) in enumerate(units):
+            if i >= 1:
+                gate_of(t, h * HALF, (h + 1) * HALF)
+                if i >= EARLY_UNITS:
+                    picture(t, h * HALF, (h + 1) * HALF, "late")
+                text(t, h * HALF, (h + 1) * HALF)
+        wgo_last = keep.tile([P, HALF], F32, name="wgo_last", align_bytes=64)
+        woven = [keep.tile([P, hi - lo, PACK], BF16, name="woven%d" % lo, tag=tag, align_bytes=64)
+                 for (lo, hi), tag in zip(CHUNKS, ["v_w0", "v2_w512", "v_s0", "v2_s0", "tab2_w"])]
+
         diffs = [differ(nc.vector, ring, *cols) for cols in quarters]
-        gateds = [weigh(nc.vector, diff, *cols) for diff, cols in zip(diffs, quarters)]
+        gateds = [weigh(nc.vector, pool, diff, *cols) for pool, diff, cols in zip((ring, single), diffs, quarters)]
         for gated, cols in zip(gateds, quarters):
             join(nc.vector, gated, *cols)
         for cols in quarters:
             scale(*cols)
         place(*units[0])
 
-        edges = list(range(HALF, PACK * J + 1, HALF))
-        pieces = list(zip(edges, edges[1:]))
-        last_unit = span(*units[-1]).start
-        diff = differ(nc.gpsimd, single, *pieces[0])
-        for i, (lo, hi) in enumerate(pieces):
-            gated = weigh(nc.gpsimd, diff, lo, hi)
-            if i == 0:
-                join(nc.gpsimd, gated, lo, hi)
-            if i + 1 < len(pieces):
-                diff = differ(nc.gpsimd, single, *pieces[i + 1])
-            if i > 0:
-                join(nc.gpsimd, gated, lo, hi)
-            if lo < last_unit:
+        for unit in units[1:]:
+            lo, hi = span(*unit).start, span(*unit).stop
+            join(nc.gpsimd, weigh(nc.gpsimd, ring, differ(nc.gpsimd, single, lo, hi), lo, hi), lo, hi)
+            if unit != units[-1]:
                 scale(lo, hi)
-            place(*units[lo // HALF])
+            place(*unit)
 
         out_words = words_of(out_1)
-        planes = [keep.tile([P, 2 * CHUNK], U8, name="plane%d" % g, align_bytes=64) for g in range(CHUNKS // 2)]
-        for c in range(CHUNKS):
-            codes = keep.tile([P, CHUNK], U32, name="codes%d" % c, align_bytes=64)
-            plane = planes[c // 2]
+        planes = [keep.tile([P, J], U8, name="plane%d" % g, align_bytes=64) for g in range(T // J)]
+        for (lo, hi), tile in zip(CHUNKS, woven):
+            codes = keep.tile([P, hi - lo], U32, name="codes%d" % lo, align_bytes=64)
+            plane = planes[lo // J]
             nc.vector.quantize_mx(
-                out=codes[:].bitcast(FP8X4), scales=plane[:, (c % 2) * CHUNK : (c % 2 + 1) * CHUNK],
-                in_=woven[c][:].rearrange("p c i -> p (c i)"),
+                out=codes[:].bitcast(FP8X4), scales=plane[:, lo % J : lo % J + hi - lo],
+                in_=tile[:].rearrange("p c i -> p (c i)"),
             )
-            nc.sync.dma_start(out=out_words[:, c * CHUNK : (c + 1) * CHUNK], in_=codes[:].bitcast(I32))
-            if c % 2 == 1:
+            nc.sync.dma_start(out=out_words[:, lo:hi], in_=codes[:].bitcast(I32))
+            if hi % J == 0:
                 for r in range(4):
                     nc.sync.dma_start(
-                        out=out_2[0, r : 16 : 4, (c - 1) * CHUNK : (c + 1) * CHUNK].bitcast(I32),
-                        in_=plane[r : P : 32, :].bitcast(I32),
-                    )
+                        out=out_2[0, r : 16 : 4, hi - J : hi].bitcast(I32), in_=plane[r : P : 32, :].bitcast(I32))

@@ -26,7 +26,6 @@ BLOCKS = HALF // P
 CHUNK = 512
 CHUNKS = [(0, 512), (512, 1024), (1024, 1536), (1536, 1792), (1792, 2048)]
 VECTOR_COLUMNS = 896
-EARLY_UNITS = 4
 QUARTER = 256
 RING_BANKS = 3
 ZT_ROW, ZV_ROW = 0, 4
@@ -80,6 +79,7 @@ def tile_list_gmu_tanh_scatP_kernel(
         bias = keep.tile([P, PACK], F32, name="bias")
         wgo_rows = keep.tile([P, P], F32, name="wgo_rows", align_bytes=64)
         wgo_cols = keep.tile([P, J // P], F32, name="wgo_cols", align_bytes=64)
+        wgo_sb = keep.tile([P, J], F32, name="wgo_sb", align_bytes=64)
         ident = keep.tile([P, P], F32, name="ident", align_bytes=64)
         cleared = keep.tile([P, 1], F32, name="cleared")
         half = keep.tile([P, 1], F32, name="half")
@@ -207,6 +207,41 @@ def tile_list_gmu_tanh_scatP_kernel(
             text_passes(acc, wt_w[:, t % 2, :].bitcast(FP8X4), wt_s[:, t % 2, :], first, last, True)
             nc.scalar.activation(at[:, t * J + first : t * J + last], acc, ACT.Tanh, bias=no_bias[:])
 
+        def branch_turned(result, t, words, scales, weight_w, weight_s, sign, kind):
+            acc = next_bank(kind)
+            for j in range(0, HALF, P):
+                nc.tensor.matmul_mx(
+                    out=acc[:, j : j + P], lhsT=words(j), lhsT_scale=scales[:, j : j + P],
+                    rhs=weight_w.bitcast(FP8X4), rhs_scale=weight_s, start=True, stop=True,
+                )
+            nc.scalar.activation(result[:, span(t, 0)], acc[:], ACT.Tanh, bias=no_bias[:], scale=sign)
+
+        def picture_turned(t, kind):
+            branch_turned(av, t, lambda j: v_w[:, j : j + P].bitcast(FP8X4), v_s, wv_w[:, t, :], wv_s[:, t, :],
+                          1.0, kind)
+
+        def text_turned(t):
+            wt_w, wt_s = wt_q[t // 2]
+            branch_turned(
+                at, t, lambda j: v2_w[j // QUARTER * QUARTER][:, j % QUARTER : j % QUARTER + P].bitcast(FP8X4),
+                v2_s, wt_w[:, t % 2, :], wt_s[:, t % 2, :], -1.0, "late")
+
+        def turn(t):
+            lo = t * J
+            minus = next_bank("early")
+            for c in range(0, HALF, P):
+                nc.tensor.transpose(minus[:, c : c + P], at[:, lo + c : lo + c + P], ident[:])
+            base = keep.tile([P, HALF], F32, name="base%d" % t, align_bytes=64)
+            nc.scalar.copy(base[:], minus[:])
+            diff = next_bank("early")
+            for c in range(0, HALF, P):
+                nc.tensor.matmul(diff[:, c : c + P], av[:, lo + c : lo + c + P], ident[:],
+                                 start=c == 0, stop=False, is_transpose=True)
+            for c in range(0, HALF, P):
+                nc.tensor.matmul(diff[:, c : c + P], at[:, lo + c : lo + c + P], ident[:],
+                                 start=False, stop=c + P == HALF, is_transpose=True)
+            return diff, base
+
         def differ(engine, pool, lo, hi):
             diff = pool.tile([P, hi - lo], F32, name="diff", tag="work", align_bytes=64)
             engine.tensor_tensor(diff[:], av[:, lo:hi], at[:, lo:hi], ALU.subtract)
@@ -228,6 +263,8 @@ def tile_list_gmu_tanh_scatP_kernel(
             for r in range(J // P):
                 nc.tensor.transpose(banks[r // BLOCKS][:, r % BLOCKS * P : (r % BLOCKS + 1) * P],
                                     wgo_cols[:, r : r + 1].to_broadcast([P, P]), ident[:])
+            for h in range(2):
+                nc.scalar.copy(wgo_sb[:, h * HALF : (h + 1) * HALF], banks[h][:])
             return banks
 
         out_rows = out_0.rearrange("(p t) c -> p t c", t=PACK)
@@ -240,11 +277,9 @@ def tile_list_gmu_tanh_scatP_kernel(
         def place(t, h):
             window = pages[t][:].indirect(entries(list1, h * HALF, (h + 1) * HALF))
             if (t, h) == units[-1]:
-                nc.vector.tensor_tensor(window, mixed[:, span(t, h)], wgo_last[:], ALU.mult)
+                nc.vector.tensor_tensor(window, mixed[:, span(t, h)], wgo_sb[:, HALF:], ALU.mult)
             else:
                 nc.vector.tensor_copy(window, weighted[:, span(t, h)])
-            if (t, h) == (PACK - 2, 1):
-                nc.scalar.copy(wgo_last[:], wgo_banks[1][:])
             if h == 1:
                 nc.sync.dma_start(out=out_rows[:, t, :], in_=pages[t][:])
                 weave(t)
@@ -264,18 +299,26 @@ def tile_list_gmu_tanh_scatP_kernel(
         units = [(t, h) for t in range(PACK) for h in range(2)]
         wgo_banks = spread_wgo()
         quarters = [(0, QUARTER), (QUARTER, HALF)]
-        for t, h in units[:EARLY_UNITS]:
-            picture(t, h * HALF, (h + 1) * HALF, "early")
+        picture(0, 0, HALF, "early")
+        picture(0, HALF, J, "early")
+        picture_turned(1, "early")
+        picture(1, HALF, J, "early")
         for cols in quarters:
             gate_of(0, *cols)
             text(0, *cols)
-        for i, (t, h) in enumerate(units):
-            if i >= 1:
-                gate_of(t, h * HALF, (h + 1) * HALF)
-                if i >= EARLY_UNITS:
-                    picture(t, h * HALF, (h + 1) * HALF, "late")
-                text(t, h * HALF, (h + 1) * HALF)
-        wgo_last = keep.tile([P, HALF], F32, name="wgo_last", align_bytes=64)
+        gate_of(0, HALF, J)
+        text(0, HALF, J)
+        turned = {}
+        for t in range(1, PACK):
+            gate_of(t, 0, HALF)
+            if t > 1:
+                picture_turned(t, "late")
+            text_turned(t)
+            turned[t] = turn(t)
+            gate_of(t, HALF, J)
+            if t > 1:
+                picture(t, HALF, J, "late")
+            text(t, HALF, J)
         woven = [keep.tile([P, hi - lo, PACK], BF16, name="woven%d" % lo, tag=tag, align_bytes=64)
                  for (lo, hi), tag in zip(CHUNKS, ["v_w0", "v2_w512", "v_s0", "v2_s0", "tab2_w"])]
 
@@ -287,12 +330,22 @@ def tile_list_gmu_tanh_scatP_kernel(
             scale(*cols)
         place(*units[0])
 
-        for unit in units[1:]:
-            lo, hi = span(*unit).start, span(*unit).stop
-            join(nc.gpsimd, weigh(nc.gpsimd, ring, differ(nc.gpsimd, single, lo, hi), lo, hi), lo, hi)
-            if unit != units[-1]:
-                scale(lo, hi)
-            place(*unit)
+        diff = differ(nc.gpsimd, single, HALF, J)
+        gated = weigh(nc.gpsimd, ring, diff, HALF, J)
+        join(nc.gpsimd, gated, HALF, J)
+        for t in range(1, PACK):
+            earlier, now, later = span(t - 1, 1), span(t, 0), span(t, 1)
+            turned_diff, base = turned[t]
+            scale(earlier.start, earlier.stop)
+            nc.vector.tensor_tensor(at[:, earlier], gate[:, now], turned_diff[:], ALU.mult)
+            place(t - 1, 1)
+            diff = differ(nc.gpsimd, single, later.start, later.stop)
+            nc.gpsimd.tensor_tensor(mixed[:, now], at[:, earlier], base[:], ALU.subtract)
+            nc.gpsimd.tensor_tensor(weighted[:, now], mixed[:, now], wgo_sb[:, :HALF], ALU.mult)
+            place(t, 0)
+            nc.gpsimd.tensor_tensor(mixed[:, now], diff[:], gate[:, later], ALU.mult)
+            nc.gpsimd.tensor_tensor(mixed[:, later], mixed[:, now], at[:, later], ALU.add)
+        place(PACK - 1, 1)
 
         out_words = words_of(out_1)
         planes = [keep.tile([P, J], U8, name="plane%d" % g, align_bytes=64) for g in range(T // J)]

@@ -25,7 +25,7 @@ HALF = 512
 BLOCKS = HALF // P
 CHUNK = 512
 CHUNKS = [(0, 512), (512, 1024), (1024, 1536), (1536, 1792), (1792, 2048)]
-VECTOR_COLUMNS = 896
+VECTOR_COLUMNS = 768
 QUARTER = 256
 RING_BANKS = 3
 ZT_ROW, ZV_ROW = 0, 4
@@ -57,10 +57,10 @@ def tile_list_gmu_tanh_scatP_kernel(
         single = ctx.enter_context(tc.tile_pool(name="single", bufs=1))
         sums = ctx.enter_context(tc.psum_pool(name="sums", bufs=1))
 
-        taken = {"early": [], "late": []}
+        taken = {"early": [-1], "late": [-1]}
 
-        def next_bank(kind):
-            taken[kind].append(len(taken[kind]) % RING_BANKS)
+        def next_bank(kind, again=False):
+            taken[kind].append(taken[kind][-1] if again else (taken[kind][-1] + 1) % RING_BANKS)
             return sums.tile([P, HALF], F32, name="%s%d" % (kind, len(taken[kind])),
                              tag="%s%d" % (kind, taken[kind][-1]))
 
@@ -68,7 +68,7 @@ def tile_list_gmu_tanh_scatP_kernel(
         list2 = keep.tile([P, J // PER_COLUMN], U16, name="list2")
         tab_w = keep.tile([P, T], U32, name="tab_w", align_bytes=64)
         tab_s = keep.tile([P, T], U8, name="tab_s", align_bytes=64)
-        tab2_w = keep.tile([P, T], U32, name="tab2_w", tag="tab2_w", align_bytes=64)
+        tab2_w = keep.tile([P, T], U32, name="tab2_w", align_bytes=64)
         tab2_s = keep.tile([P, T], U8, name="tab2_s", align_bytes=64)
         z_raw_s = keep.tile([P, N], U8, name="z_raw_s", tag="z_raw_s", align_bytes=64)
         wv_raw_s = keep.tile([P, N], U8, name="wv_raw_s", align_bytes=64)
@@ -129,21 +129,14 @@ def tile_list_gmu_tanh_scatP_kernel(
         v_w = pick("v_w", tab_w, U32, list1, 0, J)
         v2_s = pick("v2_s", tab2_s, U8, list2, 0, J)
 
-        def quantise_wt(pair, codes_tag):
-            wt_bf = keep.tile([P, 2, P, PACK], BF16, name="wt_bf%d" % pair, align_bytes=64)
-            nc.scalar.copy(
-                wt_bf[:].rearrange("p t m i -> p m i t"),
-                wt_raw[:].rearrange("p i (m t) -> p m i t", t=PACK)[:, :, :, 2 * pair : 2 * pair + 2],
-            )
-            codes = keep.tile([P, 2, P], U32, name="wt_w%d" % pair, tag=codes_tag, align_bytes=64)
-            scales = keep.tile([P, 2, P], U8, name="wt_s%d" % pair, align_bytes=64)
-            nc.vector.quantize_mx(
-                out=codes[:].rearrange("p t m -> p (t m)").bitcast(FP8X4),
-                scales=scales[:].rearrange("p t m -> p (t m)"),
-                in_=wt_bf[:].rearrange("p t m i -> p (t m i)"))
-            return codes, scales
-
-        wt_q = [quantise_wt(0, "wt_w0")]
+        wt_bf = keep.tile([P, PACK, P, PACK], BF16, name="wt_bf", align_bytes=64)
+        nc.scalar.copy(
+            wt_bf[:].rearrange("p t m i -> p m i t"), wt_raw[:].rearrange("p i (m t) -> p m i t", t=PACK))
+        wt_w = keep.tile([P, PACK, P], U32, name="wt_w", tag="wt_w", align_bytes=64)
+        wt_s = keep.tile([P, PACK, P], U8, name="wt_s", align_bytes=64)
+        nc.vector.quantize_mx(
+            out=wt_w[:].rearrange("p t m -> p (t m)").bitcast(FP8X4), scales=wt_s[:].rearrange("p t m -> p (t m)"),
+            in_=wt_bf[:].rearrange("p t m i -> p (t m i)"))
 
         wv_w = keep.tile([P, PACK, P], I32, name="wv_w", align_bytes=64)
         zv_w = keep.tile([P, PACK, P], I32, name="zv_w", align_bytes=64)
@@ -159,7 +152,6 @@ def tile_list_gmu_tanh_scatP_kernel(
                 z_s[:, pages_dealt, :], z_raw_s[:].rearrange("p (m t) -> p t m", t=PACK)[:, pages_dealt, :])
         v2_w = {first: pick("v2_w", tab2_w, U32, list2, first, last)
                 for first, last in ((0, QUARTER), (QUARTER, HALF), (HALF, J))}
-        wt_q.append(quantise_wt(1, "tab2_w"))
         outer_page = keep.tile([P, T], F32, name="page0", tag="z_raw_s", align_bytes=64)
         for first in range(0, T, CHUNK):
             nc.gpsimd.memset(outer_page[:, first : first + CHUNK], 0.0)
@@ -201,10 +193,9 @@ def tile_list_gmu_tanh_scatP_kernel(
                         first, last, False)
             nc.scalar.activation(gate[:, t * J + first : t * J + last], acc, ACT.Sigmoid, bias=bias[:, t : t + 1])
 
-        def text(t, first, last):
-            acc = next_bank("late")[:, : last - first]
-            wt_w, wt_s = wt_q[t // 2]
-            text_passes(acc, wt_w[:, t % 2, :].bitcast(FP8X4), wt_s[:, t % 2, :], first, last, True)
+        def text(t, first, last, again=False):
+            acc = next_bank("late", again)[:, : last - first]
+            text_passes(acc, wt_w[:, t, :].bitcast(FP8X4), wt_s[:, t, :], first, last, True)
             nc.scalar.activation(at[:, t * J + first : t * J + last], acc, ACT.Tanh, bias=no_bias[:])
 
         def branch_turned(result, t, words, scales, weight_w, weight_s, sign, kind):
@@ -221,25 +212,24 @@ def tile_list_gmu_tanh_scatP_kernel(
                           1.0, kind)
 
         def text_turned(t):
-            wt_w, wt_s = wt_q[t // 2]
             branch_turned(
                 at, t, lambda j: v2_w[j // QUARTER * QUARTER][:, j % QUARTER : j % QUARTER + P].bitcast(FP8X4),
-                v2_s, wt_w[:, t % 2, :], wt_s[:, t % 2, :], -1.0, "late")
+                v2_s, wt_w[:, t, :], wt_s[:, t, :], -1.0, "late")
 
         def turn(t):
             lo = t * J
-            minus = next_bank("early")
-            for c in range(0, HALF, P):
-                nc.tensor.transpose(minus[:, c : c + P], at[:, lo + c : lo + c + P], ident[:])
-            base = keep.tile([P, HALF], F32, name="base%d" % t, align_bytes=64)
-            nc.scalar.copy(base[:], minus[:])
-            diff = next_bank("early")
+            diff = sums.tile([P, HALF], F32, name="diff_bank%d" % t, tag="early%d" % (1 + t % 2))
             for c in range(0, HALF, P):
                 nc.tensor.matmul(diff[:, c : c + P], av[:, lo + c : lo + c + P], ident[:],
                                  start=c == 0, stop=False, is_transpose=True)
             for c in range(0, HALF, P):
                 nc.tensor.matmul(diff[:, c : c + P], at[:, lo + c : lo + c + P], ident[:],
                                  start=False, stop=c + P == HALF, is_transpose=True)
+            minus = sums.tile([P, HALF], F32, name="minus_bank%d" % t, tag="early0")
+            for c in range(0, HALF, P):
+                nc.tensor.transpose(minus[:, c : c + P], at[:, lo + c : lo + c + P], ident[:])
+            base = keep.tile([P, HALF], F32, name="base%d" % t, align_bytes=64)
+            nc.scalar.copy(base[:], minus[:])
             return diff, base
 
         def differ(engine, pool, lo, hi):
@@ -303,24 +293,25 @@ def tile_list_gmu_tanh_scatP_kernel(
         picture(0, HALF, J, "early")
         picture_turned(1, "early")
         picture(1, HALF, J, "early")
-        for cols in quarters:
-            gate_of(0, *cols)
-            text(0, *cols)
-        gate_of(0, HALF, J)
+        gate_of(0, *quarters[0])
+        text(0, *quarters[0])
+        text(0, *quarters[1], again=True)
+        gate_of(0, *quarters[1])
         text(0, HALF, J)
+        gate_of(0, HALF, J)
         turned = {}
         for t in range(1, PACK):
-            gate_of(t, 0, HALF)
             if t > 1:
                 picture_turned(t, "late")
             text_turned(t)
             turned[t] = turn(t)
+            gate_of(t, 0, HALF)
             gate_of(t, HALF, J)
             if t > 1:
                 picture(t, HALF, J, "late")
             text(t, HALF, J)
         woven = [keep.tile([P, hi - lo, PACK], BF16, name="woven%d" % lo, tag=tag, align_bytes=64)
-                 for (lo, hi), tag in zip(CHUNKS, ["v_w0", "v2_w512", "v_s0", "v2_s0", "tab2_w"])]
+                 for (lo, hi), tag in zip(CHUNKS, ["v_w0", "v2_w512", "v_s0", "v2_s0", "wt_w"])]
 
         diffs = [differ(nc.vector, ring, *cols) for cols in quarters]
         gateds = [weigh(nc.vector, pool, diff, *cols) for pool, diff, cols in zip((ring, single), diffs, quarters)]
@@ -340,24 +331,25 @@ def tile_list_gmu_tanh_scatP_kernel(
             nc.vector.tensor_tensor(at[:, earlier], gate[:, now], turned_diff[:], ALU.mult)
             place(t - 1, 1)
             diff = differ(nc.gpsimd, single, later.start, later.stop)
-            nc.gpsimd.tensor_tensor(mixed[:, now], at[:, earlier], base[:], ALU.subtract)
-            nc.gpsimd.tensor_tensor(weighted[:, now], mixed[:, now], wgo_sb[:, :HALF], ALU.mult)
+            nc.gpsimd.tensor_tensor(av[:, later], at[:, earlier], base[:], ALU.subtract)
+            nc.gpsimd.tensor_tensor(weighted[:, now], av[:, later], wgo_sb[:, :HALF], ALU.mult)
             place(t, 0)
-            nc.gpsimd.tensor_tensor(mixed[:, now], diff[:], gate[:, later], ALU.mult)
-            nc.gpsimd.tensor_tensor(mixed[:, later], mixed[:, now], at[:, later], ALU.add)
+            nc.gpsimd.tensor_tensor(av[:, later], diff[:], gate[:, later], ALU.mult)
+            nc.gpsimd.tensor_tensor(mixed[:, later], av[:, later], at[:, later], ALU.add)
         place(PACK - 1, 1)
 
         out_words = words_of(out_1)
-        planes = [keep.tile([P, J], U8, name="plane%d" % g, align_bytes=64) for g in range(T // J)]
+        codes = keep.tile([P, T], U32, name="codes", align_bytes=64)
+        plane = keep.tile([P, T], U8, name="plane", align_bytes=64)
+        stored = 0
         for (lo, hi), tile in zip(CHUNKS, woven):
-            codes = keep.tile([P, hi - lo], U32, name="codes%d" % lo, align_bytes=64)
-            plane = planes[lo // J]
             nc.vector.quantize_mx(
-                out=codes[:].bitcast(FP8X4), scales=plane[:, lo % J : lo % J + hi - lo],
+                out=codes[:, lo:hi].bitcast(FP8X4), scales=plane[:, lo:hi],
                 in_=tile[:].rearrange("p c i -> p (c i)"),
             )
-            nc.sync.dma_start(out=out_words[:, lo:hi], in_=codes[:].bitcast(I32))
-            if hi % J == 0:
-                for r in range(4):
-                    nc.sync.dma_start(
-                        out=out_2[0, r : 16 : 4, hi - J : hi].bitcast(I32), in_=plane[r : P : 32, :].bitcast(I32))
+            if hi >= J:
+                nc.sync.dma_start(out=out_words[:, stored:hi], in_=codes[:, stored:hi].bitcast(I32))
+                stored = hi
+        for r in range(4):
+            queue = nc.scalar if r % 2 else nc.sync
+            queue.dma_start(out=out_2[0, r : 16 : 4, :].bitcast(I32), in_=plane[r : P : 32, :].bitcast(I32))

@@ -22,13 +22,11 @@ P = 128
 PACK = 4
 PER_COLUMN = 16
 HALF = 512
-BLOCKS = HALF // P
-CHUNK = 512
+QUARTER = 256
 CHUNKS = [(0, 512), (512, 1024), (1024, 1536), (1536, 1792), (1792, 2048)]
 VECTOR_COLUMNS = 768
-QUARTER = 256
 RING_BANKS = 3
-ZT_ROW, ZV_ROW = 0, 4
+TAB_ROW, WV_ROW, ZT_ROW, ZV_ROW = 4, 4, 0, 8
 
 
 def plane_loads(plane, first_row, scales):
@@ -53,14 +51,13 @@ def tile_list_gmu_tanh_scatP_kernel(
     nc = tc.nc
     with ExitStack() as ctx:
         keep = ctx.enter_context(tc.tile_pool(name="keep", bufs=1))
-        ring = ctx.enter_context(tc.tile_pool(name="ring", bufs=4))
-        single = ctx.enter_context(tc.tile_pool(name="single", bufs=1))
+        reused = ctx.enter_context(tc.tile_pool(name="reused", bufs=1))
         sums = ctx.enter_context(tc.psum_pool(name="sums", bufs=1))
 
         taken = {"early": [-1], "late": [-1]}
 
-        def next_bank(kind, again=False):
-            taken[kind].append(taken[kind][-1] if again else (taken[kind][-1] + 1) % RING_BANKS)
+        def next_bank(kind, step=1):
+            taken[kind].append((taken[kind][-1] + step) % RING_BANKS)
             return sums.tile([P, HALF], F32, name="%s%d" % (kind, len(taken[kind])),
                              tag="%s%d" % (kind, taken[kind][-1]))
 
@@ -70,54 +67,54 @@ def tile_list_gmu_tanh_scatP_kernel(
         tab_s = keep.tile([P, T], U8, name="tab_s", align_bytes=64)
         tab2_w = keep.tile([P, T], U32, name="tab2_w", align_bytes=64)
         tab2_s = keep.tile([P, T], U8, name="tab2_s", align_bytes=64)
-        z_raw_s = keep.tile([P, N], U8, name="z_raw_s", tag="z_raw_s", align_bytes=64)
+        z_raw_s = keep.tile([P, N], U8, name="z_raw_s", align_bytes=64)
         wv_raw_s = keep.tile([P, N], U8, name="wv_raw_s", align_bytes=64)
-        wv_raw = keep.tile([P, N], I32, name="wv_raw", align_bytes=64)
-        zv_raw = keep.tile([P, N], I32, name="zv_raw", align_bytes=64)
-        zt_raw = keep.tile([P, 2 * N], U8, name="zt_raw", align_bytes=64)
-        wt_raw = keep.tile([P, PACK, N], F32, name="wt_raw", tag="wt_raw", align_bytes=64)
+        wv_raw = keep.tile([P, N], U32, name="wv_raw", align_bytes=64)
+        zv_raw = keep.tile([P, N], U32, name="zv_raw", align_bytes=64)
+        zt_raw = keep.tile([P, N], U16, name="zt_raw", align_bytes=64)
+        wt_raw = keep.tile([P, PACK, N], F32, name="wt_raw", align_bytes=64)
         bias = keep.tile([P, PACK], F32, name="bias")
-        wgo_rows = keep.tile([P, P], F32, name="wgo_rows", align_bytes=64)
-        wgo_cols = keep.tile([P, J // P], F32, name="wgo_cols", align_bytes=64)
+        wgo_cols = keep.tile([P, 2, PACK], F32, name="wgo_cols", align_bytes=64)
         wgo_sb = keep.tile([P, J], F32, name="wgo_sb", align_bytes=64)
         ident = keep.tile([P, P], F32, name="ident", align_bytes=64)
         cleared = keep.tile([P, 1], F32, name="cleared")
         half = keep.tile([P, 1], F32, name="half")
         no_bias = keep.tile([P, 1], F32, name="no_bias")
+        windows = [keep.tile([P, T], F32, name="page%d" % t, align_bytes=64) for t in range(PACK - 1)]
+        pages = windows + windows[:1]
 
         nc.gpsimd.memset(tab_s[:].bitcast(I32), 0)
         nc.vector.memset(cleared[:], 0.0)
-        nc.vector.memset(tab2_s[:].bitcast(I32), 0)
-        nc.vector.memset(wv_raw_s[:].bitcast(I32), 0)
         nc.vector.memset(z_raw_s[:].bitcast(I32), 0)
+        nc.vector.memset(wv_raw_s[:].bitcast(I32), 0)
+        nc.vector.memset(tab2_s[:].bitcast(I32), 0)
         nc.scalar.activation(half[:], cleared[:], ACT.Sigmoid)
         nc.scalar.activation(no_bias[:], half[:], ACT.Tanh, scale=0.0)
 
-        tab_planes = plane_loads(tab_s, 0, tab_scales)
-        tab2_planes = plane_loads(tab2_s, 0, tab2_scales)
-        wv_planes = plane_loads(wv_raw_s, 0, wv_scales)
         z_planes = plane_loads(z_raw_s, ZV_ROW, zv_scales) + plane_loads(z_raw_s, ZT_ROW, zt_scales)
+        wv_planes = plane_loads(wv_raw_s, WV_ROW, wv_scales)
         loads = (
-            [(list1[:], offs), (wgo_rows[:], wgo[0 : P * P // J, :].rearrange("o (r j) -> (o r) j", j=P))]
-            + tab_planes
-            + [(tab_w[:].bitcast(I32), words_of(tab_words)), (wv_raw[:], words_of(wv_words)), (list2[:], offs2)]
-            + tab2_planes
-            + [(wt_raw[:], wt.rearrange("(p i) n -> p i n", i=PACK))]
+            [(list1[:], offs), (wgo_cols[:], wgo[0:1, :].rearrange("o (h p r) -> p (o h) r", h=2, r=PACK))]
+            + plane_loads(tab_s, TAB_ROW, tab_scales)
+            + [(tab_w[:].bitcast(I32), words_of(tab_words)), (list2[:], offs2)]
             + wv_planes
-            + [(zv_raw[:], words_of(zv_words)), (zt_raw[:].bitcast(I32), zt_words[0].bitcast(I32)),
-               (tab2_w[:].bitcast(I32), words_of(tab2_words))]
-            + z_planes[:-1]
-            + [(bias[:], b.rearrange("(p t) -> p t", t=PACK))]
+            + [(wv_raw[:].bitcast(I32), words_of(wv_words)), (wt_raw[:], wt.rearrange("(p i) n -> p i n", i=PACK))]
+            + plane_loads(tab2_s, 0, tab2_scales)
+            + z_planes[:1]
+            + [(zt_raw[:].bitcast(I32), zt_words[0].bitcast(I32)), (tab2_w[:].bitcast(I32), words_of(tab2_words)),
+               (zv_raw[:].bitcast(I32), words_of(zv_words))]
+            + z_planes[1:-1]
+            + [(wgo_sb[:], wgo)]
         )
         for out, in_ in loads:
             nc.sync.dma_start(out, in_)
-        nc.gpsimd.dma_start(*z_planes[-1])
 
-        middle_pages = [keep.tile([P, T], F32, name="page%d" % t, align_bytes=64) for t in range(1, PACK - 1)]
         make_identity(nc, ident[:])
-        nc.vector.memset(middle_pages[0][:].bitcast(I32), 0)
-        for first in range(0, T, J):
-            nc.gpsimd.memset(middle_pages[1][:, first : first + J], 0.0)
+        nc.gpsimd.dma_start(bias[:], b.rearrange("(p t) -> p t", t=PACK))
+        nc.gpsimd.dma_start(*z_planes[-1])
+        nc.vector.memset(windows[0][:].bitcast(I32), 0)
+        for window in windows[1:]:
+            nc.gpsimd.memset(window[:], 0.0)
 
         def pick(name, window, dtype, offsets, first, last, tag=None):
             got = keep.tile([P, last - first], dtype, name="%s%d" % (name, first),
@@ -129,46 +126,53 @@ def tile_list_gmu_tanh_scatP_kernel(
         v_w = pick("v_w", tab_w, U32, list1, 0, J)
         v2_s = pick("v2_s", tab2_s, U8, list2, 0, J)
 
-        wt_bf = keep.tile([P, PACK, P, PACK], BF16, name="wt_bf", align_bytes=64)
-        nc.scalar.copy(
-            wt_bf[:].rearrange("p t m i -> p m i t"), wt_raw[:].rearrange("p i (m t) -> p m i t", t=PACK))
-        wt_w = keep.tile([P, PACK, P], U32, name="wt_w", tag="wt_w", align_bytes=64)
-        wt_s = keep.tile([P, PACK, P], U8, name="wt_s", align_bytes=64)
-        nc.vector.quantize_mx(
-            out=wt_w[:].rearrange("p t m -> p (t m)").bitcast(FP8X4), scales=wt_s[:].rearrange("p t m -> p (t m)"),
-            in_=wt_bf[:].rearrange("p t m i -> p (t m i)"))
+        def deal(engine_copy, name, raw, dtype, pool=keep, offset=None):
+            dealt = pool.tile([P, PACK, P], dtype, name=name, align_bytes=64, offset=offset)
+            engine_copy(dealt[:], raw[:].rearrange("p (m t) -> p t m", t=PACK))
+            return dealt
 
-        wv_w = keep.tile([P, PACK, P], I32, name="wv_w", align_bytes=64)
-        zv_w = keep.tile([P, PACK, P], I32, name="zv_w", align_bytes=64)
-        zt_w = keep.tile([P, PACK, P, 2], U8, name="zt_w", align_bytes=64)
-        wv_s = keep.tile([P, PACK, P], U8, name="wv_s", align_bytes=64)
-        z_s = keep.tile([P, PACK, P], U8, name="z_s", align_bytes=64)
-        nc.gpsimd.tensor_copy(wv_w[:], wv_raw[:].rearrange("p (m t) -> p t m", t=PACK))
-        nc.gpsimd.tensor_copy(wv_s[:], wv_raw_s[:].rearrange("p (m t) -> p t m", t=PACK))
-        nc.gpsimd.tensor_copy(zv_w[:], zv_raw[:].rearrange("p (m t) -> p t m", t=PACK))
-        nc.gpsimd.tensor_copy(zt_w[:], zt_raw[:].rearrange("p (m t e) -> p t m e", t=PACK, e=2))
-        for pages_dealt in (slice(0, 1), slice(1, PACK)):
-            nc.gpsimd.tensor_copy(
-                z_s[:, pages_dealt, :], z_raw_s[:].rearrange("p (m t) -> p t m", t=PACK)[:, pages_dealt, :])
-        v2_w = {first: pick("v2_w", tab2_w, U32, list2, first, last)
-                for first, last in ((0, QUARTER), (QUARTER, HALF), (HALF, J))}
-        outer_page = keep.tile([P, T], F32, name="page0", tag="z_raw_s", align_bytes=64)
-        for first in range(0, T, CHUNK):
-            nc.gpsimd.memset(outer_page[:, first : first + CHUNK], 0.0)
-        pages = [outer_page] + middle_pages + [outer_page]
+        wv_s = deal(nc.vector.tensor_copy, "wv_s", wv_raw_s, U8)
+        wv_w = deal(nc.scalar.copy, "wv_w", wv_raw, U32)
+        wt_bf = [reused.tile([P, 2, P, PACK], BF16, name="wt_bf0", align_bytes=64, offset=0),
+                 keep.tile([P, 2, P, PACK], BF16, name="wt_bf1", align_bytes=64)]
+        for h, tile in enumerate(wt_bf):
+            nc.gpsimd.tensor_scalar(
+                tile[:].rearrange("p t m i -> p m t i"),
+                wt_raw[:].rearrange("p i (m t) -> p m t i", t=PACK)[:, :, 2 * h : 2 * h + 2, :],
+                1.0, 0.0, ALU.mult, ALU.add)
+        wt_w, wt_s = [], []
+
+        def quantise_wt(h, scales):
+            words = keep.tile([P, 2 * P], U32, name="wt_w%d" % h, align_bytes=64)
+            nc.vector.quantize_mx(out=words[:].bitcast(FP8X4), scales=scales[:],
+                                  in_=wt_bf[h][:].rearrange("p t m i -> p (t m i)"))
+            wt_w.extend([words[:, :P], words[:, P:]])
+            wt_s.extend([scales[:, :P], scales[:, P:]])
+
+        quantise_wt(0, keep.tile([P, 2 * P], U8, name="wt_s0", tag="tab2_s", align_bytes=64))
+        zt_w = deal(nc.scalar.copy, "zt_w", zt_raw, U16)
+        zv_w = deal(nc.scalar.copy, "zv_w", zv_raw, U32)
+        v2_w = {0: pick("v2_w", tab2_w, U32, list2, 0, HALF)}
+        z_s = deal(nc.gpsimd.tensor_copy, "z_s", z_raw_s, U8)
+        v2_w[HALF] = pick("v2_w", tab2_w, U32, list2, HALF, J, "z_raw_s")
+        quantise_wt(1, keep.tile([P, 2 * P], U8, name="wt_s1", tag="tab2_w", align_bytes=64))
 
         def picture_pass(acc, weight_w, weight_s, first, last, start, stop):
             nc.tensor.matmul_mx(
                 out=acc, lhsT=weight_w.bitcast(FP8X4), lhsT_scale=weight_s,
-                rhs=v_w[:, first:last].bitcast(FP8X4), rhs_scale=v_s[:, first:last], start=start, stop=stop,
+                rhs=v_w[:, first:last].bitcast(FP8X4), rhs_scale=v_s[TAB_ROW:, first:last], start=start, stop=stop,
             )
 
+        def text_words(first, last):
+            piece = max(j for j in v2_w if j <= first)
+            return v2_w[piece][:, first - piece : last - piece].bitcast(FP8X4)
+
         def text_passes(acc, weight, weight_s, first, last, start):
-            gathered = [j for j in sorted(v2_w) if first <= j < last]
-            for j, end in zip(gathered, gathered[1:] + [last]):
+            cuts = [first] + [j for j in sorted(v2_w) if first < j < last] + [last]
+            for j, end in zip(cuts, cuts[1:]):
                 nc.tensor.matmul_mx(
                     out=acc[:, j - first : end - first], lhsT=weight, lhsT_scale=weight_s,
-                    rhs=v2_w[j][:].bitcast(FP8X4), rhs_scale=v2_s[:, j:end],
+                    rhs=text_words(j, end), rhs_scale=v2_s[:, j:end],
                     start=start and j == first, stop=end == last,
                 )
 
@@ -178,47 +182,41 @@ def tile_list_gmu_tanh_scatP_kernel(
         mixed = keep.tile([P, PACK * J], F32, name="mixed", align_bytes=64)
         weighted = keep.tile([P, PACK * J], F32, name="weighted", align_bytes=64)
 
-        def span(t, h):
-            return slice(t * J + h * HALF, t * J + (h + 1) * HALF)
-
         def picture(t, first, last, kind):
             acc = next_bank(kind)[:, : last - first]
-            picture_pass(acc, wv_w[:, t, :], wv_s[:, t, :], first, last, True, True)
+            picture_pass(acc, wv_w[:, t, :], wv_s[WV_ROW:, t, :], first, last, True, True)
             nc.scalar.activation(av[:, t * J + first : t * J + last], acc, ACT.Tanh, bias=no_bias[:])
 
-        def gate_of(t, first, last):
-            acc = next_bank("late")[:, : last - first]
+        def gate_of(t, first, last, step=1):
+            acc = next_bank("late", step)[:, : last - first]
             picture_pass(acc, zv_w[:, t, :], z_s[ZV_ROW:, t, :], first, last, True, False)
-            text_passes(acc, zt_w[:, t, :, :].rearrange("p m e -> p (m e)").bitcast(FP4X4), z_s[ZT_ROW:, t, :],
-                        first, last, False)
+            text_passes(acc, zt_w[:, t, :].bitcast(U8).bitcast(FP4X4), z_s[ZT_ROW:, t, :], first, last, False)
             nc.scalar.activation(gate[:, t * J + first : t * J + last], acc, ACT.Sigmoid, bias=bias[:, t : t + 1])
 
-        def text(t, first, last, again=False):
-            acc = next_bank("late", again)[:, : last - first]
-            text_passes(acc, wt_w[:, t, :].bitcast(FP8X4), wt_s[:, t, :], first, last, True)
+        def text(t, first, last, step=1):
+            acc = next_bank("late", step)[:, : last - first]
+            text_passes(acc, wt_w[t].bitcast(FP8X4), wt_s[t], first, last, True)
             nc.scalar.activation(at[:, t * J + first : t * J + last], acc, ACT.Tanh, bias=no_bias[:])
 
-        def branch_turned(result, t, words, scales, weight_w, weight_s, sign, kind):
-            acc = next_bank(kind)
+        def branch_turned(result, t, words, scales, weight_w, weight_s, sign, kind, step=1):
+            acc = next_bank(kind, step)
             for j in range(0, HALF, P):
                 nc.tensor.matmul_mx(
-                    out=acc[:, j : j + P], lhsT=words(j), lhsT_scale=scales[:, j : j + P],
+                    out=acc[:, j : j + P], lhsT=words(j, j + P), lhsT_scale=scales[:, j : j + P],
                     rhs=weight_w.bitcast(FP8X4), rhs_scale=weight_s, start=True, stop=True,
                 )
-            nc.scalar.activation(result[:, span(t, 0)], acc[:], ACT.Tanh, bias=no_bias[:], scale=sign)
+            nc.scalar.activation(result[:, t * J : t * J + HALF], acc[:], ACT.Tanh, bias=no_bias[:], scale=sign)
 
         def picture_turned(t, kind):
-            branch_turned(av, t, lambda j: v_w[:, j : j + P].bitcast(FP8X4), v_s, wv_w[:, t, :], wv_s[:, t, :],
-                          1.0, kind)
+            branch_turned(av, t, lambda j, end: v_w[:, j:end].bitcast(FP8X4), v_s[TAB_ROW:, :], wv_w[:, t, :],
+                          wv_s[WV_ROW:, t, :], 1.0, kind)
 
-        def text_turned(t):
-            branch_turned(
-                at, t, lambda j: v2_w[j // QUARTER * QUARTER][:, j % QUARTER : j % QUARTER + P].bitcast(FP8X4),
-                v2_s, wt_w[:, t, :], wt_s[:, t, :], -1.0, "late")
+        def turned_sums(t, step):
+            branch_turned(at, t, text_words, v2_s, wt_w[t], wt_s[t], -1.0, "late", step)
 
         def turn(t):
             lo = t * J
-            diff = sums.tile([P, HALF], F32, name="diff_bank%d" % t, tag="early%d" % (1 + t % 2))
+            diff = sums.tile([P, HALF], F32, name="diff_bank%d" % t, tag=["early2", "early1", "wgo0"][t - 1])
             for c in range(0, HALF, P):
                 nc.tensor.matmul(diff[:, c : c + P], av[:, lo + c : lo + c + P], ident[:],
                                  start=c == 0, stop=False, is_transpose=True)
@@ -232,45 +230,49 @@ def tile_list_gmu_tanh_scatP_kernel(
             nc.scalar.copy(base[:], minus[:])
             return diff, base
 
-        def differ(engine, pool, lo, hi):
-            diff = pool.tile([P, hi - lo], F32, name="diff", tag="work", align_bytes=64)
-            engine.tensor_tensor(diff[:], av[:, lo:hi], at[:, lo:hi], ALU.subtract)
-            return diff
-
-        def weigh(engine, pool, diff, lo, hi):
-            gated = pool.tile([P, hi - lo], F32, name="gated", tag="work", align_bytes=64)
-            engine.tensor_tensor(gated[:], diff[:], gate[:, lo:hi], ALU.mult)
-            return gated
-
-        def join(engine, gated, lo, hi):
-            engine.tensor_tensor(mixed[:, lo:hi], gated[:], at[:, lo:hi], ALU.add)
-
-        def spread_wgo():
-            turned = next_bank("early")
-            nc.tensor.transpose(turned[:, 0:P], wgo_rows[:], ident[:])
-            nc.scalar.copy(wgo_cols[:], turned[:, 0 : J // P])
-            banks = [sums.tile([P, HALF], F32, name="wgo%d" % h) for h in range(2)]
-            for r in range(J // P):
-                nc.tensor.transpose(banks[r // BLOCKS][:, r % BLOCKS * P : (r % BLOCKS + 1) * P],
-                                    wgo_cols[:, r : r + 1].to_broadcast([P, P]), ident[:])
-            for h in range(2):
-                nc.scalar.copy(wgo_sb[:, h * HALF : (h + 1) * HALF], banks[h][:])
-            return banks
+        wgo_banks = [sums.tile([P, PACK, P], F32, name="wgo%d" % h, tag="wgo%d" % h) for h in range(2)]
+        for h in range(2):
+            for r in range(PACK):
+                nc.tensor.transpose(wgo_banks[h][:, r, :], wgo_cols[:, h, r : r + 1].to_broadcast([P, P]), ident[:])
 
         out_rows = out_0.rearrange("(p t) c -> p t c", t=PACK)
 
+        def differ(engine, diff, lo, hi):
+            engine.tensor_tensor(diff, av[:, lo:hi], at[:, lo:hi], ALU.subtract)
+            return diff
+
+        def work(tag):
+            return keep.tile([P, HALF], F32, name="work", tag=tag, align_bytes=64)
+
+        def weigh(engine, diff, lo, hi):
+            engine.tensor_tensor(av[:, lo:hi], diff, gate[:, lo:hi], ALU.mult)
+
+        def join(engine, lo, hi):
+            engine.tensor_tensor(mixed[:, lo:hi], av[:, lo:hi], at[:, lo:hi], ALU.add)
+
         def scale(lo, hi):
             j = lo % J
+            first, last = j % HALF // PACK, (j % HALF + hi - lo) // PACK
             nc.vector.tensor_tensor(
-                weighted[:, lo:hi], mixed[:, lo:hi], wgo_banks[j // HALF][:, j % HALF : j % HALF + hi - lo], ALU.mult)
+                weighted[:, lo:hi].rearrange("p (m r) -> p m r", r=PACK),
+                mixed[:, lo:hi].rearrange("p (m r) -> p m r", r=PACK),
+                wgo_banks[j // HALF][:].rearrange("p r m -> p m r")[:, first:last, :], ALU.mult)
 
-        def place(t, h):
-            window = pages[t][:].indirect(entries(list1, h * HALF, (h + 1) * HALF))
-            if (t, h) == units[-1]:
-                nc.vector.tensor_tensor(window, mixed[:, span(t, h)], wgo_sb[:, HALF:], ALU.mult)
+        def gate_turned(t, spent):
+            nc.vector.tensor_tensor(spent, gate[:, t * J : t * J + HALF], turned[t][0][:], ALU.mult)
+
+        def mix_turned(t, gated):
+            joined = av[:, t * J + HALF : (t + 1) * J]
+            nc.gpsimd.tensor_tensor(joined, gated, turned[t][1][:], ALU.subtract)
+            nc.gpsimd.tensor_tensor(weighted[:, t * J : t * J + HALF], joined, wgo_sb[:, :HALF], ALU.mult)
+
+        def place(t, first, last):
+            window = pages[t][:].indirect(entries(list1, first, last))
+            if (t, last) == (PACK - 1, J):
+                nc.vector.tensor_tensor(window, mixed[:, t * J + first : t * J + last], wgo_sb[:, first:], ALU.mult)
             else:
-                nc.vector.tensor_copy(window, weighted[:, span(t, h)])
-            if h == 1:
+                nc.vector.tensor_copy(window, weighted[:, t * J + first : t * J + last])
+            if last == J:
                 nc.sync.dma_start(out=out_rows[:, t, :], in_=pages[t][:])
                 weave(t)
 
@@ -286,24 +288,19 @@ def tile_list_gmu_tanh_scatP_kernel(
                 if first < hi:
                     nc.scalar.copy(tile[:, first - lo :, t], pages[t][:, first:hi])
 
-        units = [(t, h) for t in range(PACK) for h in range(2)]
-        wgo_banks = spread_wgo()
         quarters = [(0, QUARTER), (QUARTER, HALF)]
         picture(0, 0, HALF, "early")
         picture(0, HALF, J, "early")
         picture_turned(1, "early")
         picture(1, HALF, J, "early")
-        gate_of(0, *quarters[0])
-        text(0, *quarters[0])
-        text(0, *quarters[1], again=True)
-        gate_of(0, *quarters[1])
-        text(0, HALF, J)
-        gate_of(0, HALF, J)
+        for first in (0, HALF):
+            text(0, first, first + HALF)
+            gate_of(0, first, first + HALF)
         turned = {}
         for t in range(1, PACK):
             if t > 1:
                 picture_turned(t, "late")
-            text_turned(t)
+            turned_sums(t, 1)
             turned[t] = turn(t)
             gate_of(t, 0, HALF)
             gate_of(t, HALF, J)
@@ -311,32 +308,30 @@ def tile_list_gmu_tanh_scatP_kernel(
                 picture(t, HALF, J, "late")
             text(t, HALF, J)
         woven = [keep.tile([P, hi - lo, PACK], BF16, name="woven%d" % lo, tag=tag, align_bytes=64)
-                 for (lo, hi), tag in zip(CHUNKS, ["v_w0", "v2_w512", "v_s0", "v2_s0", "wt_w"])]
+                 for (lo, hi), tag in zip(CHUNKS, ["v_w0", "z_raw_s", "v_s0", "v2_s0", "wt_w1"])]
 
-        diffs = [differ(nc.vector, ring, *cols) for cols in quarters]
-        gateds = [weigh(nc.vector, pool, diff, *cols) for pool, diff, cols in zip((ring, single), diffs, quarters)]
-        for gated, cols in zip(gateds, quarters):
-            join(nc.vector, gated, *cols)
+        first_diff = work("wt_bf1")
+        diffs = [differ(nc.vector, first_diff[:, lo:hi], lo, hi) for lo, hi in quarters]
+        for diff, cols in zip(diffs, quarters):
+            weigh(nc.vector, diff, *cols)
+        for cols in quarters:
+            join(nc.vector, *cols)
         for cols in quarters:
             scale(*cols)
-        place(*units[0])
-
-        diff = differ(nc.gpsimd, single, HALF, J)
-        gated = weigh(nc.gpsimd, ring, diff, HALF, J)
-        join(nc.gpsimd, gated, HALF, J)
+        place(0, 0, HALF)
+        weigh(nc.gpsimd, differ(nc.gpsimd, work("diff")[:], HALF, J), HALF, J)
+        join(nc.gpsimd, HALF, J)
         for t in range(1, PACK):
-            earlier, now, later = span(t - 1, 1), span(t, 0), span(t, 1)
-            turned_diff, base = turned[t]
-            scale(earlier.start, earlier.stop)
-            nc.vector.tensor_tensor(at[:, earlier], gate[:, now], turned_diff[:], ALU.mult)
-            place(t - 1, 1)
-            diff = differ(nc.gpsimd, single, later.start, later.stop)
-            nc.gpsimd.tensor_tensor(av[:, later], at[:, earlier], base[:], ALU.subtract)
-            nc.gpsimd.tensor_tensor(weighted[:, now], av[:, later], wgo_sb[:, :HALF], ALU.mult)
-            place(t, 0)
-            nc.gpsimd.tensor_tensor(av[:, later], diff[:], gate[:, later], ALU.mult)
-            nc.gpsimd.tensor_tensor(mixed[:, later], av[:, later], at[:, later], ALU.add)
-        place(PACK - 1, 1)
+            earlier, later = ((t - 1) * J + HALF, t * J), (t * J + HALF, (t + 1) * J)
+            scale(*earlier)
+            gate_turned(t, at[:, slice(*earlier)])
+            place(t - 1, HALF, J)
+            diff = differ(nc.gpsimd, work("diff")[:], *later)
+            mix_turned(t, at[:, slice(*earlier)])
+            place(t, 0, HALF)
+            weigh(nc.gpsimd, diff, *later)
+            join(nc.gpsimd, *later)
+        place(PACK - 1, HALF, J)
 
         out_words = words_of(out_1)
         codes = keep.tile([P, T], U32, name="codes", align_bytes=64)

@@ -23,6 +23,7 @@ PACK = 4
 PER_COLUMN = 16
 HALF = 512
 QUARTER = 256
+EARLY_PAGES = 3
 CHUNKS = [(0, 512), (512, 1024), (1024, 1536), (1536, 1792), (1792, 2048)]
 VECTOR_COLUMNS = 768
 RING_BANKS = 3
@@ -67,7 +68,7 @@ def tile_list_gmu_tanh_scatP_kernel(
         tab_s = keep.tile([P, T], U8, name="tab_s", align_bytes=64)
         tab2_w = keep.tile([P, T], U32, name="tab2_w", align_bytes=64)
         tab2_s = keep.tile([P, T], U8, name="tab2_s", align_bytes=64)
-        z_raw_s = keep.tile([P, N], U8, name="z_raw_s", align_bytes=64)
+        z_raw_s = reused.tile([P, N], U8, name="z_raw_s", align_bytes=64, offset=4 * HALF - N // 2)
         wv_raw_s = keep.tile([P, N], U8, name="wv_raw_s", align_bytes=64)
         wv_raw = keep.tile([P, N], U32, name="wv_raw", align_bytes=64)
         zv_raw = keep.tile([P, N], U32, name="zv_raw", align_bytes=64)
@@ -94,31 +95,30 @@ def tile_list_gmu_tanh_scatP_kernel(
         z_planes = plane_loads(z_raw_s, ZV_ROW, zv_scales) + plane_loads(z_raw_s, ZT_ROW, zt_scales)
         wv_planes = plane_loads(wv_raw_s, WV_ROW, wv_scales)
         loads = (
-            [(list1[:], offs), (wgo_cols[:], wgo[0:1, :].rearrange("o (h p r) -> p (o h) r", h=2, r=PACK))]
+            [(list1[:], offs), (zv_raw[:].bitcast(I32), words_of(zv_words)),
+             (wv_raw[:].bitcast(I32), words_of(wv_words))]
             + plane_loads(tab_s, TAB_ROW, tab_scales)
             + [(tab_w[:].bitcast(I32), words_of(tab_words)), (list2[:], offs2)]
             + wv_planes
-            + [(wv_raw[:].bitcast(I32), words_of(wv_words)), (wt_raw[:], wt.rearrange("(p i) n -> p i n", i=PACK))]
+            + [(wt_raw[:], wt.rearrange("(p i) n -> p i n", i=PACK))]
             + plane_loads(tab2_s, 0, tab2_scales)
+            + [(zt_raw[:].bitcast(I32), zt_words[0].bitcast(I32))]
             + z_planes[:1]
-            + [(zt_raw[:].bitcast(I32), zt_words[0].bitcast(I32)), (tab2_w[:].bitcast(I32), words_of(tab2_words)),
-               (zv_raw[:].bitcast(I32), words_of(zv_words))]
-            + z_planes[1:-1]
-            + [(wgo_sb[:], wgo)]
+            + [(tab2_w[:].bitcast(I32), words_of(tab2_words))]
+            + z_planes[1:]
+            + [(bias[:], b.rearrange("(p t) -> p t", t=PACK)), (wgo_sb[:], wgo)]
         )
         for out, in_ in loads:
             nc.sync.dma_start(out, in_)
 
         make_identity(nc, ident[:])
-        nc.gpsimd.dma_start(bias[:], b.rearrange("(p t) -> p t", t=PACK))
-        nc.gpsimd.dma_start(*z_planes[-1])
+        nc.gpsimd.dma_start(wgo_cols[:], wgo[0:1, :].rearrange("o (h p r) -> p (o h) r", h=2, r=PACK))
         nc.vector.memset(windows[0][:].bitcast(I32), 0)
         for window in windows[1:]:
             nc.gpsimd.memset(window[:], 0.0)
 
-        def pick(name, window, dtype, offsets, first, last, tag=None):
-            got = keep.tile([P, last - first], dtype, name="%s%d" % (name, first),
-                            tag=tag or "%s%d" % (name, first), align_bytes=64)
+        def pick(name, window, dtype, offsets, first, last, pool=keep, offset=None):
+            got = pool.tile([P, last - first], dtype, name="%s%d" % (name, first), align_bytes=64, offset=offset)
             nc.vector.tensor_copy(got[:], window[:].indirect(entries(offsets, first, last)))
             return got
 
@@ -126,35 +126,39 @@ def tile_list_gmu_tanh_scatP_kernel(
         v_w = pick("v_w", tab_w, U32, list1, 0, J)
         v2_s = pick("v2_s", tab2_s, U8, list2, 0, J)
 
-        def deal(engine_copy, name, raw, dtype, pool=keep, offset=None):
-            dealt = pool.tile([P, PACK, P], dtype, name=name, align_bytes=64, offset=offset)
+        def deal(engine_copy, name, raw, dtype):
+            dealt = keep.tile([P, PACK, P], dtype, name=name, align_bytes=64)
             engine_copy(dealt[:], raw[:].rearrange("p (m t) -> p t m", t=PACK))
             return dealt
 
-        wv_s = deal(nc.vector.tensor_copy, "wv_s", wv_raw_s, U8)
+        zv_w = deal(nc.scalar.copy, "zv_w", zv_raw, U32)
         wv_w = deal(nc.scalar.copy, "wv_w", wv_raw, U32)
-        wt_bf = [reused.tile([P, 2, P, PACK], BF16, name="wt_bf0", align_bytes=64, offset=0),
-                 keep.tile([P, 2, P, PACK], BF16, name="wt_bf1", align_bytes=64)]
-        for h, tile in enumerate(wt_bf):
+        wv_s = deal(nc.gpsimd.tensor_copy, "wv_s", wv_raw_s, U8)
+        wt_bf = []
+
+        def round_wt(h, tile):
             nc.gpsimd.tensor_scalar(
-                tile[:].rearrange("p t m i -> p m t i"),
+                tile.rearrange("p (t m i) -> p m t i", t=2, i=PACK),
                 wt_raw[:].rearrange("p i (m t) -> p m t i", t=PACK)[:, :, 2 * h : 2 * h + 2, :],
                 1.0, 0.0, ALU.mult, ALU.add)
+            wt_bf.append(tile)
+
+        round_wt(0, keep.tile([P, J], BF16, name="wt_bf0", tag="wv_raw_s", align_bytes=64)[:])
         wt_w, wt_s = [], []
 
         def quantise_wt(h, scales):
             words = keep.tile([P, 2 * P], U32, name="wt_w%d" % h, align_bytes=64)
             nc.vector.quantize_mx(out=words[:].bitcast(FP8X4), scales=scales[:],
-                                  in_=wt_bf[h][:].rearrange("p t m i -> p (t m i)"))
+                                  in_=wt_bf[h])
             wt_w.extend([words[:, :P], words[:, P:]])
             wt_s.extend([scales[:, :P], scales[:, P:]])
 
         quantise_wt(0, keep.tile([P, 2 * P], U8, name="wt_s0", tag="tab2_s", align_bytes=64))
         zt_w = deal(nc.scalar.copy, "zt_w", zt_raw, U16)
-        zv_w = deal(nc.scalar.copy, "zv_w", zv_raw, U32)
         v2_w = {0: pick("v2_w", tab2_w, U32, list2, 0, HALF)}
         z_s = deal(nc.gpsimd.tensor_copy, "z_s", z_raw_s, U8)
-        v2_w[HALF] = pick("v2_w", tab2_w, U32, list2, HALF, J, "z_raw_s")
+        round_wt(1, reused.tile([P, J], BF16, name="wt_bf1", align_bytes=64, offset=4 * HALF)[:])
+        v2_w[HALF] = pick("v2_w", tab2_w, U32, list2, HALF, J, reused, 0)
         quantise_wt(1, keep.tile([P, 2 * P], U8, name="wt_s1", tag="tab2_w", align_bytes=64))
 
         def picture_pass(acc, weight_w, weight_s, first, last, start, stop):
@@ -191,7 +195,10 @@ def tile_list_gmu_tanh_scatP_kernel(
             acc = next_bank("late", step)[:, : last - first]
             picture_pass(acc, zv_w[:, t, :], z_s[ZV_ROW:, t, :], first, last, True, False)
             text_passes(acc, zt_w[:, t, :].bitcast(U8).bitcast(FP4X4), z_s[ZT_ROW:, t, :], first, last, False)
-            nc.scalar.activation(gate[:, t * J + first : t * J + last], acc, ACT.Sigmoid, bias=bias[:, t : t + 1])
+            width = QUARTER if (t, first) == (0, 0) else HALF
+            for j in range(first, last, width):
+                nc.scalar.activation(gate[:, t * J + j : t * J + j + width], acc[:, j - first : j - first + width],
+                                     ACT.Sigmoid, bias=bias[:, t : t + 1])
 
         def text(t, first, last, step=1):
             acc = next_bank("late", step)[:, : last - first]
@@ -291,26 +298,28 @@ def tile_list_gmu_tanh_scatP_kernel(
         quarters = [(0, QUARTER), (QUARTER, HALF)]
         picture(0, 0, HALF, "early")
         picture(0, HALF, J, "early")
-        picture_turned(1, "early")
-        picture(1, HALF, J, "early")
-        for first in (0, HALF):
-            text(0, first, first + HALF)
-            gate_of(0, first, first + HALF)
+        for t in range(1, EARLY_PAGES):
+            picture_turned(t, "early")
+            picture(t, HALF, J, "early")
+        text(0, 0, HALF)
+        gate_of(0, 0, HALF)
+        gate_of(0, HALF, J)
+        text(0, HALF, J)
         turned = {}
         for t in range(1, PACK):
-            if t > 1:
+            if t >= EARLY_PAGES:
                 picture_turned(t, "late")
             turned_sums(t, 1)
             turned[t] = turn(t)
             gate_of(t, 0, HALF)
             gate_of(t, HALF, J)
-            if t > 1:
+            if t >= EARLY_PAGES:
                 picture(t, HALF, J, "late")
             text(t, HALF, J)
         woven = [keep.tile([P, hi - lo, PACK], BF16, name="woven%d" % lo, tag=tag, align_bytes=64)
-                 for (lo, hi), tag in zip(CHUNKS, ["v_w0", "z_raw_s", "v_s0", "v2_s0", "wt_w1"])]
+                 for (lo, hi), tag in zip(CHUNKS, ["v_w0", "tab2_w", "v_s0", "v2_s0", "wt_w1"])]
 
-        first_diff = work("wt_bf1")
+        first_diff = reused.tile([P, HALF], F32, name="first_diff", align_bytes=64, offset=4 * HALF)
         diffs = [differ(nc.vector, first_diff[:, lo:hi], lo, hi) for lo, hi in quarters]
         for diff, cols in zip(diffs, quarters):
             weigh(nc.vector, diff, *cols)
@@ -336,15 +345,12 @@ def tile_list_gmu_tanh_scatP_kernel(
         out_words = words_of(out_1)
         codes = keep.tile([P, T], U32, name="codes", align_bytes=64)
         plane = keep.tile([P, T], U8, name="plane", align_bytes=64)
-        stored = 0
         for (lo, hi), tile in zip(CHUNKS, woven):
             nc.vector.quantize_mx(
                 out=codes[:, lo:hi].bitcast(FP8X4), scales=plane[:, lo:hi],
                 in_=tile[:].rearrange("p c i -> p (c i)"),
             )
-            if hi >= J:
-                nc.sync.dma_start(out=out_words[:, stored:hi], in_=codes[:, stored:hi].bitcast(I32))
-                stored = hi
+            nc.sync.dma_start(out=out_words[:, lo:hi], in_=codes[:, lo:hi].bitcast(I32))
         for r in range(4):
             queue = nc.scalar if r % 2 else nc.sync
             queue.dma_start(out=out_2[0, r : 16 : 4, :].bitcast(I32), in_=plane[r : P : 32, :].bitcast(I32))

@@ -200,10 +200,12 @@ def tile_list_gmu_tanh_scatP_kernel(
                 nc.scalar.activation(gate[:, t * J + j : t * J + j + width], acc[:, j - first : j - first + width],
                                      ACT.Sigmoid, bias=bias[:, t : t + 1])
 
-        def text(t, first, last, step=1):
-            acc = next_bank("late", step)[:, : last - first]
+        def text(t, first, last, result=None):
+            acc = next_bank("late")[:, : last - first]
             text_passes(acc, wt_w[t].bitcast(FP8X4), wt_s[t], first, last, True)
-            nc.scalar.activation(at[:, t * J + first : t * J + last], acc, ACT.Tanh, bias=no_bias[:])
+            if result is None:
+                result = at[:, t * J + first : t * J + last]
+            nc.scalar.activation(result, acc, ACT.Tanh, bias=no_bias[:])
 
         def branch_turned(result, t, words, scales, weight_w, weight_s, sign, kind, step=1):
             acc = next_bank(kind, step)
@@ -230,12 +232,7 @@ def tile_list_gmu_tanh_scatP_kernel(
             for c in range(0, HALF, P):
                 nc.tensor.matmul(diff[:, c : c + P], at[:, lo + c : lo + c + P], ident[:],
                                  start=False, stop=c + P == HALF, is_transpose=True)
-            minus = sums.tile([P, HALF], F32, name="minus_bank%d" % t, tag="early0")
-            for c in range(0, HALF, P):
-                nc.tensor.transpose(minus[:, c : c + P], at[:, lo + c : lo + c + P], ident[:])
-            base = keep.tile([P, HALF], F32, name="base%d" % t, align_bytes=64)
-            nc.scalar.copy(base[:], minus[:])
-            return diff, base
+            return diff
 
         wgo_banks = [sums.tile([P, PACK, P], F32, name="wgo%d" % h, tag="wgo%d" % h) for h in range(2)]
         for h in range(2):
@@ -270,7 +267,7 @@ def tile_list_gmu_tanh_scatP_kernel(
 
         def mix_turned(t, gated):
             joined = av[:, t * J + HALF : (t + 1) * J]
-            nc.gpsimd.tensor_tensor(joined, gated, turned[t][1][:], ALU.subtract)
+            nc.gpsimd.tensor_tensor(joined, gated, turned[t][1][:], ALU.add)
             nc.gpsimd.tensor_tensor(weighted[:, t * J : t * J + HALF], joined, wgo_sb[:, :HALF], ALU.mult)
 
         def place(t, first, last):
@@ -310,14 +307,16 @@ def tile_list_gmu_tanh_scatP_kernel(
             if t >= EARLY_PAGES:
                 picture_turned(t, "late")
             turned_sums(t, 1)
-            turned[t] = turn(t)
-            gate_of(t, 0, HALF)
-            gate_of(t, HALF, J)
             if t >= EARLY_PAGES:
                 picture(t, HALF, J, "late")
             text(t, HALF, J)
+            gate_of(t, 0, HALF)
+            base = keep.tile([P, HALF], F32, name="base%d" % t, align_bytes=64)
+            turned[t] = (turn(t), base)
+            text(t, 0, HALF, base[:])
+            gate_of(t, HALF, J)
         woven = [keep.tile([P, hi - lo, PACK], BF16, name="woven%d" % lo, tag=tag, align_bytes=64)
-                 for (lo, hi), tag in zip(CHUNKS, ["v_w0", "tab2_w", "v_s0", "v2_s0", "wt_w1"])]
+                 for (lo, hi), tag in zip(CHUNKS, ["v_w0", "z_s", "v_s0", "v2_s0", "zv_w"])]
 
         first_diff = reused.tile([P, HALF], F32, name="first_diff", align_bytes=64, offset=4 * HALF)
         diffs = [differ(nc.vector, first_diff[:, lo:hi], lo, hi) for lo, hi in quarters]

@@ -86,6 +86,7 @@ def tile_list_gmu_tanh_scatP_kernel(
 
         nc.gpsimd.memset(tab_s[:].bitcast(I32), 0)
         nc.vector.memset(cleared[:], 0.0)
+        nc.vector.memset(windows[0][:].bitcast(I32), 0)
         nc.vector.memset(z_raw_s[:].bitcast(I32), 0)
         nc.vector.memset(wv_raw_s[:].bitcast(I32), 0)
         nc.vector.memset(tab2_s[:].bitcast(I32), 0)
@@ -113,7 +114,6 @@ def tile_list_gmu_tanh_scatP_kernel(
 
         make_identity(nc, ident[:])
         nc.gpsimd.dma_start(wgo_cols[:], wgo[0:1, :].rearrange("o (h p r) -> p (o h) r", h=2, r=PACK))
-        nc.vector.memset(windows[0][:].bitcast(I32), 0)
         for window in windows[1:]:
             nc.gpsimd.memset(window[:], 0.0)
 
@@ -225,12 +225,13 @@ def tile_list_gmu_tanh_scatP_kernel(
 
         def turn(t):
             lo = t * J
-            diff = sums.tile([P, HALF], F32, name="diff_bank%d" % t, tag=["early2", "early1", "wgo0"][t - 1])
+            opening, closing = (av, at) if t == 1 else (at, av)
+            diff = sums.tile([P, HALF], F32, name="diff_bank%d" % t, tag="early%d" % (t - 1))
             for c in range(0, HALF, P):
-                nc.tensor.matmul(diff[:, c : c + P], av[:, lo + c : lo + c + P], ident[:],
+                nc.tensor.matmul(diff[:, c : c + P], opening[:, lo + c : lo + c + P], ident[:],
                                  start=c == 0, stop=False, is_transpose=True)
             for c in range(0, HALF, P):
-                nc.tensor.matmul(diff[:, c : c + P], at[:, lo + c : lo + c + P], ident[:],
+                nc.tensor.matmul(diff[:, c : c + P], closing[:, lo + c : lo + c + P], ident[:],
                                  start=False, stop=c + P == HALF, is_transpose=True)
             return diff
 

@@ -301,8 +301,8 @@ def tile_list_gmu_tanh_scatP_kernel(
             picture(t, HALF, J, "early")
         text(0, 0, HALF)
         gate_of(0, 0, HALF)
-        gate_of(0, HALF, J)
         text(0, HALF, J)
+        gate_of(0, HALF, J)
         turned = {}
         for t in range(1, PACK):
             if t >= EARLY_PAGES:

@@ -23,10 +23,9 @@ PACK = 4
 PER_COLUMN = 16
 HALF = 512
 QUARTER = 256
-EARLY_PAGES = 3
 CHUNKS = [(0, 512), (512, 1024), (1024, 1536), (1536, 1792), (1792, 2048)]
 VECTOR_COLUMNS = 768
-RING_BANKS = 3
+RING_BANKS = 4
 TAB_ROW, WV_ROW, ZT_ROW, ZV_ROW = 4, 4, 0, 8
 
 
@@ -55,12 +54,14 @@ def tile_list_gmu_tanh_scatP_kernel(
         reused = ctx.enter_context(tc.tile_pool(name="reused", bufs=1))
         sums = ctx.enter_context(tc.psum_pool(name="sums", bufs=1))
 
-        taken = {"early": [-1], "late": [-1]}
+        ring = [sums.tile([P, HALF], F32, name="ring%d" % i) for i in range(RING_BANKS)]
+        first_banks = [sums.tile([P, HALF], F32, name="first%d" % i) for i in range(2)]
+        wgo_banks = [sums.tile([P, HALF], F32, name="wgo%d" % h) for h in range(2)]
+        taken = []
 
-        def next_bank(kind, step=1):
-            taken[kind].append((taken[kind][-1] + step) % RING_BANKS)
-            return sums.tile([P, HALF], F32, name="%s%d" % (kind, len(taken[kind])),
-                             tag="%s%d" % (kind, taken[kind][-1]))
+        def next_bank():
+            taken.append(ring[len(taken) % RING_BANKS])
+            return taken[-1]
 
         list1 = keep.tile([P, J // PER_COLUMN], U16, name="list1")
         list2 = keep.tile([P, J // PER_COLUMN], U16, name="list2")
@@ -68,13 +69,15 @@ def tile_list_gmu_tanh_scatP_kernel(
         tab_s = keep.tile([P, T], U8, name="tab_s", align_bytes=64)
         tab2_w = keep.tile([P, T], U32, name="tab2_w", align_bytes=64)
         tab2_s = keep.tile([P, T], U8, name="tab2_s", align_bytes=64)
-        z_raw_s = reused.tile([P, N], U8, name="z_raw_s", align_bytes=64, offset=4 * HALF - N // 2)
+        z_room = reused.tile([P, 6 * N], U8, name="z_room", align_bytes=64, offset=4 * HALF - N // 2)
+        z_raw_s = z_room[:, :N]
         wv_raw_s = keep.tile([P, N], U8, name="wv_raw_s", align_bytes=64)
         wv_raw = keep.tile([P, N], U32, name="wv_raw", align_bytes=64)
         zv_raw = keep.tile([P, N], U32, name="zv_raw", align_bytes=64)
         zt_raw = keep.tile([P, N], U16, name="zt_raw", align_bytes=64)
         wt_raw = keep.tile([P, PACK, N], F32, name="wt_raw", align_bytes=64)
         bias = keep.tile([P, PACK], F32, name="bias")
+        minus_bias = keep.tile([P, 1], F32, name="minus_bias")
         wgo_cols = keep.tile([P, 2, PACK], F32, name="wgo_cols", align_bytes=64)
         wgo_sb = keep.tile([P, J], F32, name="wgo_sb", align_bytes=64)
         ident = keep.tile([P, P], F32, name="ident", align_bytes=64)
@@ -86,9 +89,9 @@ def tile_list_gmu_tanh_scatP_kernel(
 
         nc.gpsimd.memset(tab_s[:].bitcast(I32), 0)
         nc.vector.memset(cleared[:], 0.0)
-        nc.vector.memset(windows[0][:].bitcast(I32), 0)
-        nc.vector.memset(z_raw_s[:].bitcast(I32), 0)
         nc.vector.memset(wv_raw_s[:].bitcast(I32), 0)
+        nc.vector.memset(windows[0][:].bitcast(I32), 0)
+        nc.vector.memset(z_raw_s.bitcast(I32), 0)
         nc.vector.memset(tab2_s[:].bitcast(I32), 0)
         nc.scalar.activation(half[:], cleared[:], ACT.Sigmoid)
         nc.scalar.activation(no_bias[:], half[:], ACT.Tanh, scale=0.0)
@@ -99,7 +102,8 @@ def tile_list_gmu_tanh_scatP_kernel(
             [(list1[:], offs), (zv_raw[:].bitcast(I32), words_of(zv_words)),
              (wv_raw[:].bitcast(I32), words_of(wv_words))]
             + plane_loads(tab_s, TAB_ROW, tab_scales)
-            + [(tab_w[:].bitcast(I32), words_of(tab_words)), (list2[:], offs2)]
+            + [(tab_w[:].bitcast(I32), words_of(tab_words)), (list2[:], offs2),
+               (bias[:], b.rearrange("(p t) -> p t", t=PACK))]
             + wv_planes
             + [(wt_raw[:], wt.rearrange("(p i) n -> p i n", i=PACK))]
             + plane_loads(tab2_s, 0, tab2_scales)
@@ -107,7 +111,7 @@ def tile_list_gmu_tanh_scatP_kernel(
             + z_planes[:1]
             + [(tab2_w[:].bitcast(I32), words_of(tab2_words))]
             + z_planes[1:]
-            + [(bias[:], b.rearrange("(p t) -> p t", t=PACK)), (wgo_sb[:], wgo)]
+            + [(wgo_sb[:], wgo)]
         )
         for out, in_ in loads:
             nc.sync.dma_start(out, in_)
@@ -117,22 +121,24 @@ def tile_list_gmu_tanh_scatP_kernel(
         for window in windows[1:]:
             nc.gpsimd.memset(window[:], 0.0)
 
-        def pick(name, window, dtype, offsets, first, last, pool=keep, offset=None):
-            got = pool.tile([P, last - first], dtype, name="%s%d" % (name, first), align_bytes=64, offset=offset)
-            nc.vector.tensor_copy(got[:], window[:].indirect(entries(offsets, first, last)))
-            return got
+        def gather(got, window, offsets, first, last):
+            nc.vector.tensor_copy(got, window[:].indirect(entries(offsets, first, last)))
 
-        v_s = pick("v_s", tab_s, U8, list1, 0, J)
-        v_w = pick("v_w", tab_w, U32, list1, 0, J)
-        v2_s = pick("v2_s", tab2_s, U8, list2, 0, J)
+        v_s = keep.tile([P, J], U8, name="v_s", align_bytes=64)
+        v_w = keep.tile([P, J], U32, name="v_w", align_bytes=64)
+        v2_s = keep.tile([P, J], U8, name="v2_s", align_bytes=64)
+        gather(v_s[:], tab_s, list1, 0, J)
+        gather(v_w[:, :HALF], tab_w, list1, 0, HALF)
+        gather(v_w[:, HALF:], tab_w, list1, HALF, J)
+        gather(v2_s[:], tab2_s, list2, 0, J)
 
         def deal(engine_copy, name, raw, dtype):
             dealt = keep.tile([P, PACK, P], dtype, name=name, align_bytes=64)
             engine_copy(dealt[:], raw[:].rearrange("p (m t) -> p t m", t=PACK))
             return dealt
 
-        zv_w = deal(nc.scalar.copy, "zv_w", zv_raw, U32)
         wv_w = deal(nc.scalar.copy, "wv_w", wv_raw, U32)
+        zv_w = deal(nc.scalar.copy, "zv_w", zv_raw, U32)
         wv_s = deal(nc.gpsimd.tensor_copy, "wv_s", wv_raw_s, U8)
         wt_bf = []
 
@@ -148,138 +154,161 @@ def tile_list_gmu_tanh_scatP_kernel(
 
         def quantise_wt(h, scales):
             words = keep.tile([P, 2 * P], U32, name="wt_w%d" % h, align_bytes=64)
-            nc.vector.quantize_mx(out=words[:].bitcast(FP8X4), scales=scales[:],
-                                  in_=wt_bf[h])
+            nc.vector.quantize_mx(out=words[:].bitcast(FP8X4), scales=scales[:], in_=wt_bf[h])
             wt_w.extend([words[:, :P], words[:, P:]])
             wt_s.extend([scales[:, :P], scales[:, P:]])
 
         quantise_wt(0, keep.tile([P, 2 * P], U8, name="wt_s0", tag="tab2_s", align_bytes=64))
         zt_w = deal(nc.scalar.copy, "zt_w", zt_raw, U16)
-        v2_w = {0: pick("v2_w", tab2_w, U32, list2, 0, HALF)}
+        v2_w = [keep.tile([P, HALF], U32, name="v2_w0", align_bytes=64)]
+        gather(v2_w[0][:, :QUARTER], tab2_w, list2, 0, QUARTER)
+        gather(v2_w[0][:, QUARTER:], tab2_w, list2, QUARTER, HALF)
         z_s = deal(nc.gpsimd.tensor_copy, "z_s", z_raw_s, U8)
         round_wt(1, reused.tile([P, J], BF16, name="wt_bf1", align_bytes=64, offset=4 * HALF)[:])
-        v2_w[HALF] = pick("v2_w", tab2_w, U32, list2, HALF, J, reused, 0)
+        v2_w.append(reused.tile([P, HALF], U32, name="v2_w1", align_bytes=64, offset=0))
+        gather(v2_w[1][:], tab2_w, list2, HALF, J)
         quantise_wt(1, keep.tile([P, 2 * P], U8, name="wt_s1", tag="tab2_w", align_bytes=64))
+        nc.scalar.activation(minus_bias[:], bias[:, 0:1], ACT.Copy, scale=-1.0)
 
-        def picture_pass(acc, weight_w, weight_s, first, last, start, stop):
-            nc.tensor.matmul_mx(
-                out=acc, lhsT=weight_w.bitcast(FP8X4), lhsT_scale=weight_s,
-                rhs=v_w[:, first:last].bitcast(FP8X4), rhs_scale=v_s[TAB_ROW:, first:last], start=start, stop=stop,
-            )
+        def picture_words(first, last):
+            return v_w[:, first:last].bitcast(FP8X4)
 
         def text_words(first, last):
-            piece = max(j for j in v2_w if j <= first)
-            return v2_w[piece][:, first - piece : last - piece].bitcast(FP8X4)
+            h = first // HALF
+            return v2_w[h][:, first - h * HALF : last - h * HALF].bitcast(FP8X4)
 
-        def text_passes(acc, weight, weight_s, first, last, start):
-            cuts = [first] + [j for j in sorted(v2_w) if first < j < last] + [last]
-            for j, end in zip(cuts, cuts[1:]):
-                nc.tensor.matmul_mx(
-                    out=acc[:, j - first : end - first], lhsT=weight, lhsT_scale=weight_s,
-                    rhs=text_words(j, end), rhs_scale=v2_s[:, j:end],
-                    start=start and j == first, stop=end == last,
-                )
+        def picture_side(t):
+            return wv_w[:, t, :].bitcast(FP8X4), wv_s[WV_ROW:, t, :], picture_words, v_s[TAB_ROW:, :]
+
+        def text_side(t):
+            return wt_w[t].bitcast(FP8X4), wt_s[t], text_words, v2_s
 
         av = keep.tile([P, PACK * J], F32, name="av", align_bytes=64)
         at = keep.tile([P, PACK * J], F32, name="at", align_bytes=64)
         gate = keep.tile([P, PACK * J], F32, name="gate", align_bytes=64)
-        mixed = keep.tile([P, PACK * J], F32, name="mixed", align_bytes=64)
-        weighted = keep.tile([P, PACK * J], F32, name="weighted", align_bytes=64)
+        ready = keep.tile([P, PACK * J], F32, name="ready", align_bytes=64)
+        base = keep.tile([P, PACK * HALF], F32, name="base", align_bytes=64)
+        gated = keep.tile([P, PACK * HALF], F32, name="gated", align_bytes=64)
+        work = keep.tile([P, HALF], F32, name="work", align_bytes=64)
 
-        def picture(t, first, last, kind):
-            acc = next_bank(kind)[:, : last - first]
-            picture_pass(acc, wv_w[:, t, :], wv_s[WV_ROW:, t, :], first, last, True, True)
-            nc.scalar.activation(av[:, t * J + first : t * J + last], acc, ACT.Tanh, bias=no_bias[:])
+        def cols(tile, u, lo=0, hi=HALF):
+            return tile[:, u * HALF + lo : u * HALF + hi]
 
-        def gate_of(t, first, last, step=1):
-            acc = next_bank("late", step)[:, : last - first]
-            picture_pass(acc, zv_w[:, t, :], z_s[ZV_ROW:, t, :], first, last, True, False)
-            text_passes(acc, zt_w[:, t, :].bitcast(U8).bitcast(FP4X4), z_s[ZT_ROW:, t, :], first, last, False)
-            width = QUARTER if (t, first) == (0, 0) else HALF
-            for j in range(first, last, width):
-                nc.scalar.activation(gate[:, t * J + j : t * J + j + width], acc[:, j - first : j - first + width],
-                                     ACT.Sigmoid, bias=bias[:, t : t + 1])
+        def plain(side, result, u):
+            weight, weight_s, words, scales = side(u // 2)
+            j = u % 2 * HALF
+            acc = next_bank()
+            nc.tensor.matmul_mx(out=acc[:], lhsT=weight, lhsT_scale=weight_s, rhs=words(j, j + HALF),
+                                rhs_scale=scales[:, j : j + HALF], start=True, stop=True)
+            nc.scalar.activation(result, acc[:], ACT.Tanh, bias=no_bias[:])
 
-        def text(t, first, last, result=None):
-            acc = next_bank("late")[:, : last - first]
-            text_passes(acc, wt_w[t].bitcast(FP8X4), wt_s[t], first, last, True)
-            if result is None:
-                result = at[:, t * J + first : t * J + last]
-            nc.scalar.activation(result, acc, ACT.Tanh, bias=no_bias[:])
+        def turned(side, result, u, sign, lo=0, hi=HALF):
+            weight, weight_s, words, scales = side(u // 2)
+            j = u % 2 * HALF
+            acc = next_bank()
+            for c in range(lo, hi, P):
+                nc.tensor.matmul_mx(out=acc[:, c - lo : c - lo + P], lhsT=words(j + c, j + c + P),
+                                    lhsT_scale=scales[:, j + c : j + c + P], rhs=weight, rhs_scale=weight_s,
+                                    start=True, stop=True)
+            nc.scalar.activation(cols(result, u, lo, hi), acc[:, : hi - lo], ACT.Tanh, bias=no_bias[:], scale=sign)
 
-        def branch_turned(result, t, words, scales, weight_w, weight_s, sign, kind, step=1):
-            acc = next_bank(kind, step)
-            for j in range(0, HALF, P):
-                nc.tensor.matmul_mx(
-                    out=acc[:, j : j + P], lhsT=words(j, j + P), lhsT_scale=scales[:, j : j + P],
-                    rhs=weight_w.bitcast(FP8X4), rhs_scale=weight_s, start=True, stop=True,
-                )
-            nc.scalar.activation(result[:, t * J : t * J + HALF], acc[:], ACT.Tanh, bias=no_bias[:], scale=sign)
+        def gate_of(u):
+            t, j = u // 2, u % 2 * HALF
+            acc = next_bank()
+            nc.tensor.matmul_mx(out=acc[:], lhsT=zv_w[:, t, :].bitcast(FP8X4), lhsT_scale=z_s[ZV_ROW:, t, :],
+                                rhs=picture_words(j, j + HALF), rhs_scale=v_s[TAB_ROW:, j : j + HALF],
+                                start=True, stop=False)
+            nc.tensor.matmul_mx(out=acc[:], lhsT=zt_w[:, t, :].bitcast(U8).bitcast(FP4X4),
+                                lhsT_scale=z_s[ZT_ROW:, t, :], rhs=text_words(j, j + HALF),
+                                rhs_scale=v2_s[:, j : j + HALF], start=False, stop=True)
+            if u == 0:
+                for lo, hi in quarters:
+                    nc.scalar.activation(cols(gate, u, lo, hi), acc[:, lo:hi], ACT.Sigmoid, bias=minus_bias[:],
+                                         scale=-1.0)
+            else:
+                nc.scalar.activation(cols(gate, u), acc[:], ACT.Sigmoid, bias=bias[:, t : t + 1])
 
-        def picture_turned(t, kind):
-            branch_turned(av, t, lambda j, end: v_w[:, j:end].bitcast(FP8X4), v_s[TAB_ROW:, :], wv_w[:, t, :],
-                          wv_s[WV_ROW:, t, :], 1.0, kind)
+        def turn_back(bank, source, opens, closes):
+            width = source.shape[1]
+            for c in range(0, width, P):
+                nc.tensor.matmul(bank[:, c : c + P], source[:, c : c + P], ident[:],
+                                 start=opens and c == 0, stop=closes and c + P == width, is_transpose=True)
 
-        def turned_sums(t, step):
-            branch_turned(at, t, text_words, v2_s, wt_w[t], wt_s[t], -1.0, "late", step)
-
-        def turn(t):
-            lo = t * J
-            opening, closing = (av, at) if t == 1 else (at, av)
-            diff = sums.tile([P, HALF], F32, name="diff_bank%d" % t, tag="early%d" % (t - 1))
-            for c in range(0, HALF, P):
-                nc.tensor.matmul(diff[:, c : c + P], opening[:, lo + c : lo + c + P], ident[:],
-                                 start=c == 0, stop=False, is_transpose=True)
-            for c in range(0, HALF, P):
-                nc.tensor.matmul(diff[:, c : c + P], closing[:, lo + c : lo + c + P], ident[:],
-                                 start=False, stop=c + P == HALF, is_transpose=True)
-            return diff
-
-        wgo_banks = [sums.tile([P, PACK, P], F32, name="wgo%d" % h, tag="wgo%d" % h) for h in range(2)]
         for h in range(2):
             for r in range(PACK):
-                nc.tensor.transpose(wgo_banks[h][:, r, :], wgo_cols[:, h, r : r + 1].to_broadcast([P, P]), ident[:])
+                nc.tensor.transpose(wgo_banks[h][:, r * P : (r + 1) * P],
+                                    wgo_cols[:, h, r : r + 1].to_broadcast([P, P]), ident[:])
+
+        quarters = [(0, QUARTER), (QUARTER, HALF)]
+        diffs = {2: first_banks[0], 4: first_banks[1], 6: wgo_banks[0]}
+        turned(picture_side, av, 0, 1.0)
+        plain(picture_side, cols(av, 1), 1)
+        for (lo, hi), bank in zip(quarters, first_banks):
+            turn_back(bank[:, :QUARTER], cols(av, 0, lo, hi), True, True)
+            turn_back(bank[:, QUARTER:], cols(av, 0, lo, hi), True, False)
+        turned(picture_side, av, 2, 1.0)
+        plain(picture_side, cols(av, 3), 3)
+        turned(picture_side, av, 4, 1.0)
+        plain(picture_side, cols(av, 5), 5)
+        first_at = reused.tile([P, HALF], F32, name="first_at", align_bytes=64, offset=8 * HALF)
+        for (lo, hi), bank in zip(quarters, first_banks):
+            turned(text_side, first_at, 0, -1.0, lo, hi)
+            turn_back(bank[:, QUARTER:], first_at[:, lo:hi], False, True)
+        gate_of(0)
+        plain(text_side, cols(at, 1), 1)
+        gate_of(1)
+        ring[3], ring[0] = ring[0], ring[3]
 
         out_rows = out_0.rearrange("(p t) c -> p t c", t=PACK)
 
-        def differ(engine, diff, lo, hi):
-            engine.tensor_tensor(diff, av[:, lo:hi], at[:, lo:hi], ALU.subtract)
-            return diff
-
-        def work(tag):
-            return keep.tile([P, HALF], F32, name="work", tag=tag, align_bytes=64)
-
-        def weigh(engine, diff, lo, hi):
-            engine.tensor_tensor(av[:, lo:hi], diff, gate[:, lo:hi], ALU.mult)
-
-        def join(engine, lo, hi):
-            engine.tensor_tensor(mixed[:, lo:hi], av[:, lo:hi], at[:, lo:hi], ALU.add)
-
-        def scale(lo, hi):
-            j = lo % J
-            first, last = j % HALF // PACK, (j % HALF + hi - lo) // PACK
+        def times_wgo(result, mixed, h, lo=0, hi=HALF):
             nc.vector.tensor_tensor(
-                weighted[:, lo:hi].rearrange("p (m r) -> p m r", r=PACK),
-                mixed[:, lo:hi].rearrange("p (m r) -> p m r", r=PACK),
-                wgo_banks[j // HALF][:].rearrange("p r m -> p m r")[:, first:last, :], ALU.mult)
+                result.rearrange("p (m r) -> p m r", r=PACK), mixed.rearrange("p (m r) -> p m r", r=PACK),
+                wgo_banks[h][:].rearrange("p (r m) -> p m r", r=PACK)[:, lo // PACK : hi // PACK, :], ALU.mult)
 
-        def gate_turned(t, spent):
-            nc.vector.tensor_tensor(spent, gate[:, t * J : t * J + HALF], turned[t][0][:], ALU.mult)
+        def gate_product(u, result):
+            nc.vector.tensor_tensor(result, cols(gate, u), diffs[u][:], ALU.mult)
 
-        def mix_turned(t, gated):
-            joined = av[:, t * J + HALF : (t + 1) * J]
-            nc.gpsimd.tensor_tensor(joined, gated, turned[t][1][:], ALU.add)
-            nc.gpsimd.tensor_tensor(weighted[:, t * J : t * J + HALF], joined, wgo_sb[:, :HALF], ALU.mult)
+        first_product = reused.tile([P, HALF], F32, name="first_product", align_bytes=64, offset=4 * HALF)
+        for (lo, hi), bank in zip(quarters, first_banks):
+            nc.vector.tensor_tensor(first_product[:, lo:hi], cols(gate, 0, lo, hi), bank[:, QUARTER:], ALU.mult)
+        for (lo, hi), bank in zip(quarters, first_banks):
+            nc.vector.tensor_tensor(cols(gate, 0, lo, hi), bank[:, :QUARTER], first_product[:, lo:hi], ALU.subtract)
+        for lo, hi in quarters:
+            times_wgo(cols(ready, 0, lo, hi), cols(gate, 0, lo, hi), 0, lo, hi)
 
-        def place(t, first, last):
-            window = pages[t][:].indirect(entries(list1, first, last))
-            if (t, last) == (PACK - 1, J):
-                nc.vector.tensor_tensor(window, mixed[:, t * J + first : t * J + last], wgo_sb[:, first:], ALU.mult)
+        def later_turned(u):
+            turned(text_side, at, u, -1.0)
+            gate_of(u)
+            turn_back(diffs[u], cols(av, u), True, False)
+            turn_back(diffs[u], cols(at, u), False, True)
+
+        later_turned(2)
+        plain(text_side, cols(at, 3), 3)
+        plain(text_side, cols(base, 1), 2)
+        later_turned(4)
+        gate_of(3)
+        plain(text_side, cols(base, 2), 4)
+        plain(text_side, cols(at, 5), 5)
+        turned(picture_side, av, 6, 1.0)
+        later_turned(6)
+        gate_of(5)
+        plain(text_side, cols(base, 3), 6)
+        plain(picture_side, cols(av, 7), 7)
+        plain(text_side, cols(at, 7), 7)
+        gate_of(7)
+        woven = [keep.tile([P, hi - lo, PACK], BF16, name="woven%d" % lo, tag=tag, align_bytes=64)
+                 for (lo, hi), tag in zip(CHUNKS, ["v_w", "z_s", "v_s", "v2_s", "zv_w"])]
+
+        def place(u, source):
+            t, j = u // 2, u % 2 * HALF
+            window = pages[t][:].indirect(entries(list1, j, j + HALF))
+            if u == 2 * PACK - 1:
+                nc.vector.tensor_tensor(window, source, wgo_sb[:, j:], ALU.mult)
             else:
-                nc.vector.tensor_copy(window, weighted[:, t * J + first : t * J + last])
-            if last == J:
+                nc.vector.tensor_copy(window, source)
+            if j:
                 nc.sync.dma_start(out=out_rows[:, t, :], in_=pages[t][:])
-                weave(t)
 
         def weave(t):
             for (lo, hi), tile in zip(CHUNKS, woven):
@@ -293,54 +322,47 @@ def tile_list_gmu_tanh_scatP_kernel(
                 if first < hi:
                     nc.scalar.copy(tile[:, first - lo :, t], pages[t][:, first:hi])
 
-        quarters = [(0, QUARTER), (QUARTER, HALF)]
-        picture(0, 0, HALF, "early")
-        picture(0, HALF, J, "early")
-        for t in range(1, EARLY_PAGES):
-            picture_turned(t, "early")
-            picture(t, HALF, J, "early")
-        text(0, 0, HALF)
-        gate_of(0, 0, HALF)
-        text(0, HALF, J)
-        gate_of(0, HALF, J)
-        turned = {}
-        for t in range(1, PACK):
-            if t >= EARLY_PAGES:
-                picture_turned(t, "late")
-            turned_sums(t, 1)
-            if t >= EARLY_PAGES:
-                picture(t, HALF, J, "late")
-            text(t, HALF, J)
-            gate_of(t, 0, HALF)
-            base = keep.tile([P, HALF], F32, name="base%d" % t, align_bytes=64)
-            turned[t] = (turn(t), base)
-            text(t, 0, HALF, base[:])
-            gate_of(t, HALF, J)
-        woven = [keep.tile([P, hi - lo, PACK], BF16, name="woven%d" % lo, tag=tag, align_bytes=64)
-                 for (lo, hi), tag in zip(CHUNKS, ["v_w0", "z_s", "v_s0", "v2_s0", "zv_w"])]
+        def pool_step(result, left, right, op):
+            nc.gpsimd.tensor_tensor(result, left, right, op)
 
-        first_diff = reused.tile([P, HALF], F32, name="first_diff", align_bytes=64, offset=4 * HALF)
-        diffs = [differ(nc.vector, first_diff[:, lo:hi], lo, hi) for lo, hi in quarters]
-        for diff, cols in zip(diffs, quarters):
-            weigh(nc.vector, diff, *cols)
-        for cols in quarters:
-            join(nc.vector, *cols)
-        for cols in quarters:
-            scale(*cols)
-        place(0, 0, HALF)
-        weigh(nc.gpsimd, differ(nc.gpsimd, work("diff")[:], HALF, J), HALF, J)
-        join(nc.gpsimd, HALF, J)
-        for t in range(1, PACK):
-            earlier, later = ((t - 1) * J + HALF, t * J), (t * J + HALF, (t + 1) * J)
-            scale(*earlier)
-            gate_turned(t, at[:, slice(*earlier)])
-            place(t - 1, HALF, J)
-            diff = differ(nc.gpsimd, work("diff")[:], *later)
-            mix_turned(t, at[:, slice(*earlier)])
-            place(t, 0, HALF)
-            weigh(nc.gpsimd, diff, *later)
-            join(nc.gpsimd, *later)
-        place(PACK - 1, HALF, J)
+        second = keep.tile([P, HALF], F32, name="second", tag="wt_raw", align_bytes=64)
+        low, high = wgo_sb[:, :HALF], wgo_sb[:, HALF:]
+        place(0, cols(ready, 0))
+        pool_step(second[:], cols(av, 1), cols(at, 1), ALU.subtract)
+        pool_step(work[:], second[:], cols(gate, 1), ALU.mult)
+        pool_step(cols(av, 1), work[:], cols(at, 1), ALU.add)
+        times_wgo(cols(ready, 1), cols(av, 1), 1)
+        gate_product(2, cols(gated, 1))
+        place(1, cols(ready, 1))
+        weave(0)
+        pool_step(second[:], cols(av, 3), cols(at, 3), ALU.subtract)
+        pool_step(work[:], cols(gated, 1), cols(base, 1), ALU.add)
+        pool_step(cols(ready, 2), work[:], low, ALU.mult)
+        place(2, cols(ready, 2))
+        pool_step(work[:], second[:], cols(gate, 3), ALU.mult)
+        pool_step(cols(av, 3), work[:], cols(at, 3), ALU.add)
+        times_wgo(cols(ready, 3), cols(av, 3), 1)
+        gate_product(4, cols(gated, 2))
+        place(3, cols(ready, 3))
+        weave(1)
+        pool_step(work[:], cols(av, 5), cols(at, 5), ALU.subtract)
+        pool_step(cols(at, 3), cols(gated, 2), cols(base, 2), ALU.add)
+        pool_step(cols(ready, 4), cols(at, 3), low, ALU.mult)
+        gate_product(6, cols(gated, 3))
+        place(4, cols(ready, 4))
+        pool_step(cols(at, 3), work[:], cols(gate, 5), ALU.mult)
+        pool_step(work[:], cols(at, 3), cols(at, 5), ALU.add)
+        pool_step(cols(ready, 5), work[:], high, ALU.mult)
+        place(5, cols(ready, 5))
+        pool_step(work[:], cols(gated, 3), cols(base, 3), ALU.add)
+        pool_step(cols(ready, 6), work[:], low, ALU.mult)
+        place(6, cols(ready, 6))
+        pool_step(work[:], cols(av, 7), cols(at, 7), ALU.subtract)
+        pool_step(cols(av, 7), work[:], cols(gate, 7), ALU.mult)
+        pool_step(cols(gate, 7), cols(av, 7), cols(at, 7), ALU.add)
+        weave(2)
+        place(7, cols(gate, 7))
+        weave(3)
 
         out_words = words_of(out_1)
         codes = keep.tile([P, T], U32, name="codes", align_bytes=64)

from contextlib import ExitStack

import concourse.mybir as mybir
from concourse.masks import make_identity

N, T, J = 512, 2048, 1024
CONTRACTION = 512
FLOPS = 4 * 2 * CONTRACTION * N * J

F32 = mybir.dt.float32
BF16 = mybir.dt.bfloat16
I32 = mybir.dt.int32
U32 = mybir.dt.uint32
U16 = mybir.dt.uint16
U8 = mybir.dt.uint8
FP8X4 = mybir.dt.float8_e4m3fn_x4
FP4X4 = mybir.dt.float4_e2m1fn_x4
ACT = mybir.ActivationFunctionType
ALU = mybir.AluOpType

P = 128
PACK = 4
PER_COLUMN = 16
HALF = 512
QUARTER = 256
CHUNKS = [(0, 512), (512, 1024), (1024, 1536), (1536, 1792), (1792, 2048)]
VECTOR_COLUMNS = 768
RING_BANKS = 4
TAB_ROW, WV_ROW, ZT_ROW, ZV_ROW = 4, 4, 0, 8


def plane_loads(plane, first_row, scales):
    return [
        (plane[first_row + r : P : 32, :].bitcast(I32), scales[0, r : 16 : 4, :].bitcast(I32))
        for r in range(4)
    ]


def words_of(dram):
    return dram[0].rearrange("p n i -> p (n i)").bitcast(I32)


def entries(offsets, first, last):
    return offsets[:, first // PER_COLUMN : last // PER_COLUMN]


def tile_list_gmu_tanh_scatP_kernel(
    tc, tab_words, tab_scales, tab2_words, tab2_scales, zv_words, zv_scales, zt_words, zt_scales,
    b, wv_words, wv_scales, wt, wgo, offs, offs2, out_0, out_1, out_2,
):
    nc = tc.nc
    with ExitStack() as ctx:
        keep = ctx.enter_context(tc.tile_pool(name="keep", bufs=1))
        reused = ctx.enter_context(tc.tile_pool(name="reused", bufs=1))
        sums = ctx.enter_context(tc.psum_pool(name="sums", bufs=1))

        ring = [sums.tile([P, HALF], F32, name="ring%d" % i) for i in range(RING_BANKS)]
        first_banks = [sums.tile([P, HALF], F32, name="first%d" % i) for i in range(2)]
        wgo_banks = [sums.tile([P, HALF], F32, name="wgo%d" % h) for h in range(2)]
        taken = []

        def next_bank():
            taken.append(ring[len(taken) % RING_BANKS])
            return taken[-1]

        list1 = keep.tile([P, J // PER_COLUMN], U16, name="list1")
        list2 = keep.tile([P, J // PER_COLUMN], U16, name="list2")
        tab_w = keep.tile([P, T], U32, name="tab_w", align_bytes=64)
        tab_s = keep.tile([P, T], U8, name="tab_s", align_bytes=64)
        tab2_w = keep.tile([P, T], U32, name="tab2_w", align_bytes=64)
        tab2_s = keep.tile([P, T], U8, name="tab2_s", align_bytes=64)
        z_room = reused.tile([P, 6 * N], U8, name="z_room", align_bytes=64, offset=4 * HALF - N // 2)
        z_raw_s = z_room[:, :N]
        wv_raw_s = keep.tile([P, N], U8, name="wv_raw_s", align_bytes=64)
        wv_raw = keep.tile([P, N], U32, name="wv_raw", align_bytes=64)
        zv_raw = keep.tile([P, N], U32, name="zv_raw", align_bytes=64)
        zt_raw = keep.tile([P, N], U16, name="zt_raw", align_bytes=64)
        wt_raw = keep.tile([P, PACK, N], F32, name="wt_raw", align_bytes=64)
        bias = keep.tile([P, PACK], F32, name="bias")
        minus_bias = keep.tile([P, 1], F32, name="minus_bias")
        wgo_cols = keep.tile([P, 2, PACK], F32, name="wgo_cols", align_bytes=64)
        wgo_sb = keep.tile([P, J], F32, name="wgo_sb", align_bytes=64)
        ident = keep.tile([P, P], F32, name="ident", align_bytes=64)
        cleared = keep.tile([P, 1], F32, name="cleared")
        half = keep.tile([P, 1], F32, name="half")
        no_bias = keep.tile([P, 1], F32, name="no_bias")
        windows = [keep.tile([P, T], F32, name="page%d" % t, align_bytes=64) for t in range(PACK - 1)]
        pages = windows + windows[:1]

        nc.gpsimd.memset(tab_s[:].bitcast(I32), 0)
        nc.vector.memset(cleared[:], 0.0)
        nc.vector.memset(wv_raw_s[:].bitcast(I32), 0)
        nc.vector.memset(windows[0][:].bitcast(I32), 0)
        nc.vector.memset(z_raw_s.bitcast(I32), 0)
        nc.vector.memset(tab2_s[:].bitcast(I32), 0)
        nc.scalar.activation(half[:], cleared[:], ACT.Sigmoid)
        nc.scalar.activation(no_bias[:], half[:], ACT.Tanh, scale=0.0)

        z_planes = plane_loads(z_raw_s, ZV_ROW, zv_scales) + plane_loads(z_raw_s, ZT_ROW, zt_scales)
        wv_planes = plane_loads(wv_raw_s, WV_ROW, wv_scales)
        loads = (
            [(list1[:], offs), (zv_raw[:].bitcast(I32), words_of(zv_words)),
             (wv_raw[:].bitcast(I32), words_of(wv_words))]
            + plane_loads(tab_s, TAB_ROW, tab_scales)
            + [(tab_w[:].bitcast(I32), words_of(tab_words)), (list2[:], offs2),
               (bias[:], b.rearrange("(p t) -> p t", t=PACK))]
            + wv_planes
            + [(wt_raw[:], wt.rearrange("(p i) n -> p i n", i=PACK))]
            + plane_loads(tab2_s, 0, tab2_scales)
            + [(zt_raw[:].bitcast(I32), zt_words[0].bitcast(I32))]
            + z_planes[:1]
            + [(tab2_w[:].bitcast(I32), words_of(tab2_words))]
            + z_planes[1:]
            + [(wgo_sb[:], wgo)]
        )
        for out, in_ in loads:
            nc.sync.dma_start(out, in_)

        make_identity(nc, ident[:])
        nc.gpsimd.dma_start(wgo_cols[:], wgo[0:1, :].rearrange("o (h p r) -> p (o h) r", h=2, r=PACK))
        for window in windows[1:]:
            nc.gpsimd.memset(window[:], 0.0)

        def gather(got, window, offsets, first, last):
            nc.vector.tensor_copy(got, window[:].indirect(entries(offsets, first, last)))

        v_s = keep.tile([P, J], U8, name="v_s", align_bytes=64)
        v_w = keep.tile([P, J], U32, name="v_w", align_bytes=64)
        v2_s = keep.tile([P, J], U8, name="v2_s", align_bytes=64)
        gather(v_s[:], tab_s, list1, 0, J)
        gather(v_w[:, :HALF], tab_w, list1, 0, HALF)
        gather(v_w[:, HALF:], tab_w, list1, HALF, J)
        gather(v2_s[:], tab2_s, list2, 0, J)

        def deal(engine_copy, name, raw, dtype):
            dealt = keep.tile([P, PACK, P], dtype, name=name, align_bytes=64)
            engine_copy(dealt[:], raw[:].rearrange("p (m t) -> p t m", t=PACK))
            return dealt

        wv_w = deal(nc.scalar.copy, "wv_w", wv_raw, U32)
        zv_w = deal(nc.scalar.copy, "zv_w", zv_raw, U32)
        wv_s = deal(nc.gpsimd.tensor_copy, "wv_s", wv_raw_s, U8)
        wt_bf = []

        def round_wt(h, tile):
            nc.gpsimd.tensor_scalar(
                tile.rearrange("p (t m i) -> p m t i", t=2, i=PACK),
                wt_raw[:].rearrange("p i (m t) -> p m t i", t=PACK)[:, :, 2 * h : 2 * h + 2, :],
                1.0, 0.0, ALU.mult, ALU.add)
            wt_bf.append(tile)

        round_wt(0, keep.tile([P, J], BF16, name="wt_bf0", tag="wv_raw_s", align_bytes=64)[:])
        wt_w, wt_s = [], []

        def quantise_wt(h, scales):
            words = keep.tile([P, 2 * P], U32, name="wt_w%d" % h, align_bytes=64)
            nc.vector.quantize_mx(out=words[:].bitcast(FP8X4), scales=scales[:], in_=wt_bf[h])
            wt_w.extend([words[:, :P], words[:, P:]])
            wt_s.extend([scales[:, :P], scales[:, P:]])

        quantise_wt(0, keep.tile([P, 2 * P], U8, name="wt_s0", tag="tab2_s", align_bytes=64))
        zt_w = deal(nc.scalar.copy, "zt_w", zt_raw, U16)
        v2_w = [keep.tile([P, HALF], U32, name="v2_w0", align_bytes=64)]
        gather(v2_w[0][:, :QUARTER], tab2_w, list2, 0, QUARTER)
        gather(v2_w[0][:, QUARTER:], tab2_w, list2, QUARTER, HALF)
        z_s = deal(nc.gpsimd.tensor_copy, "z_s", z_raw_s, U8)
        round_wt(1, reused.tile([P, J], BF16, name="wt_bf1", align_bytes=64, offset=4 * HALF)[:])
        v2_w.append(reused.tile([P, HALF], U32, name="v2_w1", align_bytes=64, offset=0))
        gather(v2_w[1][:], tab2_w, list2, HALF, J)
        quantise_wt(1, keep.tile([P, 2 * P], U8, name="wt_s1", tag="tab2_w", align_bytes=64))
        nc.scalar.activation(minus_bias[:], bias[:, 0:1], ACT.Copy, scale=-1.0)

        def picture_words(first, last):
            return v_w[:, first:last].bitcast(FP8X4)

        def text_words(first, last):
            h = first // HALF
            return v2_w[h][:, first - h * HALF : last - h * HALF].bitcast(FP8X4)

        def picture_side(t):
            return wv_w[:, t, :].bitcast(FP8X4), wv_s[WV_ROW:, t, :], picture_words, v_s[TAB_ROW:, :]

        def text_side(t):
            return wt_w[t].bitcast(FP8X4), wt_s[t], text_words, v2_s

        av = keep.tile([P, PACK * J], F32, name="av", align_bytes=64)
        at = keep.tile([P, PACK * J], F32, name="at", align_bytes=64)
        gate = keep.tile([P, PACK * J], F32, name="gate", align_bytes=64)
        ready = keep.tile([P, PACK * J], F32, name="ready", align_bytes=64)
        base = keep.tile([P, PACK * HALF], F32, name="base", align_bytes=64)
        gated = keep.tile([P, PACK * HALF], F32, name="gated", align_bytes=64)
        work = keep.tile([P, HALF], F32, name="work", align_bytes=64)

        def cols(tile, u, lo=0, hi=HALF):
            return tile[:, u * HALF + lo : u * HALF + hi]

        def plain(side, result, u):
            weight, weight_s, words, scales = side(u // 2)
            j = u % 2 * HALF
            acc = next_bank()
            nc.tensor.matmul_mx(out=acc[:], lhsT=weight, lhsT_scale=weight_s, rhs=words(j, j + HALF),
                                rhs_scale=scales[:, j : j + HALF], start=True, stop=True)
            nc.scalar.activation(result, acc[:], ACT.Tanh, bias=no_bias[:])

        def turned(side, result, u, sign, lo=0, hi=HALF):
            weight, weight_s, words, scales = side(u // 2)
            j = u % 2 * HALF
            acc = next_bank()
            for c in range(lo, hi, P):
                nc.tensor.matmul_mx(out=acc[:, c - lo : c - lo + P], lhsT=words(j + c, j + c + P),
                                    lhsT_scale=scales[:, j + c : j + c + P], rhs=weight, rhs_scale=weight_s,
                                    start=True, stop=True)
            nc.scalar.activation(cols(result, u, lo, hi), acc[:, : hi - lo], ACT.Tanh, bias=no_bias[:], scale=sign)

        def gate_of(u):
            t, j = u // 2, u % 2 * HALF
            acc = next_bank()
            nc.tensor.matmul_mx(out=acc[:], lhsT=zv_w[:, t, :].bitcast(FP8X4), lhsT_scale=z_s[ZV_ROW:, t, :],
                                rhs=picture_words(j, j + HALF), rhs_scale=v_s[TAB_ROW:, j : j + HALF],
                                start=True, stop=False)
            nc.tensor.matmul_mx(out=acc[:], lhsT=zt_w[:, t, :].bitcast(U8).bitcast(FP4X4),
                                lhsT_scale=z_s[ZT_ROW:, t, :], rhs=text_words(j, j + HALF),
                                rhs_scale=v2_s[:, j : j + HALF], start=False, stop=True)
            if u == 0:
                for lo, hi in quarters:
                    nc.scalar.activation(cols(gate, u, lo, hi), acc[:, lo:hi], ACT.Sigmoid, bias=minus_bias[:],
                                         scale=-1.0)
            else:
                nc.scalar.activation(cols(gate, u), acc[:], ACT.Sigmoid, bias=bias[:, t : t + 1])

        def turn_back(bank, source, opens, closes):
            width = source.shape[1]
            for c in range(0, width, P):
                nc.tensor.matmul(bank[:, c : c + P], source[:, c : c + P], ident[:],
                                 start=opens and c == 0, stop=closes and c + P == width, is_transpose=True)

        for h in range(2):
            for r in range(PACK):
                nc.tensor.transpose(wgo_banks[h][:, r * P : (r + 1) * P],
                                    wgo_cols[:, h, r : r + 1].to_broadcast([P, P]), ident[:])

        quarters = [(0, QUARTER), (QUARTER, HALF)]
        diffs = {2: first_banks[0], 4: first_banks[1], 6: wgo_banks[0]}
        turned(picture_side, av, 0, 1.0)
        plain(picture_side, cols(av, 1), 1)
        for (lo, hi), bank in zip(quarters, first_banks):
            turn_back(bank[:, :QUARTER], cols(av, 0, lo, hi), True, True)
            turn_back(bank[:, QUARTER:], cols(av, 0, lo, hi), True, False)
        turned(picture_side, av, 2, 1.0)
        plain(picture_side, cols(av, 3), 3)
        turned(picture_side, av, 4, 1.0)
        plain(picture_side, cols(av, 5), 5)
        first_at = reused.tile([P, HALF], F32, name="first_at", align_bytes=64, offset=8 * HALF)
        for (lo, hi), bank in zip(quarters, first_banks):
            turned(text_side, first_at, 0, -1.0, lo, hi)
            turn_back(bank[:, QUARTER:], first_at[:, lo:hi], False, True)
        gate_of(0)
        plain(text_side, cols(at, 1), 1)
        gate_of(1)
        ring[3], ring[0] = ring[0], ring[3]

        out_rows = out_0.rearrange("(p t) c -> p t c", t=PACK)

        def times_wgo(result, mixed, h, lo=0, hi=HALF):
            nc.vector.tensor_tensor(
                result.rearrange("p (m r) -> p m r", r=PACK), mixed.rearrange("p (m r) -> p m r", r=PACK),
                wgo_banks[h][:].rearrange("p (r m) -> p m r", r=PACK)[:, lo // PACK : hi // PACK, :], ALU.mult)

        def gate_product(u, result):
            nc.vector.tensor_tensor(result, cols(gate, u), diffs[u][:], ALU.mult)

        first_product = reused.tile([P, HALF], F32, name="first_product", align_bytes=64, offset=4 * HALF)
        for (lo, hi), bank in zip(quarters, first_banks):
            nc.vector.tensor_tensor(first_product[:, lo:hi], cols(gate, 0, lo, hi), bank[:, QUARTER:], ALU.mult)
        for (lo, hi), bank in zip(quarters, first_banks):
            nc.vector.tensor_tensor(cols(gate, 0, lo, hi), bank[:, :QUARTER], first_product[:, lo:hi], ALU.subtract)
        for lo, hi in quarters:
            times_wgo(cols(ready, 0, lo, hi), cols(gate, 0, lo, hi), 0, lo, hi)

        def later_turned(u):
            turned(text_side, at, u, -1.0)
            gate_of(u)
            turn_back(diffs[u], cols(av, u), True, False)
            turn_back(diffs[u], cols(at, u), False, True)

        later_turned(2)
        plain(text_side, cols(at, 3), 3)
        plain(text_side, cols(base, 1), 2)
        later_turned(4)
        gate_of(3)
        plain(text_side, cols(base, 2), 4)
        plain(text_side, cols(at, 5), 5)
        turned(picture_side, av, 6, 1.0)
        later_turned(6)
        gate_of(5)
        plain(text_side, cols(base, 3), 6)
        plain(picture_side, cols(av, 7), 7)
        plain(text_side, cols(at, 7), 7)
        gate_of(7)
        woven = [keep.tile([P, hi - lo, PACK], BF16, name="woven%d" % lo, tag=tag, align_bytes=64)
                 for (lo, hi), tag in zip(CHUNKS, ["v_w", "z_s", "v_s", "v2_s", "zv_w"])]

        def place(u, source):
            t, j = u // 2, u % 2 * HALF
            window = pages[t][:].indirect(entries(list1, j, j + HALF))
            if u == 2 * PACK - 1:
                nc.vector.tensor_tensor(window, source, wgo_sb[:, j:], ALU.mult)
            else:
                nc.vector.tensor_copy(window, source)
            if j:
                nc.sync.dma_start(out=out_rows[:, t, :], in_=pages[t][:])

        def weave(t):
            for (lo, hi), tile in zip(CHUNKS, woven):
                split = min(max(VECTOR_COLUMNS, lo), hi)
                if t == PACK - 2 and split > lo:
                    nc.scalar.copy(tile[:, : split - lo, t:],
                                   pages[t][:, lo:split].unsqueeze(2).to_broadcast([P, split - lo, 2]))
                elif t == PACK - 1 and split > lo:
                    nc.vector.tensor_copy(tile[:, : split - lo, t], pages[t][:, lo:split])
                first = split if t >= PACK - 2 else lo
                if first < hi:
                    nc.scalar.copy(tile[:, first - lo :, t], pages[t][:, first:hi])

        def pool_step(result, left, right, op):
            nc.gpsimd.tensor_tensor(result, left, right, op)

        second = keep.tile([P, HALF], F32, name="second", tag="wt_raw", align_bytes=64)
        low, high = wgo_sb[:, :HALF], wgo_sb[:, HALF:]
        place(0, cols(ready, 0))
        pool_step(second[:], cols(av, 1), cols(at, 1), ALU.subtract)
        pool_step(work[:], second[:], cols(gate, 1), ALU.mult)
        pool_step(cols(av, 1), work[:], cols(at, 1), ALU.add)
        times_wgo(cols(ready, 1), cols(av, 1), 1)
        gate_product(2, cols(gated, 1))
        place(1, cols(ready, 1))
        weave(0)
        pool_step(second[:], cols(av, 3), cols(at, 3), ALU.subtract)
        pool_step(work[:], cols(gated, 1), cols(base, 1), ALU.add)
        pool_step(cols(ready, 2), work[:], low, ALU.mult)
        place(2, cols(ready, 2))
        pool_step(work[:], second[:], cols(gate, 3), ALU.mult)
        pool_step(cols(av, 3), work[:], cols(at, 3), ALU.add)
        times_wgo(cols(ready, 3), cols(av, 3), 1)
        gate_product(4, cols(gated, 2))
        place(3, cols(ready, 3))
        weave(1)
        pool_step(work[:], cols(av, 5), cols(at, 5), ALU.subtract)
        pool_step(cols(at, 3), cols(gated, 2), cols(base, 2), ALU.add)
        pool_step(cols(ready, 4), cols(at, 3), low, ALU.mult)
        gate_product(6, cols(gated, 3))
        place(4, cols(ready, 4))
        pool_step(cols(at, 3), work[:], cols(gate, 5), ALU.mult)
        pool_step(work[:], cols(at, 3), cols(at, 5), ALU.add)
        pool_step(cols(ready, 5), work[:], high, ALU.mult)
        place(5, cols(ready, 5))
        pool_step(work[:], cols(gated, 3), cols(base, 3), ALU.add)
        pool_step(cols(ready, 6), work[:], low, ALU.mult)
        place(6, cols(ready, 6))
        pool_step(work[:], cols(av, 7), cols(at, 7), ALU.subtract)
        pool_step(cols(av, 7), work[:], cols(gate, 7), ALU.mult)
        pool_step(cols(gate, 7), cols(av, 7), cols(at, 7), ALU.add)
        weave(2)
        place(7, cols(gate, 7))
        weave(3)

        out_words = words_of(out_1)
        codes = keep.tile([P, T], U32, name="codes", align_bytes=64)
        plane = keep.tile([P, T], U8, name="plane", align_bytes=64)
        for (lo, hi), tile in zip(CHUNKS, woven):
            nc.vector.quantize_mx(
                out=codes[:, lo:hi].bitcast(FP8X4), scales=plane[:, lo:hi],
                in_=tile[:].rearrange("p c i -> p (c i)"),
            )
            nc.sync.dma_start(out=out_words[:, lo:hi], in_=codes[:, lo:hi].bitcast(I32))
        for r in range(4):
            queue = nc.scalar if r % 2 else nc.sync
            queue.dma_start(out=out_2[0, r : 16 : 4, :].bitcast(I32), in_=plane[r : P : 32, :].bitcast(I32))
